import numpy as np, ml_dtypes
CORES = [1,5,17,21,33,37,49,53]
N = 8
BF = ml_dtypes.bfloat16
S, SETS, SH, B, L, RO, NS, EPS = 4096, 16, 4, 226, 256, 3, 6, 130
def sky(rng):
    c = rng.integers(0, 16, (N, 8, 16, S)); t = rng.integers(0, S, (N, 8, 16, SETS * B))
    return c, np.where(rng.random(t.shape) < 0.0625, S, t)
def pack(c, t, v):
    return {"cvec": np.ascontiguousarray(c).reshape(N, 128, S).astype(np.float32).astype(BF), "tsee": np.ascontiguousarray(t).reshape(N, 128, SETS * B).astype(np.int32),
            "obs": np.ascontiguousarray(v).reshape(N, 128, NS * L).astype(np.float32).astype(BF)}
def uneven(rng, shape):
    k = shape[:-2] + (1, shape[-1]); m = rng.choice(np.array([0, 1, 2, 4, 7, 11, 15]), k)
    x = np.minimum((rng.random(shape) * (m + 1)).astype(np.int64), m)
    return np.where(rng.random(k) < 0.25, 15 - x, x)
def sized(n):
    w = np.indices((15, 15, 15, 15)).reshape(4, -1).T; at = np.unique(np.sum(w * w, axis=1), return_index=True)[1]
    return np.concatenate([15 * (np.arange(12) < n[..., None] // 225), w[at[n % 225]]], axis=-1)
def setup_inputs(rng):
    c, t = sky(rng); P = 24; pool = rng.integers(0, 16, (8, SETS, 16, P)); size = rng.integers(NS + 2, P + 1, (1, 8, 1, 1))
    pick = np.argsort(rng.random((N, 8, L, P)) + (np.arange(P) >= size), axis=-1)[..., :NS]
    v = pool[np.arange(8).reshape(1, 8, 1, 1), (np.arange(L) % SETS).reshape(1, 1, L, 1), :, pick]
    v = v.transpose(0, 1, 4, 3, 2); near = rng.random((N, 8, 1, NS, L)) < 0.25
    return pack(c, t, np.clip(v + near * rng.integers(-1, 2, v.shape), 0, 15))
def setup_inputs_spread(rng):
    c = uneven(rng, (N, 8, 16, S)); v = uneven(rng, (N, 8, 16, NS * L)).reshape(N, 8, 16, NS, L)
    u = rng.random((N, 8, 16, SETS * B)); t = np.minimum((S * u * u * u * u).astype(np.int64), S - 1)
    return pack(c, np.where(rng.random(t.shape) < 0.08, S, t), v)
def setup_inputs_ends(rng):
    c = 15 * (rng.random((N, 8, 16, S)) < rng.choice(np.array([0.0, 0.25, 0.5, 0.75, 1.0]), (N, 8, 1, S)))
    c[:, 1::2, :, 0] = 15; c[..., S - 1] = 15
    kind = rng.integers(0, 4, (N, 8, 1, 1, L)); kind[..., 0] = 1; kind[..., L - 1] = 0; kind[..., L - 1 - SETS] = 0
    some = rng.random((N, 8, 16, NS, L)) < 0.5; bit = rng.random((N, 8, 1, NS, L)) < 0.5
    v = 15 * np.where(kind == 0, True, np.where(kind == 1, False, np.where(kind == 2, some, bit)))
    u = rng.random((N, 8, 16, SETS * B)); t = np.where(u < 0.4, 0, np.where(u < 0.7, S, np.where(u < 0.8, S - 1, rng.integers(1, S, u.shape))))
    tv = t.reshape(N, 8, 16, SETS, B); m = rng.random((N, 8, 1, SETS)) < 0.5; m[..., SETS - 1] = True
    late = np.array([S] * 13 + [0, S - 1, S - 1]).reshape(1, 1, 16, 1)
    tv[..., B - 1] = np.where(m, late, tv[..., B - 1])
    return pack(c, tv.reshape(N, 8, 16, SETS * B), v)
def setup_inputs_corners(rng):
    c, t = sky(rng); x = np.zeros((10, 16), np.int64)
    x[0, 0:6] = 15; x[1, 0:6] = 15; x[2, 3:6] = 15; x[3, 0:6] = 15; x[4, 0:3] = 15; x[4, 6:9] = 15; x[5, 0:3] = 15; x[6, 3:9] = 15; x[7, 6:9] = 15
    x[1, 12] = EPS // 10; x[1, 13] = EPS % 10; x[3, 12] = (EPS + 1) // 10; x[3, 13] = (EPS + 1) % 10; x[4:6, 12] = 10; x[4:6, 13] = 1
    for k, n in ((8, 675 - EPS), (9, 674 - EPS)):
        x[k, 0:2] = 15; x[k, 2] = n // 15 - 30; x[k, 3:6] = 15; x[k, 12] = (n % 15) // 10; x[k, 13] = (n % 15) % 10
    nm = np.zeros((N, 8, 10), np.int64)
    for q in range(N):
        for g in range(8):
            nm[q, g] = rng.permutation(np.concatenate([np.array([0, S - 1]), 1 + rng.permutation(S - 2)[:8]])); c[q, g][:, nm[q, g]] = x.T
    pt = np.array([[0, 0, 0, 0, 0, 0], [16, 16, 0, 0, 0, 0], [16, 15, 0, 0, 0, 0], [15, 16, 0, 0, 0, 0], [0, 16, 16, 0, 0, 0], [16, 0, 15, 0, 0, 0], [15, 0, 16, 0, 0, 0], [0, 15, 16, 0, 0, 0],
                   [1, 0, 0, 0, 0, 0], [0, 1, 0, 0, 0, 0], [0, 0, 1, 0, 0, 0], [1, 1, 0, 0, 1, 0], [1, 1, 1, 0, 1, 2], [2, 3, 0, 0, 0, 0], [3, 2, 0, 0, 1, 0], [0, 3, 2, 0, 0, 3], [0, 2, 3, 0, 0, 1],
                   [2, 0, 3, 0, 0, 0], [3, 0, 2, 0, 0, 2], [5, 5, 5, 0, 5, 10], [5, 6, 5, 0, 5, 11], [8, 8, 8, 0, 4, 8], [1, 1, 1, 0, 0, 0], [16, 16, 16, 0, 0, 0], [15, 15, 15, 0, 0, 0], [16, 16, 1, 0, 0, 0], [2, 16, 2, 0, 0, 1], [16, 0, 16, 0, 0, 0]])
    kd = rng.integers(0, len(pt), (N, 8, SETS, 5)); pos = np.argsort(rng.random((N, 8, SETS, 5, 16)), axis=-1)
    pos = np.where(rng.random((N, 8, SETS, 5, 1)) < 0.25, 15 - np.arange(16), pos); w = pt[kd][..., None, :]
    hold = ((pos[..., None] - w[..., 3:]) % 16) < w[..., :3]; way = rng.integers(0, 3, pos.shape)
    qi = np.arange(N).reshape(N, 1, 1, 1, 1); gi = np.arange(8).reshape(1, 8, 1, 1, 1)
    na = nm[qi, gi, np.where(hold[..., 0], np.array([0, 1, 8])[way], np.array([2, 3, 9])[way])]
    na = np.where((kd[..., None] == 0) & (rng.random(pos.shape) < 0.5), S, na)
    nb = nm[qi, gi, np.where(hold[..., 2], 4, 5)]; ne = nm[qi, gi, np.where(hold[..., 1], 6, 7)]
    tv = t.reshape(N, 8, 16, SETS, B)
    for k in range(5):
        for y, z in ((na, 1), (nb, 6), (ne, 11)): tv[..., (15 * (k + z)) >> SH] = y[:, :, :, k].transpose(0, 1, 3, 2)
    k = rng.integers(1, 6, (N, 8, L)); v = np.zeros((N, 8, 16, NS, L), np.int64)
    v[:, :, 9:12, 0] = 15; v[:, :, 0:6, 1] = 15; v[:, :, 9, 1] = k; v[:, :, 0:3, 2] = 15; v[:, :, 6:9, 2] = 15; v[:, :, 10, 2] = k + 5; v[:, :, 3:9, 3] = 15; v[:, :, 11, 3] = k + 10
    v[:, :, :, 4:] = np.take_along_axis(v, rng.integers(1, 4, (N, 8, 1, NS - 4, L)), 3)
    v = np.where(rng.random((N, 8, 1, 1, L)) < 0.2, rng.integers(0, 16, v.shape), v)
    return pack(c, tv.reshape(N, 8, 16, SETS * B), v)
def setup_inputs_crowd(rng):
    M = NS + N; base = rng.integers(0, 16, (8, SETS, 16, M)); D = np.einsum("ghfj,ghfk->ghjk", base, base)
    c, t = sky(rng); nm = np.argsort(rng.random((N, 8, S)), axis=-1)[..., :SETS * M].reshape(N, 8, SETS, M); tv = t.reshape(N, 8, 16, SETS, B)
    gi = np.arange(8).reshape(8, 1, 1); hi = np.arange(SETS).reshape(1, SETS, 1); pi = np.arange(16).reshape(1, 1, 16)
    for q in range(N):
        for g in range(8): c[q, g][:, nm[q, g].reshape(-1)] = base[g].transpose(1, 0, 2).reshape(16, -1)
        kind = rng.integers(0, 3, (8, SETS, 1)); miss = rng.integers(0, 16, (8, SETS, 1))
        prs = [(k, k + z) for k in list(range(M - 2, -1, -1)) + [q + N] for z in (3, 2, 1) if k + z < M] + [(q, j) for j in list(range(q)) + list(range(M - 1, q, -1))]
        for k, j in prs:
            know = np.where(kind == 0, True, np.where(kind == 1, pi != miss, rng.random((8, SETS, 16)) < 0.6)); bn = (D[:, :, k, j] >> SH)[:, :, None]
            tv[q, gi, pi, hi, bn] = np.where(know, nm[q, :, :, j][:, :, None], tv[q, gi, pi, hi, bn])
    v = np.zeros((N, 8, 16, NS, L), np.int64); hl = np.arange(L) % SETS
    for r in range(N):
        o = np.zeros((8, L, NS), np.int64) + np.arange(NS) + r
        o[2::4, :, 2:] = 2 + r + np.argsort(rng.random((2, L, NS - 2)), axis=-1)
        odd = (np.arange(L) // SETS) % 2 == 1; o[3::4, odd, 1] = 2 + r; o[3::4, odd, 2] = 1 + r
        v[r] = base[gi, hl.reshape(1, L, 1), :, o].transpose(0, 3, 2, 1)
        for g in (1, 5):
            ln = np.arange(SETS) + SETS * rng.integers(0, L // SETS, SETS); v[r, g][:, :, ln] = rng.integers(0, 16, (16, NS, SETS))
    return pack(c, tv.reshape(N, 8, 16, SETS * B), v)
def setup_inputs_full(rng):
    d = setup_inputs(rng); c = d["cvec"].astype(np.float32).astype(np.int64).reshape(N, 8, 16, S); t = d["tsee"].astype(np.int64).reshape(N, 8, 16, SETS * B); v = d["obs"].astype(np.float32).astype(np.int64).reshape(N, 8, 16, NS, L)
    lane = np.arange(L); lo = ((EPS + 1) >> SH) + 1; hi = (2923 - EPS) >> SH
    for g in (0, 2, 5, 7):
        bn = np.argsort(rng.random((SETS, hi - lo)), axis=1)[:, :L // SETS] + lo
        D = ((bn << SH) + rng.integers(0, 1 << SH, bn.shape)).T.reshape(L)
        if g >= 5: D[1] = EPS; D[2] = EPS + 1
        col = B * (lane % SETS) + (D >> SH)
        for q in range(N):
            nm = rng.permutation(S)[:8 * L].reshape(L, 8)
            off = rng.integers(1 - EPS, EPS, (L, 8)); off[:, :4] = np.array([EPS, -EPS, EPS + 1, -EPS - 1])
            x = sized(np.maximum(D[:, None] + off, 0)); x = np.take_along_axis(x, np.argsort(rng.random(x.shape), axis=-1), -1)
            c[q, g][:, nm.reshape(-1)] = x.reshape(-1, 16).T
            h0 = rng.integers(0, 16, L); h0[0] = 0; h0[L - 1] = 15
            good = rng.random((L, 16)) < rng.random((L, 1)) * (g > 0); good[L - 1] = False; good[lane, h0] = True
            on = np.array([0, 1, 4, 5, 6, 7])[(rng.integers(0, 6, (L, 1)) + np.arange(16)) % 6]
            name = np.take_along_axis(nm, np.where(good, on, rng.integers(2, 4, (L, 16))), 1)
            name = np.where(~good & (rng.random((L, 16)) < 0.25), S, name)
            if g >= 5: name[1] = np.where(np.arange(16) < h0[1], nm[1, 2], S)
            t[q, g][:, col] = name.T
            y = sized(D); y = np.take_along_axis(y, np.argsort(rng.random(y.shape), axis=-1), -1); v[q, g] = y.T[:, None, :]
    return pack(c, t, v)
def check_inputs(d):
    bad = []
    for k, hi in (("cvec", 15), ("tsee", S), ("obs", 15)):
        x = np.asarray(d[k]).astype(np.float32)
        if not np.all((x >= 0) & (x <= hi) & (x == np.floor(x))): bad.append("range of " + k)
    return bad
def reference(cvec, tsee, obs):
    c = cvec.astype(np.float32).astype(np.int32).reshape(N, 8, 16, S); c = np.concatenate([c, np.zeros((N, 8, 16, 1), np.int32)], axis=3)
    t = tsee.astype(np.int64).reshape(N, 8, 16, SETS * B); v = obs.astype(np.float32).astype(np.int64).reshape(N, 8, 16, NS, L)
    gram = np.einsum("rgfjl,rgfkl->rgjkl", v, v)
    st = np.zeros((N, 4, 8, L), np.int64) + np.arange(4).reshape(1, 4, 1, 1)
    gi = np.arange(8).reshape(8, 1); ln = np.arange(L).reshape(1, L); first = B * (ln % SETS)
    out = np.zeros((N, 8, RO, 3, L), np.float32)
    for rnd in range(RO):
        for q in range(N):
            r = (q - rnd) % N
            o, a, b, e = st[r, 0], st[r, 1], st[r, 2], st[r, 3]; G = gram[r]
            col = [first + (G[gi, o, z, ln] >> SH) for z in (a, b, e)]
            nam = [np.take_along_axis(t[q], k[:, None, :], 2) for k in col]
            vec = [np.take_along_axis(c[q], k.reshape(8, 1, 16 * L), 2).reshape(8, 16, 16, L) for k in nam]
            hold = [np.abs(np.sum(vec[i] * vec[j], axis=1) - G[gi, y, z, ln][:, None, :]) <= EPS for i, j, y, z in ((0, 1, a, b), (0, 2, a, e), (1, 2, b, e))]
            every = hold[0] & hold[1] & hold[2]; found = np.any(every, axis=1); p = np.argmax(every, axis=1)
            for k in range(3): out[q, :, rnd, k] = np.where(found, np.take_along_axis(nam[k], p[:, None, :], 1)[:, 0], -1)
            if rnd == RO - 1: continue
            for g in range(8):
                w = np.nonzero(found[g])[0]; cs, at = np.unique(col[0][g, w], return_index=True); t[q, g, p[g, w[at]], cs] = S
            ab, ac, bc = [np.sum(k, axis=1) for k in hold]
            spike = np.argmin(np.stack([ab + ac, ab + bc, ac + bc]), axis=0); nxt = rnd + 4
            st[r] = np.stack([np.where(found, a, o), np.where(found, b, np.where(spike == 0, nxt, a)), np.where(found, e, np.where(spike == 1, nxt, b)), np.where(found, nxt, np.where(spike == 2, nxt, e))])
    return {"yn": out.reshape(N, 8, RO * 3 * L)}

@@ -1,0 +1,526 @@
+import numpy as np
+from concourse.bass import DstId, RemoteDMATransfer
+from concourse.mybir import AluOpType as A, ActivationFunctionType as AF
+
+SPLIT = ["2U,2W,2W 2W,2W,2W 2W,2W", "2W,2W,2W 2W,2W,2W 2W,2W", "2W,2X,2W 2W,2W,2W 2W,2W"]
+OBALL = 1
+EVS = 8
+FINE = 2
+SCS = 0
+TT = 1.0
+FIGS = [(1.56, 3.8, 0.42, 150.0, 3500.0), (1.1, 2.0, 0.42, 120.0, 3000.0), (2.0, 5.5, 0.42, 120.0, 3000.0), (1.56, 3.8, 0.55, 250.0, 5000.0)]
+TRIES = 1200
+SB = [[[(int(x[0]), x[1:]) for x in c.split(",")] for c in r.split()] for r in SPLIT]
+NC = len(SB[0])
+HS = [sum(x[0] for x in c) for c in SB[0]]
+H0 = [sum(HS[:c]) for c in range(NC)]
+DUM = 1808
+OFF = 1800.0
+
+PAIRS = [(0, 2), (0, 3), (0, 1), (2, 3), (1, 3), (1, 2), (0, 4), (1, 5), (1, 4), (2, 5), (2, 4), (3, 5), (3, 4), (4, 5), (0, 5)]
+
+
+def _col(x, y):
+    i = PAIRS.index((min(x, y), max(x, y)))
+    return i if i < 3 else i + 3
+
+
+def _val(x, y):
+    i = PAIRS.index((min(x, y), max(x, y)))
+    return i if i < 6 else i + 12
+
+
+def _cand1():
+    out = []
+    for n, (o, a, b, c) in enumerate([(0, 4, 2, 3), (0, 1, 4, 3), (0, 1, 2, 4), (1, 2, 3, 4)]):
+        out += [_col(o, b), _col(o, c), _col(o, a), _val(b, c), _val(a, c), _val(a, b), _col(o, 5), _col(a, b), _col(a, c),
+                _col(a, 5), _val(a, 5), _val(b, 5), _val(c, 5), _col(0, 1) if n == 3 else 27]
+    return out
+
+
+CAND1 = _cand1()
+CAND2 = [0, 1, 6, 3, 12, 11, 13, 13, 6, 1, 2, 12, 4, 10, 13, 13, 0, 6, 2, 11, 10, 5, 13, 13, 8, 9, 7, 12, 11, 3, 2, 13]
+
+SCRATCH = {
+    "cv": ("sbuf", [128, 4112], "bfloat16"), "ob": ("sbuf", [128, 1536], "bfloat16"), "gp": ("sbuf", [128, 15, 256], "bfloat16"),
+    "pi": ("sbuf", [128, 8], "int32"), "pf": ("sbuf", [128, 8], "float32"),
+    "ia": ("sbuf", [128, 144], "float32"), "ib": ("sbuf", [128, 128], "float32"), "ik": ("sbuf", [128, 128], "float32"),
+    "ic": ("sbuf", [128, 128], "float32"), "id3": ("sbuf", [128, 24], "float32"), "tm": ("sbuf", [128, 128], "float32"),
+    "blk": ("sbuf", [128, 128], "bfloat16"), "hblk": ("sbuf", [128, 128], "bfloat16"), "eye": ("sbuf", [128, 128], "bfloat16"),
+    "neye": ("sbuf", [128, 128], "bfloat16"), "imt": ("sbuf", [128, 128], "bfloat16"), "t2": ("sbuf", [128, 128], "bfloat16"),
+    "zz": ("sbuf", [128, 144], "bfloat16"), "zo": ("sbuf", [128, 32], "float32"), "of": ("sbuf", [128, 24], "bfloat16"),
+    "sk": ("sbuf", [128, 16], "float32"), "nr": ("sbuf", [128, 16, 128], "bfloat16"), "ee": ("sbuf", [128, 16, 128], "bfloat16"),
+    "c1": ("sbuf", [128, 128], "float16"), "rs": ("sbuf", [128, 128], "float32"), "tie": ("sbuf", [128, 4, 8], "bfloat16"),
+    "zero": ("sbuf", [128, 3, 128], "bfloat16"), "cb": ("sbuf", [128, 12, 16], "int32"), "gi": ("sbuf", [128, 240], "int32"),
+    "gs": ("sbuf", [128, 240], "int32"), "s0": ("sbuf", [128, 6, 16], "float32"), "ww": ("sbuf", [128, 464], "float32"),
+    "dm": ("sbuf", [128, 24], "float32"), "tab": ("sbuf", [128, 136], "float32"), "tb2": ("sbuf", [128, 48], "float32"),
+    "tb3": ("sbuf", [128, 48], "float32"), "o1": ("sbuf", [128, NC, 28], "uint16"), "o2": ("sbuf", [128, 16], "uint16"),
+    "orp": ("sbuf", [128, 48], "uint16"),
+    "cand1": ("sbuf", [128, NC, 448], "float32"), "cand2": ("sbuf", [128, NC, 256], "float32"),
+    "msk": ("sbuf", [128, 2 * NC, 448], "float16"), "sc": ("sbuf", [128, 2 * NC, 32], "float32"),
+    "m1": ("sbuf", [128, 2 * NC, 16], "float32"), "m2": ("sbuf", [128, 2 * NC, 8], "float32"), "mk": ("sbuf", [128, 2 * NC, 32], "float32"),
+    "uo": ("sbuf", [128, 2 * NC, 48], "uint16"), "fo": ("sbuf", [128, 2 * NC, 6, 8], "float16"), "so": ("sbuf", [128, NC, 104], "float32"),
+    "ui": ("sbuf", [128, 3 * NC, 48], "uint16"), "fi": ("sbuf", [128, 3 * NC, 6, 8], "float16"), "si": ("sbuf", [128, NC, 112], "float32"),
+    "nm": ("sbuf", [128, 3 * NC, 384], "uint16"), "ab": ("sbuf", [128, 3 * NC, 3, 128], "bfloat16"),
+    "hd": ("sbuf", [128, 3 * NC, 4, 128], "bfloat16"), "h2": ("sbuf", [128, 3 * NC, 128], "bfloat16"),
+    "ff": ("sbuf", [128, 3 * NC, 128], "bfloat16"), "ae": ("sbuf", [128, 2 * NC, 128], "bfloat16"),
+    "yy": ("sbuf", [128, 2, 3, 128], "float32"), "sv": ("sbuf", [128, 2 * NC, 128], "int32"), "ls": ("sbuf", [128, 2 * NC, 128], "float32"),
+    "sf": ("sbuf", [128, 2 * NC, 8], "float32"), "su": ("sbuf", [128, 2 * NC, 8], "uint16"), "yb": ("sbuf", [128, 3, 16, 16], "float32"),
+    "pm0": ("psum", [128, 4, 128], "float32"), "pm1": ("psum", [128, 4, 128], "float32"), "pe": ("psum", [128, 512], "float32"),
+    "pf1": ("psum", [128, 512], "float32"), "pc": ("psum", [128, 64, 8], "float32"), "pl": ("psum", [128, 512], "float32"),
+    "ps": ("psum", [128, 64, 8], "float32"), "po": ("psum", [128, 16, 32], "float32"),
+}
+for _c in range(NC):
+    SCRATCH["ts%d" % _c] = ("sbuf", [128, 1936], "int32")
+    for _t in range(2):
+        SCRATCH["gv%d_%d" % (_t, _c)] = ("sbuf", [128, 768 * HS[_c]], "bfloat16")
+        SCRATCH["pr%d_%d" % (_t, _c)] = ("sbuf", [128, 768 * HS[_c]], "bfloat16")
+SEMAPHORES = ["eV", "eS", "eP", "eG", "sent"] + ["d%d" % i for i in range(24)] + ["r%d" % i for i in range(3 * NC)]
+
+
+BANKS = [k for k in SCRATCH if SCRATCH[k][0] == "psum"]
+
+
+def runs(vals):
+    out, i = [], 0
+    while i < len(vals):
+        j = i + 1
+        if j < len(vals):
+            st = vals[j] - vals[i]
+            while j + 1 < len(vals) and vals[j + 1] - vals[j] == st: j += 1
+            out.append((i, j - i + 1, vals[i], st)); i = j + 1
+        else:
+            out.append((i, 1, vals[i], 0)); i = j
+    return out
+
+
+def build(T, nxt, topo, core, fig=FIGS[0]):
+    ops = []
+    GC, SC, PC = fig[:3]
+
+    def add(e, ns, rd, wr, fn, kind=None): ops.append(dict(e=e, ns=ns, rd=rd, wr=wr, fn=fn, kind=kind))
+    def vns(n, r=1.0): return 30 + 0.83 * max(64, n * r)
+    def ts(out, in0, s1, s2, op0, op1, n, rd, wr, r=1.0):
+        if op1 is None: add("V", vns(n, r), rd, wr, lambda g: g.vector.tensor_scalar(out, in0, s1, None, op0))
+        else: add("V", vns(n, r), rd, wr, lambda g: g.vector.tensor_scalar(out, in0, s1, s2, op0, op1))
+    def tt(out, a, b, op, n, rd, wr, r=2.0): add("V", vns(n, r), rd, wr, lambda g: g.vector.tensor_tensor(out, a, b, op))
+    def cp(out, a, n, rd, wr, r=1.0): add("V", vns(n, r), rd, wr, lambda g: g.vector.tensor_copy(out, a))
+    def ms(ap, v, n, wr): add("V", vns(n, 0.5), [], wr, lambda g: g.vector.memset(ap, v))
+    def gtt(out, a, b, op, n, rd, wr): add("V", 50 + 0.83 * GC * n, rd, wr, lambda g: g.vector.tensor_tensor(out, a, b, op))
+    def act(out, a, f, n, rd, wr, bias=0.0, scale=1.0, r=1.0):
+        add("S", 50 + 0.83 * max(64, n * r), rd, wr, lambda g: g.scalar.activation(out, a, f, bias=bias, scale=scale))
+    def iota(out, pat, base, cm, n, wr, fl=True):
+        if fl: add("G", 130 + 1.66 * n, [], wr, lambda g: g.iota(out, pat, base, cm, allow_small_or_imprecise_dtypes=True))
+        else: add("G", 130 + 1.66 * n, [], wr, lambda g: g.iota(out, pat, base, cm))
+    def mm(lst, cyc, rd, wr):
+        def fn(g):
+            for m in lst: r = g.tensor.matmul(*m)
+            return r
+        add("P", 40 + PC * cyc + 8 * len(lst), rd, wr, fn)
+    def dma(out, in_, nbytes, rd, wr): add("Y", nbytes / 200.0, rd, wr, lambda g: g.sync.dma_start(out, in_), "dma")
+
+    n0 = SB[0][0][0][0]
+    dma(T.ob[:, 0:1024], T.obs[:, 0:1024], 128 * 2048, [], ["ob0"])
+    part = [[x[0] for x in SB[0][c]] if c < FINE else [HS[c]] for c in range(NC)]
+    def table(c, s):
+        a = sum(part[c][:s]); b = a + part[c][s]
+        dma(T["ts%d" % c][:, 226 * a:226 * b], T.tsee[:, 226 * (H0[c] + a):226 * (H0[c] + b)], 128 * 904 * (b - a), [], ["ts%d_%d" % (c, s)])
+    table(0, 0)
+    if OBALL: dma(T.ob[:, 1024:1536], T.obs[:, 1024:1536], 128 * 1024, [], ["ob1"])
+    dma(T.cv[:, 0:4096], T.cvec[:, :], 128 * 8192, [], ["cv"])
+    if not OBALL: dma(T.ob[:, 1024:1536], T.obs[:, 1024:1536], 128 * 1024, [], ["ob1"])
+    for c in range(NC):
+        for s in range(len(part[c])):
+            if c or s: table(c, s)
+
+    iota(T.pi[:, 0:1], [[0, 1]], 0, 1, 1, ["pi0"], False)
+    iota(T.ia[:, :], [[1, 144]], 0, 0, 144, ["ia"])
+    cp(T.pf[:, 0:1], T.pi[:, 0:1], 1, ["pi0"], ["pf0"])
+    ts(T.pi[:, 4:5], T.pi[:, 0:1], 4, None, A.arith_shift_right, None, 1, ["pi0"], ["pi4"])
+    ts(T.pf[:, 5:6], T.pi[:, 4:5], 16.0, 15.0, A.mult, A.add, 1, ["pi4"], ["pf5"])
+    ts(T.zz[:, :], T.ia[:, :], T.pf[:, 5:6], None, A.is_equal, None, 144, ["ia", "pf5"], ["zz"])
+    ts(T.pi[:, 1:2], T.pi[:, 0:1], 15, None, A.bitwise_and, None, 1, ["pi0"], ["pi1"])
+    ts(T.pi[:, 2:3], T.pi[:, 0:1], 7, None, A.bitwise_and, None, 1, ["pi0"], ["pi2"])
+    ts(T.pi[:, 3:4], T.pi[:, 0:1], 3, 1, A.arith_shift_right, A.bitwise_and, 1, ["pi0"], ["pi3"])
+    cp(T.pf[:, 1:5], T.pi[:, 1:5], 4, ["pi1", "pi2", "pi3", "pi4"], ["pf"])
+    ts(T.pf[:, 6:7], T.pi[:, 4:5], 3.0, 2.0, A.mult, A.add, 1, ["pi4"], ["pf6"])
+    for c in range(NC):
+        iota(T.cb[:, :, H0[c]:H0[c] + HS[c]], [[0, 12], [226, HS[c]]], 0, 0, 12 * HS[c], ["cb%d" % c], False)
+    cbs = ["cb%d" % c for c in range(NC)]
+    iota(T.ib[:, :], [[1, 8], [0, 16]], 0, 0, 128, ["ib"])
+    iota(T.ik[:, :], [[0, 8], [1, 16]], 0, 0, 128, ["ik"])
+    iota(T.ic[:, :], [[16, 8], [0, 16]], DUM - 2048 + 30000, 0, 128, ["ic"])
+    iota(T.id3[:, :], [[1, 8], [0, 3]], 0, 0, 24, ["id3"])
+    for c in range(NC):
+        iota(T.dm[:, H0[c]:H0[c] + HS[c]], [[16, HS[c]]], DUM, 0, HS[c], ["dm%d" % c])
+    iota(T.dm[:, 16:24], [[16, 8]], DUM, 0, 8, ["dmx"])
+    ts(T.blk[:, :], T.ib[:, :], T.pf[:, 4:5], None, A.is_equal, None, 128, ["ib", "pf"], ["blk"])
+    ts(T.hblk[:, :], T.ib[:, :], T.pf[:, 4:5], 0.5, A.is_equal, A.mult, 128, ["ib", "pf"], ["hblk"])
+    ts(T.eye[:, :], T.ia[:, 0:128], T.pf[:, 0:1], None, A.is_equal, None, 128, ["ia", "pf0"], ["eye"])
+    ts(T.neye[:, :], T.ia[:, 0:128], T.pf[:, 0:1], -4096.0, A.is_equal, A.mult, 128, ["ia", "pf0"], ["neye"])
+    ts(T.t2[:, :], T.ik[:, :], T.pf[:, 1:2], -1.0, A.is_gt, A.mult, 128, ["ik", "pf"], ["t2"])
+    tt(T.t2[:, :], T.t2[:, :], T.blk[:, :], A.mult, 128, ["t2", "blk"], ["t2"], TT)
+    tt(T.imt[:, :], T.t2[:, :], T.eye[:, :], A.add, 128, ["t2", "eye"], ["imt"], TT)
+    ts(T.zo[:, :], T.ia[:, 0:32], T.pf[:, 6:7], None, A.is_equal, None, 32, ["ia", "pf6"], ["zo"])
+    ts(T.of[:, :], T.id3[:, :], T.pf[:, 4:5], 1.0 / 4096, A.is_equal, A.mult, 24, ["id3", "pf"], ["of"])
+    ts(T.sk[:, :], T.ia[:, 0:16], T.pf[:, 1:2], -1.0, A.is_equal, A.mult, 16, ["ia", "pf"], ["sk"])
+    for k in range(16):
+        act(T.nr[:, k, :], T.blk[:, :], AF.Identity, 128, ["blk", "sk"], ["nr%d" % k], scale=T.sk[:, k:k + 1])
+    nrs = ["nr%d" % k for k in range(16)]
+    add("G", 170 + 1.66 * 2048, nrs, ["ee"],
+        lambda g: g.affine_select(T.ee[:, :, :], T.nr[:, :, :], [[0, 16], [-1, 128]], A.not_equal, 1.0, 0, 1))
+    ts(T.tm[:, :], T.ik[:, :], T.pf[:, 1:2], None, A.is_lt, None, 128, ["ik", "pf"], ["tm"])
+    ts(T.ic[:, :], T.ic[:, :], T.pf[:, 1:2], None, A.add, None, 128, ["ic", "pf"], ["ic"])
+    tt(T.tm[:, :], T.tm[:, :], T.ic[:, :], A.mult, 128, ["tm", "ic"], ["tm"])
+    ts(T.c1[:, :], T.tm[:, :], -30000.0, None, A.add, None, 128, ["tm"], ["c1"])
+    ts(T.rs[:, :], T.ik[:, :], 0.0, None, A.is_gt, None, 128, ["ik"], ["rs"])
+    ms(T.cv[:, 4096:4112], 0.0, 16, ["cvz"])
+    ms(T.zero[:, :, :], 0.0, 384, ["zero"])
+    ms(T.tie[:, 0, :], 2.0, 8, ["tie0"]); ms(T.tie[:, 1, :], 1.0, 8, ["tie1"]); ms(T.tie[:, 2:4, :], 0.0, 16, ["tie2"])
+    ms(T.uo[:, :, :], 0, 96 * NC, ["uoz"])
+    ts(T.fo[:, :, :, :], T.ls[:, 0:2 * NC, 0:48], 0.0, None, A.mult, None, 96 * NC, ["lsz"], ["foz"])
+    ops.insert(len(ops) - 1, dict(e="V", ns=vns(96 * NC), rd=[], wr=["lsz"], kind=None,
+                                  fn=lambda g: g.vector.memset(T.ls[:, 0:2 * NC, 0:48], 0.0)))
+    ms(T.ww[:, 448:464], 0.0, 32, ["wwz"])
+    ts(T.ww[:, 432:448], T.dm[:, 0:16], T.pf[:, 1:2], None, A.add, None, 16, ["pf"] + ["dm%d" % c for c in range(NC)], ["wwd"])
+    for c in range(NC):
+        ts(T.si[:, c, 104:112], T.dm[:, 16:24], T.pf[:, 1:2], None, A.add, None, 8, ["pf", "dmx"], ["sid%d" % c])
+    ev = [16 * CAND1[2 * i] for i in range(28)] + [8 * CAND2[2 * i] for i in range(16)]
+    df = [16 * (CAND1[2 * i + 1] - CAND1[2 * i]) for i in range(28)] + [8 * (CAND2[2 * i + 1] - CAND2[2 * i]) for i in range(16)]
+    tabs = []
+    for i, n, b, st in runs(ev + df):
+        tabs.append("tab%d" % i); iota(T.tab[:, i:i + n], [[st, n]], b, 0, n, [tabs[-1]])
+    iota(T.tab[:, 88:116], [[8, 4], [0, 7]], 0, 0, 28, ["tr1"]); iota(T.tab[:, 116:132], [[8, 4], [0, 4]], 0, 0, 16, ["tr2"])
+    iota(T.tab[:, 132:136], [[0, 4]], 0, 0, 4, ["tr3"])
+    ts(T.tb2[:, 0:44], T.tab[:, 44:88], T.pf[:, 3:4], T.pf[:, 2:3], A.mult, A.add, 44, tabs + ["pf"], ["tb2"])
+    tt(T.tb3[:, 0:44], T.tb2[:, 0:44], T.tab[:, 0:44], A.add, 44, tabs + ["tb2"], ["tb3"])
+    for c in range(NC):
+        ts(T.o1[:, c, :], T.tb3[:, 0:28], float(H0[c]), None, A.add, None, 28, ["tb3"], ["o1%d" % c])
+    cp(T.o2[:, :], T.tb3[:, 28:44], 16, ["tb3"], ["o2"])
+    ts(T.orp[:, :], T.tab[:, 88:136], T.pf[:, 2:3], None, A.add, None, 48, ["tr1", "tr2", "tr3", "pf"], ["orp"])
+
+    def star(j, n=1): return T.ob[:, 256 * j:256 * (j + n)]
+    for i in range(6):
+        tt(T.gp[:, i, :], star(PAIRS[i][0]), star(PAIRS[i][1]), A.mult, 256, ["ob0"], ["gp%d" % i], TT)
+    for i in (6, 8, 10, 12):
+        tt(T.gp[:, i:i + 2, :], star(PAIRS[i][0], 2), star(4, 2) if i < 12 else star(4, 2), A.mult, 512, ["ob0", "ob1"], ["gp%d" % i], TT)
+    tt(T.gp[:, 14, :], star(0), star(5), A.mult, 256, ["ob0", "ob1"], ["gp14"], TT)
+    def L(k): return T.zz[:, 15 - k:143 - k]
+    def gram(bank, a, b, rd, tok):
+        mm([(bank[:, 0:16 * (b - a)], L(k), T.gp[:, a:b, 16 * k:16 * k + 16], k == 0, k == 15) for k in range(16)],
+           16 * max(64, 16 * (b - a)), rd + ["zz"], [tok])
+    gram(T.pf1, 0, 3, ["gp0", "gp1", "gp2"], "pf1")
+    gram(T.pe, 3, 6, ["gp3", "gp4", "gp5"], "pe")
+    gram(T.pl, 6, 15, ["gp6", "gp8", "gp10", "gp12", "gp14"], "pl")
+    cp(T.gi[:, 0:48], T.pf1[:, 0:48], 48, [], ["pf1", "gi0"])
+    ts(T.gs[:, 0:48], T.gi[:, 0:48], 4, None, A.arith_shift_right, None, 48, ["gi0"], ["gs0"])
+    tt(T.s0[:, 0:3, :], T.gs[:, 0:48], T.cb[:, 0:3, :], A.add, 48, ["gs0"] + cbs, ["s0a"])
+    ts(T.s0[:, 3:6, :], T.pe[:, 0:48], -OFF, None, A.add, None, 48, [], ["pe", "s0b"])
+    cp(T.gi[:, 48:96], T.pe[:, 0:48], 48, [], ["pe", "gi1"])
+    cp(T.gi[:, 96:240], T.pl[:, 0:144], 144, [], ["pl", "gi2"])
+    act(T.ww[:, 288:432], T.pl[:, 0:144], AF.Identity, 144, [], ["pl", "ww3"], bias=-OFF)
+    act(T.ww[:, 0:96], T.s0[:, :, :], AF.Identity, 96, ["s0a", "s0b"], ["ww1"])
+    ts(T.gs[:, 48:240], T.gi[:, 48:240], 4, None, A.arith_shift_right, None, 192, ["gi1", "gi2"], ["gs1"])
+    tt(T.ww[:, 96:288], T.gs[:, 48:240], T.cb[:, :, :], A.add, 192, ["gs1"] + cbs, ["ww2"])
+
+    rid, pid, _ = topo.addr(nxt)
+    eng = topo.engines(core, nxt)[:8]
+    def mask(es): return sum(1 << e for e in es)
+
+    def convert(src, h0, t, c, ut, ft, rd, wr, utok, ftok):
+        H, o, one = HS[c], 0, len(SB[t][c]) == 1
+        for s, (n, kd) in enumerate(SB[t][c]):
+            cp(ut[:, 3 * o:3 * (o + n)], src[:, 0:3, h0 + o:h0 + o + n], 3 * n, rd, wr + ([utok + "y"] if one else []) + [utok + "s%d" % s]); o += n
+        cp(ft[:, 0:4, 0:H], src[:, 2:6, h0:h0 + H], 4 * H, rd, wr + [ftok])
+        if not one: cp(ut[:, 24:24 + 3 * H], src[:, 0:3, h0:h0 + H], 3 * H, rd, wr + [utok + "y"])
+
+    eb, ec, ek, kb, kk = (T.pl, 256, "pl", T.ps, "ps") if "P" in "".join(SPLIT) else (T.pe, 0, "pe", T.pc, "pc")
+    for t in range(3):
+        for c in range(NC):
+            I = t * NC + c; H = HS[c]; n = 16 * H; tsb = T["ts%d" % c]; tk = "ts%d" % c
+            tks = ["ts%d_%d" % (c, s) for s in range(len(part[c]))]; fine = t == 0 and len(tks) > 1
+            U = "ui%d" % I; F = "fi%d" % I; pm = T["pm%d" % (I % 2)]; pmk = "pm%d" % (I % 2)
+            nsb = len(SB[t][c]); us = [U + "s%d" % s for s in range(nsb)]; y0 = 0 if nsb == 1 else 24
+            if t == 0: convert(T.s0, H0[c], 0, c, T.ui[:, I], T.fi[:, I], ["s0a", "s0b"], [], U, F)
+            win = tsb[:, 0:226 * H]
+            if fine:
+                o = 0
+                for s, x in enumerate(part[c]):
+                    a, b = T.nm[:, I, 48 * o:48 * (o + x)], tsb[:, 0:226 * (o + x)].indirect(T.ui[:, I, 3 * o:3 * (o + x)])
+                    add("V", 50 + 0.83 * GC * 48 * x, [us[s]] + tks[:s + 1], ["nm%d_%d" % (I, s)], lambda g, a=a, b=b: g.vector.tensor_copy(a, b))
+                    o += x
+            else:
+                a, b = T.nm[:, I, 0:3 * n], win.indirect(T.ui[:, I, 0:3 * H])
+                add("V", 50 + 0.83 * GC * 3 * n, us + tks, ["nm%d" % I], lambda g, a=a, b=b: g.vector.tensor_copy(a, b))
+            mm([(pm[:, 0:3, 0:n], T.eye[:, :], T.zero[:, :, 0:n], True, False)], 3 * n, ["eye", "zero"], [pmk])
+            dlist = [(pm[:, 0:3, k:n:16], T.nr[:, k, :], T.fi[:, I, 1:4, 0:H], False, False) for k in range(16)]
+            cw = T.cv[:, 0:4097]; o = 0
+            old = ["mm%d" % c] if t == 2 else []
+            for s, (ns, kd) in enumerate(SB[t][c]):
+                w = 256 * ns; l = 16 * ns
+                gvb = T["gv%d_%d" % (t % 2, c)]; prb = T["pr%d_%d" % (t % 2, c)]; e0 = 768 * o
+                def gv(a, b): return gvb[:, e0 + a:e0 + b]
+                def pr(a, b): return prb[:, e0 + a:e0 + b]
+                nt = "nm%d_%d" % (I, s) if fine else "nm%d" % I
+                G = "gv%d_%d" % (I, s); P = "pr%d_%d" % (I, s)
+                def lst(a, b): return cw.indirect(T.nm[:, I, 48 * o + a // 16:48 * o + b // 16])
+                rd = [nt, "cv", "cvz"] + old
+                last = s == nsb - 1; lt = ["mm%d" % c] if last and t == 0 else []
+                def red(a, b, toks, fin):
+                    mm([(pm[:, a:b, 16 * o:16 * o + l], L(p), prb[:, e0 + a * w + p:e0 + b * w:16], False, fin and p == 15) for p in range(16)],
+                       16 * max(64, (b - a) * l), ["zz"] + toks, [pmk] + (lt if fin else []))
+                if kd[0] == "N":
+                    u = 256 * int(kd[1:])
+                    act(gv(0, w), lst(0, w), AF.Copy, w, rd, [G + "b"], r=GC)
+                    act(gv(w, 2 * w), lst(w, 2 * w), AF.Copy, w, rd, [G + "c"], r=GC)
+                    tt(pr(0, w), gv(0, w), gv(w, 2 * w), A.mult, w, [G + "b", G + "c"], [P + "a"], TT)
+                    if u:
+                        act(gv(2 * w, 2 * w + u), lst(2 * w, 2 * w + u), AF.Copy, u, rd, [G], r=GC)
+                        tt(pr(w, w + u), gv(w, w + u), gv(2 * w, 2 * w + u), A.mult, u, [G, G + "c"], [P + "b"], TT)
+                        tt(pr(2 * w, 2 * w + u), gv(0, u), gv(2 * w, 2 * w + u), A.mult, u, [G, G + "b"], [P + "c"], TT)
+                    if u < w:
+                        gtt(pr(2 * w + u, 3 * w), lst(2 * w + u, 3 * w), gv(u, w), A.mult, w - u, rd + [G + "b"], [P + "e"])
+                        gtt(pr(w + u, 2 * w), lst(2 * w + u, 3 * w), gv(w + u, 2 * w), A.mult, w - u, rd + [G + "c"], [P + "d"])
+                    if s == 0: mm(dlist, 1024, nrs + [F], [pmk])
+                    red(0, 1, [P + "a"], False); red(1, 2, [P + "b", P + "d"], False); red(2, 3, [P + "c", P + "e"], last)
+                    o += ns
+                    continue
+                if kd == "W":
+                    act(gv(0, 3 * w), lst(0, 3 * w), AF.Copy, 3 * w, rd, [G], r=GC)
+                    tt(pr(0, 2 * w), gv(0, 2 * w), gv(w, 3 * w), A.mult, 2 * w, [G], [P + "a"], TT)
+                    tt(pr(2 * w, 3 * w), gv(0, w), gv(2 * w, 3 * w), A.mult, w, [G], [P + "b"], TT)
+                elif kd == "X":
+                    act(gv(0, 2 * w), lst(0, 2 * w), AF.Copy, 2 * w, rd, [G], r=GC)
+                    tt(pr(0, w), gv(0, w), gv(w, 2 * w), A.mult, w, [G], [P + "a"], TT)
+                    gtt(pr(w, 2 * w), lst(2 * w, 3 * w), gv(w, 2 * w), A.mult, w, rd + [G], [P + "b"])
+                    gtt(pr(2 * w, 3 * w), lst(2 * w, 3 * w), gv(0, w), A.mult, w, rd + [G], [P + "c"])
+                elif kd == "P":
+                    act(gv(0, 3 * w), lst(0, 3 * w), AF.Copy, 3 * w, rd, [G], r=GC)
+                    mm([(T.pc[:, :, :], T.eye[:, :], gv(w, 2 * w), True, True)], w, ["eye", G], ["pc"])
+                    mm([(T.pe[:, :], T.eye[:, :], gv(0, w), True, True)], w, ["eye", G], ["pe"])
+                    tt(pr(w, 2 * w), T.pc[:, :, :], gv(2 * w, 3 * w), A.mult, w, [G], ["pc", P + "b"], 1.0)
+                    tt(pr(0, w), T.pe[:, :], gv(w, 2 * w), A.mult, w, [G], ["pe", P + "a"], 1.0)
+                    tt(pr(2 * w, 3 * w), T.pe[:, :], gv(2 * w, 3 * w), A.mult, w, [G], ["pe", P + "c"], 1.0)
+                elif kd == "U":
+                    act(gv(0, 2 * w), lst(0, 2 * w), AF.Copy, 2 * w, rd, [G], r=GC)
+                    add("V", 50 + 0.83 * GC * w, rd, [G + "a"], lambda g, a=gv(2 * w, 3 * w), b=lst(2 * w, 3 * w): g.vector.tensor_copy(a, b))
+                    tt(pr(0, 2 * w), gv(0, 2 * w), gv(w, 3 * w), A.mult, 2 * w, [G, G + "a"], [P + "a"], TT)
+                    tt(pr(2 * w, 3 * w), gv(0, w), gv(2 * w, 3 * w), A.mult, w, [G, G + "a"], [P + "b"], TT)
+                else:
+                    act(gv(0, 2 * w), lst(0, 2 * w), AF.Copy, 2 * w, rd, [G], r=GC)
+                    gtt(pr(0, w), lst(w, 2 * w), gv(0, w), A.mult, w, rd + [G], [P + "a"])
+                    gtt(pr(2 * w, 3 * w), lst(2 * w, 3 * w), gv(0, w), A.mult, w, rd + [G], [P + "c"])
+                    gtt(pr(w, 2 * w), lst(2 * w, 3 * w), gv(w, 2 * w), A.mult, w, rd + [G], [P + "b"])
+                if s == 0: mm(dlist, 1024, nrs + [F], [pmk])
+                if last and I == 3 * NC - 1 and kd in "WU":
+                    red(0, 2, [P + "a"], False); red(2, 3, [P + "b"], True)
+                else: red(0, 3, [P + "a", P + "b", P + "c"], last)
+                o += ns
+            if t < 2:
+                J = I
+                mm([(eb[:, ec + k:ec + n:16], T.ee[:, k, :], T.fi[:, I, 0, 0:H], True, True) for k in range(16)], 1024, ["ee", F], [ek])
+                act(T.ae[:, J, 0:n], eb[:, ec:ec + n], AF.Abs, n, [], [ek, "ae%d" % J])
+                nq = 14 if t == 0 else 8
+                if t == 0:
+                    cand = T.cand1[:, c, :]
+                    act(cand, T.ww[:, :].indirect(T.o1[:, c, :]), AF.Copy, 448, ["ww1", "ww2", "ww3", "wwd", "wwz", "o1%d" % c], ["cand%d" % J], r=GC)
+                else:
+                    cand = T.cand2[:, c, :]
+                    act(cand, T.si[:, c, :].indirect(T.o2[:, :]), AF.Copy, 256, ["si%d" % c, "sid%d" % c, "o2"], ["cand%d" % J], r=GC)
+            act(T.ab[:, I, :, 0:n], pm[:, 0:3, 0:n], AF.Abs, 3 * n, [], [pmk, "ab%d" % I], bias=-OFF)
+            ts(T.hd[:, I, 0:3, 0:n], T.ab[:, I, :, 0:n], 130.0, 16.0, A.is_le, A.mult, 3 * n, ["ab%d" % I], ["hd%d" % I], 0.5)
+            if I < EVS:
+                mm([(T.pf1[:, 128:128 + n], T.eye[:, :], T.hd[:, I, e, 0:n], e == 0, e == 2) for e in range(3)], 3 * n, ["eye", "hd%d" % I], ["pf1"])
+                act(T.hd[:, I, 3, 0:n], T.pf1[:, 128:128 + n], AF.Relu, n, [], ["pf1", "ev%d" % I], bias=-8192.0, scale=256.0)
+            else:
+                tt(T.h2[:, I, 0:n], T.hd[:, I, 0, 0:n], T.hd[:, I, 1, 0:n], A.mult, n, ["hd%d" % I], ["h2%d" % I], TT)
+                tt(T.hd[:, I, 3, 0:n], T.h2[:, I, 0:n], T.hd[:, I, 2, 0:n], A.mult, n, ["hd%d" % I, "h2%d" % I], ["ev%d" % I], TT)
+            if t < 2:
+                mm([(kb[:, 32:36, :], T.eye[:, :], T.tie[:, :, :], True, False)] +
+                   [(kb[:, 32:36, 0:H], L(k), T.hd[:, I, :, k:n:16], False, k == 15) for k in range(16)], 1088,
+                   ["eye", "tie0", "tie1", "tie2", "zz", "hd%d" % I, "ev%d" % I], [kk])
+            mm([(T.pf1[:, 0:n], T.imt[:, :], T.hd[:, I, 3, 0:n], True, True)], n, ["imt", "ev%d" % I], ["pf1"])
+            act(T.ff[:, I, 0:n], T.pf1[:, 0:n], AF.Relu, n, [], ["pf1", "ff%d" % I])
+            if t < 2:
+                if SCS: act(T.sc[:, J, :], kb[:, 32:36, :], AF.Identity, 32, [], [kk, "sc%d" % J])
+                else: cp(T.sc[:, J, :], kb[:, 32:36, :], 32, [], [kk, "sc%d" % J])
+                tt(T.m1[:, J, :], T.sc[:, J, 0:16], T.sc[:, J, 16:32], A.max, 16, ["sc%d" % J], ["m1%d" % J])
+                tt(T.m2[:, J, :], T.m1[:, J, 0:8], T.m1[:, J, 8:16], A.max, 8, ["m1%d" % J], ["m2%d" % J])
+                gtt(T.mk[:, J, :], T.m2[:, J, :].indirect(T.orp[:, 44:46]), T.sc[:, J, :], A.is_equal, 32, ["m2%d" % J, "sc%d" % J, "orp"], ["mk%d" % J])
+                rep = T.orp[:, 0:28] if t == 0 else T.orp[:, 28:44]
+                gtt(T.msk[:, J, 0:32 * nq], T.mk[:, J, :].indirect(rep), cand, A.mult, 32 * nq, ["mk%d" % J, "cand%d" % J, "orp"], ["msk%d" % J])
+                mm([(T.ps[:, 0:nq, :], T.eye[:, :], T.msk[:, J, 8 * nq * q:8 * nq * (q + 1)], q == 0, q == 3) for q in range(4)],
+                   4 * max(64, 8 * nq), ["eye", "msk%d" % J], ["ps"])
+                convert(T.ps, 0, t + 1, c, T.uo[:, J], T.fo[:, J], ["uoz", "foz"], ["ps"], "uo%d" % J, "fo%d" % J)
+                N = I + NC; nsb = len(SB[t + 1][c])
+                def snd(g, J=J, N=N):
+                    d = [DstId(rid=rid, pnc=pid)]
+                    return g.remote_dma_fused([
+                        RemoteDMATransfer(dst_ids=d, dma_engine_mask=mask(eng[:4]), remote_sem=T.sem["r%d" % J], src=T.uo[:, J], dst=T.ui[:, N]),
+                        RemoteDMATransfer(dst_ids=d, dma_engine_mask=mask(eng[4:]), remote_sem=T.sem["r%d" % J], src=T.fo[:, J], dst=T.fi[:, N])],
+                        local_sem=T.sem.sent)
+                add("G", 300, ["uo%ds%d" % (J, s) for s in range(nsb)] + ["uo%dy" % J, "fo%d" % J],
+                    ["ui%ds%d" % (N, s) for s in range(nsb)] + ["ui%dy" % N, "fi%d" % N], snd, "r%d" % J)
+                if t == 0:
+                    act(T.so[:, c, :], T.ps[:, 0:13, :], AF.Identity, 104, [], ["ps", "so%d" % c])
+                    add("G", 300, ["so%d" % c], ["si%d" % c], lambda g, c=c: g.remote_dma(
+                        T.si[:, c, 0:104], T.so[:, c, :], T.sem["r%d" % (2 * NC + c)], T.sem.sent, pid, rid, mask(eng)), "r%d" % (2 * NC + c))
+                mm([(T.pl[:, 0:n], T.eye[:, :], T.c1[:, 0:n], True, False), (T.pl[:, 0:n], T.neye[:, :], T.ae[:, J, 0:n], False, False),
+                    (T.pl[:, 0:n], T.hblk[:, :], T.ff[:, I, 0:n], False, True)], 3 * n, ["eye", "neye", "hblk", "c1", "ae%d" % J, "ff%d" % I], ["pl"])
+                add("V", vns(n), ["rs", "foz"], ["pl", "ls%d" % J], lambda g, J=J, n=n: g.vector.tensor_tensor_scan(
+                    T.ls[:, J, 0:n], T.rs[:, 0:n], T.pl[:, 0:n], 0.0, A.mult, A.max))
+                tt(T.sf[:, J, 0:H], T.ls[:, J, 15:n:16], T.ps[:, 13 if t == 0 else 6, 0:H], A.max, H, ["ls%d" % J], ["ps", "sf%d" % J])
+                cp(T.su[:, J, 0:H], T.sf[:, J, 0:H], H, ["sf%d" % J], ["su%d" % J])
+                gtt(T.sv[:, J, 0:n], win.indirect(T.ui[:, I, y0 + 2 * H:y0 + 3 * H]), T.ff[:, I, 0:n], A.max, n, tks + [U + "y", "ff%d" % I], ["sv%d" % J])
+            Y = "yy%d" % (I % 2)
+            for m in range(3):
+                x = (m + 2) % 3
+                gtt(T.yy[:, I % 2, m, 0:n], win.indirect(T.ui[:, I, y0 + x * H:y0 + (x + 1) * H]), T.ff[:, I, 0:n], A.min, n,
+                    tks + [U + "y", "ff%d" % I], [Y + str(m)])
+            if t < 2:
+                add("V", 50 + 0.83 * SC * n, ["su%d" % J, "sv%d" % J], tks, lambda g, J=J, n=n, H=H, tsb=tsb: g.vector.tensor_copy(
+                    tsb[:, 0:1936].indirect(T.su[:, J, 0:H]), T.sv[:, J, 0:n]))
+            ml = []
+            for h in range(H):
+                ml.append((T.po[0:24, :, h], T.of[:, :], T.ff[:, I, 16 * h:16 * h + 16], True, False))
+                for m in range(3):
+                    ml.append((T.po[0:24, :, h], T.zo[:, 2 - m:26 - m], T.yy[:, I % 2, m, 16 * h:16 * h + 16], False, m == 2))
+            mm(ml, H * 24 * 13, ["of", "zo", "ff%d" % I, Y + "0", Y + "1", Y + "2"], ["po"])
+            act(T.yb[0:24, t, :, H0[c]:H0[c] + H], T.po[0:24, :, 0:H], AF.Identity, n, [], ["po", "yb%d" % I], bias=-1.0)
+        dma(T.yn[:, 768 * t:768 * (t + 1)], T.yb[0:24, t], 24 * 1024, ["yb%d" % (t * NC + c) for c in range(NC)], ["yn%d" % t])
+    return ops
+
+
+def plan(ops, alt=(), dma0=2000.0, tries=TRIES):
+    lw, lr = {}, {}
+    for i, o in enumerate(ops):
+        d = set()
+        if o["e"] != "P":
+            for k in [k for k in o["wr"] if k in BANKS]:
+                o["wr"].remove(k); o["rd"] = o["rd"] + [k]
+        for k in o["rd"]:
+            if k in BANKS and o["e"] != "P": d.update(j for j in lr.get(k, []) if ops[j]["e"] != o["e"])
+        for k in o["rd"] + o["wr"]:
+            if k in lw: d.add(lw[k])
+        for k in o["wr"]: d.update(lr.get(k, []))
+        d.discard(i); o["dep"] = sorted(d)
+        for k in o["rd"]: lr.setdefault(k, []).append(i)
+        for k in o["wr"]: lw[k] = i; lr[k] = []
+    if tries < 0: return None
+    hop, wire = FIGS[0][3:]
+    n = len(ops); en = [o["e"] for o in ops]; ns = [o["ns"] for o in ops]
+    lat = [dma0 if o["kind"] == "dma" else wire if o["kind"] else 0.0 for o in ops]
+    pre = [[(j, lat[j] + (0.0 if en[j] == "P" == en[i] else hop)) for j in ops[i]["dep"]] for i in range(n)]
+    ys = [i for i in range(n) if en[i] == "Y"]
+    for a, b in zip(ys, ys[1:]): pre[b].append((a, 0.0))
+    suc = [[] for _ in ops]
+    for i in range(n):
+        for j, l in pre[i]: suc[j].append((i, l))
+
+    def place(seq, before, tail):
+        end = [0.0] * n; busy = {e: [] for e in "VSPGY"}
+        for i in seq:
+            t = tail[i]
+            for j, l in before[i]:
+                if end[j] + l > t: t = end[j] + l
+            b = busy[en[i]]; k = len(b); d = ns[i]
+            while k > 0 and b[k - 1][1] > t: k -= 1
+            while k < len(b) and b[k][0] < t + d:
+                if b[k][1] > t: t = b[k][1]
+                k += 1
+            b.insert(k, (t, t + d)); end[i] = t + d
+        return end
+
+    def topo_sort(key):
+        k2 = list(key)
+        for i in range(n):
+            for j, l in pre[i]:
+                if k2[j] >= k2[i]: k2[i] = k2[j] + 1e-6
+        return sorted(range(n), key=lambda i: (k2[i], i))
+
+    zero = [0.0] * n
+    def both(seq):
+        end = place(seq, pre, zero)
+        back = place(sorted(range(n), key=lambda i: (-end[i] - lat[i], -i)), suc, lat)
+        end = place(sorted(range(n), key=lambda i: (-back[i], i)), pre, zero)
+        ts = [max(end[i] + lat[i] for i in range(n))]
+        seq = sorted(range(n), key=lambda i: end[i] - ns[i] * 0.999)
+        for ns2, pre2, lat2 in others:
+            free = {e: 0.0 for e in "VSPGY"}; e2 = [0.0] * n
+            for i in seq:
+                t = free[en[i]]
+                for j, l in pre2[i]:
+                    if e2[j] + l > t: t = e2[j] + l
+                e2[i] = free[en[i]] = t + ns2[i]
+            ts.append(max(e2[i] + lat2[i] for i in range(n)))
+        return sum(ts) / len(ts), (end, ts)
+
+    others = []
+    for ns2, h2, w2 in alt:
+        lat2 = [dma0 if o["kind"] == "dma" else w2 if o["kind"] else 0.0 for o in ops]
+        others.append((ns2, [[(j, lat2[j] + (0.0 if en[j] == "P" == en[i] else h2)) for j in ops[i]["dep"]] for i in range(n)], lat2))
+    rnd = np.random.RandomState(1)
+    best, (end, each) = both(list(range(n)))
+    now, cur = best, end
+    for it in range(tries):
+        jit = (rnd.uniform(0.0, 1.0, n) ** 3 * (300.0, 1000.0, 2500.0)[it % 3]).tolist()
+        a = rnd.uniform(-5000.0, each[0]); b = a + rnd.uniform(3000.0, 15000.0)
+        t, e2 = both(topo_sort([cur[i] - ns[i] + (jit[i] if a <= cur[i] <= b else 0.0) for i in range(n)]))
+        if t <= now + 400.0 * (1.0 - it / tries) * rnd.uniform(): now, cur = t, e2[0]
+        if t <= best: best, (end, each) = t, e2
+    order = {e: sorted((i for i in range(n) if en[i] == e), key=lambda i: end[i]) for e in "VSPGY"}
+    for i in range(n): ops[i]["t0"] = end[i] - ns[i]
+    return order, each
+
+
+ORDER = {}
+
+
+def rank_program(g, core, T, topo):
+    rank = T.rank_of(core)
+    if rank is None:
+        return
+    nxt = T.cores[(rank + 1) % len(T.cores)]
+    ops = build(T, nxt, topo, core)
+    if not ORDER: ORDER.update(plan(ops, [([o["ns"] for o in build(T, nxt, topo, core, f)], f[3], f[4]) for f in FIGS[1:]])[0])
+    else: plan(ops, tries=-1)
+    order = ORDER
+    pos = {i: k for e in order for k, i in enumerate(order[e])}
+    nd = 0
+    for i in order["Y"]: ops[i]["sem"] = "d%d" % nd; nd += 1
+    need = set(); waits = {}
+    for e in order:
+        seen = {}
+        for i in order[e]:
+            w = {}
+            for j in ops[i]["dep"]:
+                o = ops[j]
+                if o["kind"]:
+                    key = o.get("sem", o["kind"])
+                    if key not in seen: seen[key] = 1; w[key] = j
+                elif not (o["e"] == "P" == e) and pos[j] > seen.get(o["e"], -1) and pos[j] > pos.get(w.get(o["e"]), -1):
+                    w[o["e"]] = j
+            for k, j in w.items():
+                if not ops[j]["kind"]: seen[k] = pos[j]; need.add(j)
+            waits[i] = w
+    cnt = {}
+    for e in order:
+        c = 0
+        for i in order[e]:
+            if i in need: c += 1; cnt[i] = c
+    q = {"V": g.vector, "S": g.scalar, "P": g.tensor, "G": g, "Y": g.sync}
+    sent = 0
+    for e in order:
+        for i in order[e]:
+            o = ops[i]
+            for k, j in waits[i].items():
+                if ops[j]["kind"] == "dma": q[e].wait_ge(T.sem[k], 16)
+                elif ops[j]["kind"]: q[e].wait_ge(T.sem[k], 8)
+                else: q[e].wait_ge(T.sem["e" + k], cnt[j])
+            r = o["fn"](g)
+            if o["kind"] == "dma": r.then_inc(T.sem[o["sem"]], 16)
+            elif o["kind"]: sent += 8
+            elif i in need: r.then_inc(T.sem["e" + e], 1)
+    g.wait_ge(T.sem.sent, sent)
+    for i in order["Y"]:
+        if ops[i]["wr"][0].startswith("yn"): g.sync.wait_ge(T.sem[ops[i]["sem"]], 16)

@@ -2,80 +2,76 @@ import numpy as np
 from concourse.bass import DstId, RemoteDMATransfer
 from concourse.mybir import AluOpType as A, ActivationFunctionType as AF
 
-SPLIT = ["2U,2W,2W 2W,2W,2W 2W,2W", "2W,2W,2W 2W,2W,2W 2W,2W", "2W,2X,2W 2W,2W,2W 2W,2W"]
-OBALL = 1
-EVS = 8
-FINE = 2
+SPLIT = ["UWWW WWWW", "WWWW WWWW", "WWWW WWWW"]
+FINE = 1
+EVS = 5
 SCS = 0
-TT = 1.0
-FIGS = [(1.56, 3.8, 0.42, 150.0, 3500.0), (1.1, 2.0, 0.42, 120.0, 3000.0), (2.0, 5.5, 0.42, 120.0, 3000.0), (1.56, 3.8, 0.55, 250.0, 5000.0)]
-TRIES = 1200
-SB = [[[(int(x[0]), x[1:]) for x in c.split(",")] for c in r.split()] for r in SPLIT]
+FIGS = [(1.56, 3.8, 0.42, 120.0, 2200.0), (1.1, 2.0, 0.42, 100.0, 1800.0), (2.0, 5.5, 0.42, 100.0, 2200.0), (1.56, 3.8, 0.55, 200.0, 4000.0)]
+TRIES = 600
+SB = [r.split() for r in SPLIT]
 NC = len(SB[0])
-HS = [sum(x[0] for x in c) for c in SB[0]]
+HS = [2 * len(c) for c in SB[0]]
 H0 = [sum(HS[:c]) for c in range(NC)]
 DUM = 1808
 OFF = 1800.0
+BIG = 12582912.0
+CW = 251.0 / 65536
 
-PAIRS = [(0, 2), (0, 3), (0, 1), (2, 3), (1, 3), (1, 2), (0, 4), (1, 5), (1, 4), (2, 5), (2, 4), (3, 5), (3, 4), (4, 5), (0, 5)]
-
-
-def _col(x, y):
-    i = PAIRS.index((min(x, y), max(x, y)))
-    return i if i < 3 else i + 3
+PAIRS = [(2, 3), (1, 3), (1, 2), (0, 4), (1, 5), (1, 4), (2, 5), (2, 4), (3, 5), (3, 4), (4, 5), (0, 5), (0, 2), (0, 3), (0, 1)]
 
 
-def _val(x, y):
-    i = PAIRS.index((min(x, y), max(x, y)))
-    return i if i < 6 else i + 12
+def _col(x, y): return PAIRS.index((min(x, y), max(x, y)))
+def _val(x, y): return 15 + _col(x, y)
 
 
 def _cand1():
     out = []
-    for n, (o, a, b, c) in enumerate([(0, 4, 2, 3), (0, 1, 4, 3), (0, 1, 2, 4), (1, 2, 3, 4)]):
+    for o, a, b, c in [(0, 4, 2, 3), (0, 1, 4, 3), (0, 1, 2, 4), (1, 2, 3, 4)]:
         out += [_col(o, b), _col(o, c), _col(o, a), _val(b, c), _val(a, c), _val(a, b), _col(o, 5), _col(a, b), _col(a, c),
-                _col(a, 5), _val(a, 5), _val(b, 5), _val(c, 5), _col(0, 1) if n == 3 else 27]
+                _col(a, 5), _val(a, 5), _val(b, 5), _val(c, 5)]
     return out
 
 
 CAND1 = _cand1()
-CAND2 = [0, 1, 6, 3, 12, 11, 13, 13, 6, 1, 2, 12, 4, 10, 13, 13, 0, 6, 2, 11, 10, 5, 13, 13, 8, 9, 7, 12, 11, 3, 2, 13]
+CAND2 = [0, 1, 6, 3, 12, 11, 6, 1, 2, 12, 4, 10, 0, 6, 2, 11, 10, 5, 8, 9, 7, 12, 11, 3]
+NQ = (13, 6)
 
 SCRATCH = {
-    "cv": ("sbuf", [128, 4112], "bfloat16"), "ob": ("sbuf", [128, 1536], "bfloat16"), "gp": ("sbuf", [128, 15, 256], "bfloat16"),
-    "pi": ("sbuf", [128, 8], "int32"), "pf": ("sbuf", [128, 8], "float32"),
-    "ia": ("sbuf", [128, 144], "float32"), "ib": ("sbuf", [128, 128], "float32"), "ik": ("sbuf", [128, 128], "float32"),
-    "ic": ("sbuf", [128, 128], "float32"), "id3": ("sbuf", [128, 24], "float32"), "tm": ("sbuf", [128, 128], "float32"),
+    "cv": ("sbuf", [128, 4112], "bfloat16"), "ob": ("sbuf", [128, 1536], "bfloat16"), "gp": ("sbuf", [128, 12, 256], "bfloat16"),
+    "gp0": ("sbuf", [128, 16, 8, 3, 2], "bfloat16"), "pi": ("sbuf", [128, 8], "int32"), "pf": ("sbuf", [128, 8], "float32"),
+    "ia": ("sbuf", [128, 144], "float32"), "ib": ("sbuf", [128, 128], "float32"), "ik": ("sbuf", [128, 8, 18], "float32"),
+    "ij": ("sbuf", [128, 128], "float32"), "ic": ("sbuf", [128, 8, 18], "float32"), "id3": ("sbuf", [128, 24], "float32"),
+    "tm": ("sbuf", [128, 8, 18], "float32"), "one": ("sbuf", [128, 128], "float32"), "cb0": ("sbuf", [128, 8, 3, 2], "float32"),
     "blk": ("sbuf", [128, 128], "bfloat16"), "hblk": ("sbuf", [128, 128], "bfloat16"), "eye": ("sbuf", [128, 128], "bfloat16"),
-    "neye": ("sbuf", [128, 128], "bfloat16"), "imt": ("sbuf", [128, 128], "bfloat16"), "t2": ("sbuf", [128, 128], "bfloat16"),
-    "zz": ("sbuf", [128, 144], "bfloat16"), "zo": ("sbuf", [128, 32], "float32"), "of": ("sbuf", [128, 24], "bfloat16"),
+    "neye": ("sbuf", [128, 128], "bfloat16"), "ceye": ("sbuf", [128, 128], "bfloat16"), "imt": ("sbuf", [128, 128], "bfloat16"),
+    "t2": ("sbuf", [128, 128], "bfloat16"), "zz": ("sbuf", [128, 144], "bfloat16"), "zc": ("sbuf", [128, 144], "bfloat16"),
+    "zs": ("sbuf", [128, 144], "bfloat16"), "zo": ("sbuf", [128, 32], "bfloat16"), "of": ("sbuf", [128, 2, 24], "bfloat16"),
     "sk": ("sbuf", [128, 16], "float32"), "nr": ("sbuf", [128, 16, 128], "bfloat16"), "ee": ("sbuf", [128, 16, 128], "bfloat16"),
-    "c1": ("sbuf", [128, 128], "float16"), "rs": ("sbuf", [128, 128], "float32"), "tie": ("sbuf", [128, 4, 8], "bfloat16"),
-    "zero": ("sbuf", [128, 3, 128], "bfloat16"), "cb": ("sbuf", [128, 12, 16], "int32"), "gi": ("sbuf", [128, 240], "int32"),
-    "gs": ("sbuf", [128, 240], "int32"), "s0": ("sbuf", [128, 6, 16], "float32"), "ww": ("sbuf", [128, 464], "float32"),
-    "dm": ("sbuf", [128, 24], "float32"), "tab": ("sbuf", [128, 136], "float32"), "tb2": ("sbuf", [128, 48], "float32"),
-    "tb3": ("sbuf", [128, 48], "float32"), "o1": ("sbuf", [128, NC, 28], "uint16"), "o2": ("sbuf", [128, 16], "uint16"),
-    "orp": ("sbuf", [128, 48], "uint16"),
-    "cand1": ("sbuf", [128, NC, 448], "float32"), "cand2": ("sbuf", [128, NC, 256], "float32"),
-    "msk": ("sbuf", [128, 2 * NC, 448], "float16"), "sc": ("sbuf", [128, 2 * NC, 32], "float32"),
-    "m1": ("sbuf", [128, 2 * NC, 16], "float32"), "m2": ("sbuf", [128, 2 * NC, 8], "float32"), "mk": ("sbuf", [128, 2 * NC, 32], "float32"),
-    "uo": ("sbuf", [128, 2 * NC, 48], "uint16"), "fo": ("sbuf", [128, 2 * NC, 6, 8], "float16"), "so": ("sbuf", [128, NC, 104], "float32"),
-    "ui": ("sbuf", [128, 3 * NC, 48], "uint16"), "fi": ("sbuf", [128, 3 * NC, 6, 8], "float16"), "si": ("sbuf", [128, NC, 112], "float32"),
-    "nm": ("sbuf", [128, 3 * NC, 384], "uint16"), "ab": ("sbuf", [128, 3 * NC, 3, 128], "bfloat16"),
+    "c1": ("sbuf", [128, 8, 18], "float16"), "rs": ("sbuf", [128, 144], "float32"), "tie": ("sbuf", [128, 4, 8], "bfloat16"),
+    "k18": ("sbuf", [128, 3, 128], "bfloat16"), "cb": ("sbuf", [128, 15, 16], "float32"), "gs": ("sbuf", [128, 240], "float32"),
+    "ww": ("sbuf", [128, 448], "float32"), "tab": ("sbuf", [128, 160], "float32"), "tb2": ("sbuf", [128, 80], "float32"),
+    "tb3": ("sbuf", [128, 80], "float32"), "o1": ("sbuf", [128, NC, 26], "uint16"), "ol": ("sbuf", [128, 52], "uint16"),
+    "ui0": ("sbuf", [128, 48], "uint16"), "ua0": ("sbuf", [128, 16], "uint16"), "fi0": ("sbuf", [128, 4, 16], "float16"),
+    "cand1": ("sbuf", [128, NC, 416], "float32"), "cand2": ("sbuf", [128, NC, 192], "float32"),
+    "msk": ("sbuf", [128, 2 * NC, 416], "float16"), "sc": ("sbuf", [128, 2 * NC, 32], "float32"),
+    "m1": ("sbuf", [128, 2 * NC, 16], "float32"), "m2": ("sbuf", [128, 2 * NC, 8], "float32"), "mk": ("sbuf", [128, 2 * NC, 32], "bfloat16"),
+    "uo": ("sbuf", [128, 2 * NC, 128], "uint16"), "ui": ("sbuf", [128, 2 * NC, 128], "uint16"),
+    "fi": ("sbuf", [128, 2 * NC, 4, 8], "float16"), "si": ("sbuf", [128, NC, 104], "float32"),
+    "nm": ("sbuf", [128, 3 * NC, 384], "uint16"), "nf": ("sbuf", [128, 3 * NC, 4, 3, 32], "float16"),
     "hd": ("sbuf", [128, 3 * NC, 4, 128], "bfloat16"), "h2": ("sbuf", [128, 3 * NC, 128], "bfloat16"),
-    "ff": ("sbuf", [128, 3 * NC, 128], "bfloat16"), "ae": ("sbuf", [128, 2 * NC, 128], "bfloat16"),
-    "yy": ("sbuf", [128, 2, 3, 128], "float32"), "sv": ("sbuf", [128, 2 * NC, 128], "int32"), "ls": ("sbuf", [128, 2 * NC, 128], "float32"),
-    "sf": ("sbuf", [128, 2 * NC, 8], "float32"), "su": ("sbuf", [128, 2 * NC, 8], "uint16"), "yb": ("sbuf", [128, 3, 16, 16], "float32"),
+    "ff": ("sbuf", [128, 3 * NC, 128], "bfloat16"), "ae": ("sbuf", [128, 2 * NC, 8, 18], "bfloat16"),
+    "yy": ("sbuf", [128, 3 * NC, 3, 128], "float16"), "sv": ("sbuf", [128, 2 * NC, 128], "int32"), "ls": ("sbuf", [128, 2 * NC, 144], "float32"),
+    "su": ("sbuf", [128, 2 * NC, 8], "uint16"), "yb": ("sbuf", [128, 3, 16, 16], "float32"),
     "pm0": ("psum", [128, 4, 128], "float32"), "pm1": ("psum", [128, 4, 128], "float32"), "pe": ("psum", [128, 512], "float32"),
     "pf1": ("psum", [128, 512], "float32"), "pc": ("psum", [128, 64, 8], "float32"), "pl": ("psum", [128, 512], "float32"),
-    "ps": ("psum", [128, 64, 8], "float32"), "po": ("psum", [128, 16, 32], "float32"),
+    "ps": ("psum", [128, 256, 2], "float32"), "po": ("psum", [128, 16, 32], "float32"),
 }
 for _c in range(NC):
     SCRATCH["ts%d" % _c] = ("sbuf", [128, 1936], "int32")
     for _t in range(2):
         SCRATCH["gv%d_%d" % (_t, _c)] = ("sbuf", [128, 768 * HS[_c]], "bfloat16")
         SCRATCH["pr%d_%d" % (_t, _c)] = ("sbuf", [128, 768 * HS[_c]], "bfloat16")
-SEMAPHORES = ["eV", "eS", "eP", "eG", "sent"] + ["d%d" % i for i in range(24)] + ["r%d" % i for i in range(3 * NC)]
+SEMAPHORES = ["eV", "eS", "eP", "eG", "sent"] + ["d%d" % i for i in range(24)] + ["r%d" % i for i in range(2 * NC)]
 
 
 BANKS = [k for k in SCRATCH if SCRATCH[k][0] == "psum"]
@@ -107,6 +103,7 @@ def build(T, nxt, topo, core, fig=FIGS[0]):
     def cp(out, a, n, rd, wr, r=1.0): add("V", vns(n, r), rd, wr, lambda g: g.vector.tensor_copy(out, a))
     def ms(ap, v, n, wr): add("V", vns(n, 0.5), [], wr, lambda g: g.vector.memset(ap, v))
     def gtt(out, a, b, op, n, rd, wr): add("V", 50 + 0.83 * GC * n, rd, wr, lambda g: g.vector.tensor_tensor(out, a, b, op))
+    def gcp(out, a, n, rd, wr, r=GC): add("V", 50 + 0.83 * r * n, rd, wr, lambda g: g.vector.tensor_copy(out, a))
     def act(out, a, f, n, rd, wr, bias=0.0, scale=1.0, r=1.0):
         add("S", 50 + 0.83 * max(64, n * r), rd, wr, lambda g: g.scalar.activation(out, a, f, bias=bias, scale=scale))
     def iota(out, pat, base, cm, n, wr, fl=True):
@@ -117,18 +114,16 @@ def build(T, nxt, topo, core, fig=FIGS[0]):
             for m in lst: r = g.tensor.matmul(*m)
             return r
         add("P", 40 + PC * cyc + 8 * len(lst), rd, wr, fn)
-    def dma(out, in_, nbytes, rd, wr): add("Y", nbytes / 200.0, rd, wr, lambda g: g.sync.dma_start(out, in_), "dma")
+    def dma(out, in_, nbytes, rd, wr): add("Y", nbytes / 250.0, rd, wr, lambda g: g.sync.dma_start(out, in_), "dma")
 
-    n0 = SB[0][0][0][0]
     dma(T.ob[:, 0:1024], T.obs[:, 0:1024], 128 * 2048, [], ["ob0"])
-    part = [[x[0] for x in SB[0][c]] if c < FINE else [HS[c]] for c in range(NC)]
+    part = [[2] * len(SB[0][c]) if c < FINE else [HS[c]] for c in range(NC)]
     def table(c, s):
         a = sum(part[c][:s]); b = a + part[c][s]
         dma(T["ts%d" % c][:, 226 * a:226 * b], T.tsee[:, 226 * (H0[c] + a):226 * (H0[c] + b)], 128 * 904 * (b - a), [], ["ts%d_%d" % (c, s)])
     table(0, 0)
-    if OBALL: dma(T.ob[:, 1024:1536], T.obs[:, 1024:1536], 128 * 1024, [], ["ob1"])
+    dma(T.ob[:, 1024:1536], T.obs[:, 1024:1536], 128 * 1024, [], ["ob1"])
     dma(T.cv[:, 0:4096], T.cvec[:, :], 128 * 8192, [], ["cv"])
-    if not OBALL: dma(T.ob[:, 1024:1536], T.obs[:, 1024:1536], 128 * 1024, [], ["ob1"])
     for c in range(NC):
         for s in range(len(part[c])):
             if c or s: table(c, s)
@@ -138,260 +133,217 @@ def build(T, nxt, topo, core, fig=FIGS[0]):
     cp(T.pf[:, 0:1], T.pi[:, 0:1], 1, ["pi0"], ["pf0"])
     ts(T.pi[:, 4:5], T.pi[:, 0:1], 4, None, A.arith_shift_right, None, 1, ["pi0"], ["pi4"])
     ts(T.pf[:, 5:6], T.pi[:, 4:5], 16.0, 15.0, A.mult, A.add, 1, ["pi4"], ["pf5"])
-    ts(T.zz[:, :], T.ia[:, :], T.pf[:, 5:6], None, A.is_equal, None, 144, ["ia", "pf5"], ["zz"])
+    ts(T.zs[:, :], T.ia[:, :], T.pf[:, 5:6], 1.0 / 16, A.is_equal, A.mult, 144, ["ia", "pf5"], ["zs"])
+    ts(T.zz[:, :], T.zs[:, :], 16.0, None, A.mult, None, 144, ["zs"], ["zz"], 0.5)
+    ts(T.zc[:, :], T.zs[:, :], 16.0 * CW, None, A.mult, None, 144, ["zs"], ["zc"], 0.5)
     ts(T.pi[:, 1:2], T.pi[:, 0:1], 15, None, A.bitwise_and, None, 1, ["pi0"], ["pi1"])
     ts(T.pi[:, 2:3], T.pi[:, 0:1], 7, None, A.bitwise_and, None, 1, ["pi0"], ["pi2"])
     ts(T.pi[:, 3:4], T.pi[:, 0:1], 3, 1, A.arith_shift_right, A.bitwise_and, 1, ["pi0"], ["pi3"])
     cp(T.pf[:, 1:5], T.pi[:, 1:5], 4, ["pi1", "pi2", "pi3", "pi4"], ["pf"])
     ts(T.pf[:, 6:7], T.pi[:, 4:5], 3.0, 2.0, A.mult, A.add, 1, ["pi4"], ["pf6"])
+    ms(T.one[0:1, :], 1.0 / 32, 128, ["one"])
     for c in range(NC):
-        iota(T.cb[:, :, H0[c]:H0[c] + HS[c]], [[0, 12], [226, HS[c]]], 0, 0, 12 * HS[c], ["cb%d" % c], False)
+        iota(T.cb0[0:1, H0[c] // 2:(H0[c] + HS[c]) // 2], [[64 * 226, HS[c] // 2], [0, 3], [32 * 226, 2]], -15, 0, 3 * HS[c], ["cb0%d" % c])
+    for c in range(NC):
+        iota(T.cb[:, :, H0[c]:H0[c] + HS[c]], [[0, 15], [-226, HS[c]]], int(BIG + OFF), 0, 15 * HS[c], ["cb%d" % c])
     cbs = ["cb%d" % c for c in range(NC)]
     iota(T.ib[:, :], [[1, 8], [0, 16]], 0, 0, 128, ["ib"])
-    iota(T.ik[:, :], [[0, 8], [1, 16]], 0, 0, 128, ["ik"])
-    iota(T.ic[:, :], [[16, 8], [0, 16]], DUM - 2048 + 30000, 0, 128, ["ic"])
+    iota(T.ij[:, :], [[0, 8], [1, 16]], 0, 0, 128, ["ij"])
+    iota(T.ik[:, :, :], [[0, 8], [1, 18]], 0, 0, 144, ["ik"])
+    iota(T.ic[:, :, :], [[16, 8], [0, 18]], DUM - 2048 + 30000, 0, 144, ["ic"])
     iota(T.id3[:, :], [[1, 8], [0, 3]], 0, 0, 24, ["id3"])
-    for c in range(NC):
-        iota(T.dm[:, H0[c]:H0[c] + HS[c]], [[16, HS[c]]], DUM, 0, HS[c], ["dm%d" % c])
-    iota(T.dm[:, 16:24], [[16, 8]], DUM, 0, 8, ["dmx"])
     ts(T.blk[:, :], T.ib[:, :], T.pf[:, 4:5], None, A.is_equal, None, 128, ["ib", "pf"], ["blk"])
-    ts(T.hblk[:, :], T.ib[:, :], T.pf[:, 4:5], 0.5, A.is_equal, A.mult, 128, ["ib", "pf"], ["hblk"])
+    ts(T.hblk[:, :], T.blk[:, :], 0.5, None, A.mult, None, 128, ["blk"], ["hblk"], 0.5)
     ts(T.eye[:, :], T.ia[:, 0:128], T.pf[:, 0:1], None, A.is_equal, None, 128, ["ia", "pf0"], ["eye"])
-    ts(T.neye[:, :], T.ia[:, 0:128], T.pf[:, 0:1], -4096.0, A.is_equal, A.mult, 128, ["ia", "pf0"], ["neye"])
-    ts(T.t2[:, :], T.ik[:, :], T.pf[:, 1:2], -1.0, A.is_gt, A.mult, 128, ["ik", "pf"], ["t2"])
-    tt(T.t2[:, :], T.t2[:, :], T.blk[:, :], A.mult, 128, ["t2", "blk"], ["t2"], TT)
-    tt(T.imt[:, :], T.t2[:, :], T.eye[:, :], A.add, 128, ["t2", "eye"], ["imt"], TT)
+    ts(T.neye[:, :], T.eye[:, :], -1048576.0, None, A.mult, None, 128, ["eye"], ["neye"], 0.5)
+    ts(T.ceye[:, :], T.eye[:, :], -CW, None, A.mult, None, 128, ["eye"], ["ceye"], 0.5)
+    ts(T.t2[:, :], T.ij[:, :], T.pf[:, 1:2], -1.0, A.is_gt, A.mult, 128, ["ij", "pf"], ["t2"])
+    tt(T.t2[:, :], T.t2[:, :], T.blk[:, :], A.mult, 128, ["t2", "blk"], ["t2"], 1.0)
+    tt(T.imt[:, :], T.t2[:, :], T.eye[:, :], A.add, 128, ["t2", "eye"], ["imt"], 1.0)
     ts(T.zo[:, :], T.ia[:, 0:32], T.pf[:, 6:7], None, A.is_equal, None, 32, ["ia", "pf6"], ["zo"])
-    ts(T.of[:, :], T.id3[:, :], T.pf[:, 4:5], 1.0 / 4096, A.is_equal, A.mult, 24, ["id3", "pf"], ["of"])
-    ts(T.sk[:, :], T.ia[:, 0:16], T.pf[:, 1:2], -1.0, A.is_equal, A.mult, 16, ["ia", "pf"], ["sk"])
+    ts(T.of[:, 0, :], T.id3[:, :], T.pf[:, 4:5], 0.5, A.is_equal, A.mult, 24, ["id3", "pf"], ["of0"])
+    ts(T.of[:, 1, :], T.id3[:, :], T.pf[:, 4:5], 1.0 / 4096, A.is_equal, A.mult, 24, ["id3", "pf"], ["of1"])
+    ts(T.sk[:, :], T.ia[:, 0:16], T.pf[:, 1:2], -CW, A.is_equal, A.mult, 16, ["ia", "pf"], ["sk"])
     for k in range(16):
         act(T.nr[:, k, :], T.blk[:, :], AF.Identity, 128, ["blk", "sk"], ["nr%d" % k], scale=T.sk[:, k:k + 1])
     nrs = ["nr%d" % k for k in range(16)]
     add("G", 170 + 1.66 * 2048, nrs, ["ee"],
-        lambda g: g.affine_select(T.ee[:, :, :], T.nr[:, :, :], [[0, 16], [-1, 128]], A.not_equal, 1.0, 0, 1))
-    ts(T.tm[:, :], T.ik[:, :], T.pf[:, 1:2], None, A.is_lt, None, 128, ["ik", "pf"], ["tm"])
-    ts(T.ic[:, :], T.ic[:, :], T.pf[:, 1:2], None, A.add, None, 128, ["ic", "pf"], ["ic"])
-    tt(T.tm[:, :], T.tm[:, :], T.ic[:, :], A.mult, 128, ["tm", "ic"], ["tm"])
-    ts(T.c1[:, :], T.tm[:, :], -30000.0, None, A.add, None, 128, ["tm"], ["c1"])
-    ts(T.rs[:, :], T.ik[:, :], 0.0, None, A.is_gt, None, 128, ["ik"], ["rs"])
+        lambda g: g.affine_select(T.ee[:, :, :], T.nr[:, :, :], [[0, 16], [-1, 128]], A.not_equal, CW, 0, 1))
+    ts(T.tm[:, :, :], T.ik[:, :, :], T.pf[:, 1:2], None, A.is_lt, None, 144, ["ik", "pf"], ["tm"])
+    ts(T.ic[:, :, :], T.ic[:, :, :], T.pf[:, 1:2], None, A.add, None, 144, ["ic", "pf"], ["ic"])
+    tt(T.tm[:, :, :], T.tm[:, :, :], T.ic[:, :, :], A.mult, 144, ["tm", "ic"], ["tm"])
+    ts(T.c1[:, :, :], T.tm[:, :, :], -30000.0, None, A.add, None, 144, ["tm"], ["c1"])
+    ts(T.c1[:, :, 16], T.ik[:, :, 0], OFF, None, A.add, None, 8, ["ik", "c1"], ["c1"])
+    ts(T.c1[:, :, 17], T.ic[:, :, 0], 2048.0 - 30000.0, None, A.add, None, 8, ["ic", "c1"], ["c1"])
+    ts(T.rs[:, :], T.ik[:, :, :], 0.0, None, A.is_gt, None, 144, ["ik"], ["rs"])
+    ms(T.ae[:, :, :, 16:18], 0.0, 64, ["aez"])
     ms(T.cv[:, 4096:4112], 0.0, 16, ["cvz"])
-    ms(T.zero[:, :, :], 0.0, 384, ["zero"])
-    ms(T.tie[:, 0, :], 2.0, 8, ["tie0"]); ms(T.tie[:, 1, :], 1.0, 8, ["tie1"]); ms(T.tie[:, 2:4, :], 0.0, 16, ["tie2"])
-    ms(T.uo[:, :, :], 0, 96 * NC, ["uoz"])
-    ts(T.fo[:, :, :, :], T.ls[:, 0:2 * NC, 0:48], 0.0, None, A.mult, None, 96 * NC, ["lsz"], ["foz"])
-    ops.insert(len(ops) - 1, dict(e="V", ns=vns(96 * NC), rd=[], wr=["lsz"], kind=None,
-                                  fn=lambda g: g.vector.memset(T.ls[:, 0:2 * NC, 0:48], 0.0)))
-    ms(T.ww[:, 448:464], 0.0, 32, ["wwz"])
-    ts(T.ww[:, 432:448], T.dm[:, 0:16], T.pf[:, 1:2], None, A.add, None, 16, ["pf"] + ["dm%d" % c for c in range(NC)], ["wwd"])
-    for c in range(NC):
-        ts(T.si[:, c, 104:112], T.dm[:, 16:24], T.pf[:, 1:2], None, A.add, None, 8, ["pf", "dmx"], ["sid%d" % c])
-    ev = [16 * CAND1[2 * i] for i in range(28)] + [8 * CAND2[2 * i] for i in range(16)]
-    df = [16 * (CAND1[2 * i + 1] - CAND1[2 * i]) for i in range(28)] + [8 * (CAND2[2 * i + 1] - CAND2[2 * i]) for i in range(16)]
+    ms(T.k18[:, :, :], OFF, 384, ["k18"])
+    ms(T.tie[:, 0, :], 0.5, 8, ["tie0"]); ms(T.tie[:, 1, :], 0.25, 8, ["tie1"]); ms(T.tie[:, 2:4, :], 0.0, 16, ["tie2"])
+    ms(T.ww[:, 432:448], 0.0, 32, ["wwz"])
+    rows = [16 * x for x in CAND1] + [8 * x for x in CAND2] + [8 * (i // 13) for i in range(52)] + [8 * (i // 6) for i in range(24)] + [0] * 4
     tabs = []
-    for i, n, b, st in runs(ev + df):
+    for i, n, b, st in runs(rows[0::2] + [y - x for x, y in zip(rows[0::2], rows[1::2])]):
         tabs.append("tab%d" % i); iota(T.tab[:, i:i + n], [[st, n]], b, 0, n, [tabs[-1]])
-    iota(T.tab[:, 88:116], [[8, 4], [0, 7]], 0, 0, 28, ["tr1"]); iota(T.tab[:, 116:132], [[8, 4], [0, 4]], 0, 0, 16, ["tr2"])
-    iota(T.tab[:, 132:136], [[0, 4]], 0, 0, 4, ["tr3"])
-    ts(T.tb2[:, 0:44], T.tab[:, 44:88], T.pf[:, 3:4], T.pf[:, 2:3], A.mult, A.add, 44, tabs + ["pf"], ["tb2"])
-    tt(T.tb3[:, 0:44], T.tb2[:, 0:44], T.tab[:, 0:44], A.add, 44, tabs + ["tb2"], ["tb3"])
+    ts(T.tb2[:, 0:78], T.tab[:, 78:156], T.pf[:, 3:4], T.pf[:, 2:3], A.mult, A.add, 78, tabs + ["pf"], ["tb2"])
+    tt(T.tb3[:, 0:78], T.tb2[:, 0:78], T.tab[:, 0:78], A.add, 78, tabs + ["tb2"], ["tb3"])
     for c in range(NC):
-        ts(T.o1[:, c, :], T.tb3[:, 0:28], float(H0[c]), None, A.add, None, 28, ["tb3"], ["o1%d" % c])
-    cp(T.o2[:, :], T.tb3[:, 28:44], 16, ["tb3"], ["o2"])
-    ts(T.orp[:, :], T.tab[:, 88:136], T.pf[:, 2:3], None, A.add, None, 48, ["tr1", "tr2", "tr3", "pf"], ["orp"])
+        ts(T.o1[:, c, :], T.tb3[:, 0:26], float(H0[c]), None, A.add, None, 26, ["tb3"], ["o1%d" % c])
+    cp(T.ol[:, :], T.tb3[:, 26:78], 52, ["tb3"], ["ol"])
 
     def star(j, n=1): return T.ob[:, 256 * j:256 * (j + n)]
-    for i in range(6):
-        tt(T.gp[:, i, :], star(PAIRS[i][0]), star(PAIRS[i][1]), A.mult, 256, ["ob0"], ["gp%d" % i], TT)
-    for i in (6, 8, 10, 12):
-        tt(T.gp[:, i:i + 2, :], star(PAIRS[i][0], 2), star(4, 2) if i < 12 else star(4, 2), A.mult, 512, ["ob0", "ob1"], ["gp%d" % i], TT)
-    tt(T.gp[:, 14, :], star(0), star(5), A.mult, 256, ["ob0", "ob1"], ["gp14"], TT)
-    def L(k): return T.zz[:, 15 - k:143 - k]
-    def gram(bank, a, b, rd, tok):
-        mm([(bank[:, 0:16 * (b - a)], L(k), T.gp[:, a:b, 16 * k:16 * k + 16], k == 0, k == 15) for k in range(16)],
-           16 * max(64, 16 * (b - a)), rd + ["zz"], [tok])
-    gram(T.pf1, 0, 3, ["gp0", "gp1", "gp2"], "pf1")
-    gram(T.pe, 3, 6, ["gp3", "gp4", "gp5"], "pe")
-    gram(T.pl, 6, 15, ["gp6", "gp8", "gp10", "gp12", "gp14"], "pl")
-    cp(T.gi[:, 0:48], T.pf1[:, 0:48], 48, [], ["pf1", "gi0"])
-    ts(T.gs[:, 0:48], T.gi[:, 0:48], 4, None, A.arith_shift_right, None, 48, ["gi0"], ["gs0"])
-    tt(T.s0[:, 0:3, :], T.gs[:, 0:48], T.cb[:, 0:3, :], A.add, 48, ["gs0"] + cbs, ["s0a"])
-    ts(T.s0[:, 3:6, :], T.pe[:, 0:48], -OFF, None, A.add, None, 48, [], ["pe", "s0b"])
-    cp(T.gi[:, 48:96], T.pe[:, 0:48], 48, [], ["pe", "gi1"])
-    cp(T.gi[:, 96:240], T.pl[:, 0:144], 144, [], ["pl", "gi2"])
-    act(T.ww[:, 288:432], T.pl[:, 0:144], AF.Identity, 144, [], ["pl", "ww3"], bias=-OFF)
-    act(T.ww[:, 0:96], T.s0[:, :, :], AF.Identity, 96, ["s0a", "s0b"], ["ww1"])
-    ts(T.gs[:, 48:240], T.gi[:, 48:240], 4, None, A.arith_shift_right, None, 192, ["gi1", "gi2"], ["gs1"])
-    tt(T.ww[:, 96:288], T.gs[:, 48:240], T.cb[:, :, :], A.add, 192, ["gs1"] + cbs, ["ww2"])
+    for w in range(3):
+        tt(T.gp0[:, :, :, w, :], star(0), star(PAIRS[12 + w][1]), A.mult, 256, ["ob0"], ["gq%d" % w], 1.0)
+    for i in range(3):
+        tt(T.gp[:, i, :], star(PAIRS[i][0]), star(PAIRS[i][1]), A.mult, 256, ["ob0"], ["gp%d" % i], 1.0)
+    for i in (3, 5, 7, 9):
+        tt(T.gp[:, i:i + 2, :], star(PAIRS[i][0], 2), star(4, 2), A.mult, 512, ["ob0", "ob1"], ["gp%d" % i], 1.0)
+    tt(T.gp[:, 11, :], star(0), star(5), A.mult, 256, ["ob0", "ob1"], ["gp11"], 1.0)
+    def L(z, k): return z[:, 15 - k:143 - k]
+    gq = ["gq0", "gq1", "gq2", "zs"]
+    mm([(T.pf1[:, 0:48], T.one[0:1, :], T.cb0[0:1], True, False)], 256, ["one"] + ["cb0%d" % c for c in range(NC)], ["pf1"])
+    mm([(T.pf1[:, 0:48], L(T.zs, k), T.gp0[:, k], False, k == 15) for k in range(16)], 1024, gq, ["pf1"])
+    ts(T.ui0[:, :], T.pf1[:, 0:48], BIG, BIG, A.add, A.subtract, 48, [], ["pf1", "uz"])
+    mm([(T.pe[:, 192 + 16 * w:208 + 16 * w], L(T.zs, k), T.gp0[:, k, :, w, :], k == 0, k == 15) for w in range(3) for k in range(16)], 3072, gq, ["pe"])
+    mm([(T.pe[:, 0:192], L(T.zs, k), T.gp[:, :, 16 * k:16 * k + 16], k == 0, k == 15) for k in range(16)], 3072,
+       ["zs"] + ["gp%d" % i for i in (0, 1, 2, 3, 5, 7, 9, 11)], ["pe"])
+    act(T.ww[:, 240:432], T.pe[:, 0:192], AF.Identity, 192, [], ["pe", "wwv"], bias=-OFF, scale=16.0)
+    ts(T.gs[:, :], T.pe[:, 0:240], -15.0 / 32, BIG, A.add, A.add, 240, [], ["pe", "gs"])
+    tt(T.ww[:, 0:240], T.gs[:, :], T.cb[:, :, :], A.subtract, 240, ["gs"] + cbs, ["wwc"])
+    cp(T.fi0[:, :, :], T.ww[:, 224:288], 64, ["wwc", "wwv"], ["fz"])
+    ts(T.ua0[:, :], T.ww[:, 224:240], OFF, None, A.add, None, 16, ["wwc"], ["ua0"])
 
     rid, pid, _ = topo.addr(nxt)
-    eng = topo.engines(core, nxt)[:8]
-    def mask(es): return sum(1 << e for e in es)
+    mask = sum(1 << e for e in topo.engines(core, nxt)[:8])
 
-    def convert(src, h0, t, c, ut, ft, rd, wr, utok, ftok):
-        H, o, one = HS[c], 0, len(SB[t][c]) == 1
-        for s, (n, kd) in enumerate(SB[t][c]):
-            cp(ut[:, 3 * o:3 * (o + n)], src[:, 0:3, h0 + o:h0 + o + n], 3 * n, rd, wr + ([utok + "y"] if one else []) + [utok + "s%d" % s]); o += n
-        cp(ft[:, 0:4, 0:H], src[:, 2:6, h0:h0 + H], 4 * H, rd, wr + [ftok])
-        if not one: cp(ut[:, 24:24 + 3 * H], src[:, 0:3, h0:h0 + H], 3 * H, rd, wr + [utok + "y"])
-
-    eb, ec, ek, kb, kk = (T.pl, 256, "pl", T.ps, "ps") if "P" in "".join(SPLIT) else (T.pe, 0, "pe", T.pc, "pc")
     for t in range(3):
         for c in range(NC):
-            I = t * NC + c; H = HS[c]; n = 16 * H; tsb = T["ts%d" % c]; tk = "ts%d" % c
+            I = t * NC + c; H = HS[c]; n = 16 * H; tsb = T["ts%d" % c]; nsb = H // 2; h0 = H0[c]
             tks = ["ts%d_%d" % (c, s) for s in range(len(part[c]))]; fine = t == 0 and len(tks) > 1
-            U = "ui%d" % I; F = "fi%d" % I; pm = T["pm%d" % (I % 2)]; pmk = "pm%d" % (I % 2)
-            nsb = len(SB[t][c]); us = [U + "s%d" % s for s in range(nsb)]; y0 = 0 if nsb == 1 else 24
-            if t == 0: convert(T.s0, H0[c], 0, c, T.ui[:, I], T.fi[:, I], ["s0a", "s0b"], [], U, F)
+            pm = T["pm%d" % (I % 2)]; pmk = "pm%d" % (I % 2)
+            if t == 0:
+                U, UA, F = "uz", "ua0", "fz"
+                ul, u0, ua, fa, fd = T.ui0, 3 * h0, T.ua0[:, h0:h0 + H], T.fi0[:, 0, h0:h0 + H], T.fi0[:, 1:4, h0:h0 + H]
+            else:
+                M = I - NC; U = UA = "ui%d" % M; F = "fi%d" % M
+                ul, u0, ua, fa, fd = T.ui[:, M], 8 * NQ[t - 1], T.ui[:, M, 16:16 + H], T.fi[:, M, 0, 0:H], T.fi[:, M, 1:4, 0:H]
+                ts(T.fi[:, M], T.ui[:, M, 16:48], -OFF, None, A.add, None, 32, [U], [F])
+                if t == 1: ts(T.si[:, c, :], T.ui[:, M, 0:104], -OFF, None, A.add, None, 104, [U], ["si%d" % c])
             win = tsb[:, 0:226 * H]
             if fine:
-                o = 0
-                for s, x in enumerate(part[c]):
-                    a, b = T.nm[:, I, 48 * o:48 * (o + x)], tsb[:, 0:226 * (o + x)].indirect(T.ui[:, I, 3 * o:3 * (o + x)])
-                    add("V", 50 + 0.83 * GC * 48 * x, [us[s]] + tks[:s + 1], ["nm%d_%d" % (I, s)], lambda g, a=a, b=b: g.vector.tensor_copy(a, b))
-                    o += x
+                for s in range(nsb):
+                    gcp(T.nm[:, I, 96 * s:96 * s + 96], tsb[:, 0:452 * (s + 1)].indirect(ul[:, u0 + 6 * s:u0 + 6 * s + 6]), 96,
+                        [U] + tks[:s + 1], ["nm%d_%d" % (I, s)])
+                nms = ["nm%d_%d" % (I, s) for s in range(nsb)]
             else:
-                a, b = T.nm[:, I, 0:3 * n], win.indirect(T.ui[:, I, 0:3 * H])
-                add("V", 50 + 0.83 * GC * 3 * n, us + tks, ["nm%d" % I], lambda g, a=a, b=b: g.vector.tensor_copy(a, b))
-            mm([(pm[:, 0:3, 0:n], T.eye[:, :], T.zero[:, :, 0:n], True, False)], 3 * n, ["eye", "zero"], [pmk])
-            dlist = [(pm[:, 0:3, k:n:16], T.nr[:, k, :], T.fi[:, I, 1:4, 0:H], False, False) for k in range(16)]
-            cw = T.cv[:, 0:4097]; o = 0
-            old = ["mm%d" % c] if t == 2 else []
-            for s, (ns, kd) in enumerate(SB[t][c]):
-                w = 256 * ns; l = 16 * ns
-                gvb = T["gv%d_%d" % (t % 2, c)]; prb = T["pr%d_%d" % (t % 2, c)]; e0 = 768 * o
+                gcp(T.nm[:, I, 0:3 * n], win.indirect(ul[:, u0:u0 + 3 * H]), 3 * n, [U] + tks, ["nm%d" % I]); nms = ["nm%d" % I]
+            ts(T.nf[:, I, 0:nsb], T.nm[:, I, 0:3 * n], -2048.0, 1.0 / 4096, A.add, A.mult, 3 * n, nms, ["nf%d" % I], 0.5)
+            mm([(pm[:, 0:3, 0:n], T.ceye[:, :], T.k18[:, :, 0:n], True, False)], 3 * n, ["ceye", "k18"], [pmk])
+            dlist = [(pm[:, 0:3, k:n:16], T.nr[:, k, :], fd, False, False) for k in range(16)]
+            cw = T.cv[:, 0:4097]; w = 512
+            gvb = T["gv%d_%d" % (t % 2, c)]; prb = T["pr%d_%d" % (t % 2, c)]
+            old = ["mm%d" % c] if t == 2 else []; lt = ["mm%d" % c] if t == 0 else []
+            for s, kd in enumerate(SB[t][c]):
+                e0 = 3 * w * s
                 def gv(a, b): return gvb[:, e0 + a:e0 + b]
                 def pr(a, b): return prb[:, e0 + a:e0 + b]
-                nt = "nm%d_%d" % (I, s) if fine else "nm%d" % I
                 G = "gv%d_%d" % (I, s); P = "pr%d_%d" % (I, s)
-                def lst(a, b): return cw.indirect(T.nm[:, I, 48 * o + a // 16:48 * o + b // 16])
-                rd = [nt, "cv", "cvz"] + old
-                last = s == nsb - 1; lt = ["mm%d" % c] if last and t == 0 else []
+                def lst(a, b): return cw.indirect(T.nm[:, I, 96 * s + a // 16:96 * s + b // 16])
+                rd = [nms[s] if fine else nms[0], "cv", "cvz"] + old
+                last = s == nsb - 1
                 def red(a, b, toks, fin):
-                    mm([(pm[:, a:b, 16 * o:16 * o + l], L(p), prb[:, e0 + a * w + p:e0 + b * w:16], False, fin and p == 15) for p in range(16)],
-                       16 * max(64, (b - a) * l), ["zz"] + toks, [pmk] + (lt if fin else []))
-                if kd[0] == "N":
-                    u = 256 * int(kd[1:])
-                    act(gv(0, w), lst(0, w), AF.Copy, w, rd, [G + "b"], r=GC)
-                    act(gv(w, 2 * w), lst(w, 2 * w), AF.Copy, w, rd, [G + "c"], r=GC)
-                    tt(pr(0, w), gv(0, w), gv(w, 2 * w), A.mult, w, [G + "b", G + "c"], [P + "a"], TT)
-                    if u:
-                        act(gv(2 * w, 2 * w + u), lst(2 * w, 2 * w + u), AF.Copy, u, rd, [G], r=GC)
-                        tt(pr(w, w + u), gv(w, w + u), gv(2 * w, 2 * w + u), A.mult, u, [G, G + "c"], [P + "b"], TT)
-                        tt(pr(2 * w, 2 * w + u), gv(0, u), gv(2 * w, 2 * w + u), A.mult, u, [G, G + "b"], [P + "c"], TT)
-                    if u < w:
-                        gtt(pr(2 * w + u, 3 * w), lst(2 * w + u, 3 * w), gv(u, w), A.mult, w - u, rd + [G + "b"], [P + "e"])
-                        gtt(pr(w + u, 2 * w), lst(2 * w + u, 3 * w), gv(w + u, 2 * w), A.mult, w - u, rd + [G + "c"], [P + "d"])
-                    if s == 0: mm(dlist, 1024, nrs + [F], [pmk])
-                    red(0, 1, [P + "a"], False); red(1, 2, [P + "b", P + "d"], False); red(2, 3, [P + "c", P + "e"], last)
-                    o += ns
-                    continue
+                    mm([(pm[:, a:b, 32 * s:32 * s + 32], L(T.zc, p), prb[:, e0 + a * w + p:e0 + b * w:16], False, fin and p == 15) for p in range(16)],
+                       16 * max(64, (b - a) * 32), ["zc"] + toks, [pmk] + (lt if fin else []))
                 if kd == "W":
                     act(gv(0, 3 * w), lst(0, 3 * w), AF.Copy, 3 * w, rd, [G], r=GC)
-                    tt(pr(0, 2 * w), gv(0, 2 * w), gv(w, 3 * w), A.mult, 2 * w, [G], [P + "a"], TT)
-                    tt(pr(2 * w, 3 * w), gv(0, w), gv(2 * w, 3 * w), A.mult, w, [G], [P + "b"], TT)
+                    tt(pr(0, 2 * w), gv(0, 2 * w), gv(w, 3 * w), A.mult, 2 * w, [G], [P + "a"], 1.0)
+                    tt(pr(2 * w, 3 * w), gv(0, w), gv(2 * w, 3 * w), A.mult, w, [G], [P + "b"], 1.0)
                 elif kd == "X":
                     act(gv(0, 2 * w), lst(0, 2 * w), AF.Copy, 2 * w, rd, [G], r=GC)
-                    tt(pr(0, w), gv(0, w), gv(w, 2 * w), A.mult, w, [G], [P + "a"], TT)
+                    tt(pr(0, w), gv(0, w), gv(w, 2 * w), A.mult, w, [G], [P + "a"], 1.0)
                     gtt(pr(w, 2 * w), lst(2 * w, 3 * w), gv(w, 2 * w), A.mult, w, rd + [G], [P + "b"])
                     gtt(pr(2 * w, 3 * w), lst(2 * w, 3 * w), gv(0, w), A.mult, w, rd + [G], [P + "c"])
-                elif kd == "P":
-                    act(gv(0, 3 * w), lst(0, 3 * w), AF.Copy, 3 * w, rd, [G], r=GC)
-                    mm([(T.pc[:, :, :], T.eye[:, :], gv(w, 2 * w), True, True)], w, ["eye", G], ["pc"])
-                    mm([(T.pe[:, :], T.eye[:, :], gv(0, w), True, True)], w, ["eye", G], ["pe"])
-                    tt(pr(w, 2 * w), T.pc[:, :, :], gv(2 * w, 3 * w), A.mult, w, [G], ["pc", P + "b"], 1.0)
-                    tt(pr(0, w), T.pe[:, :], gv(w, 2 * w), A.mult, w, [G], ["pe", P + "a"], 1.0)
-                    tt(pr(2 * w, 3 * w), T.pe[:, :], gv(2 * w, 3 * w), A.mult, w, [G], ["pe", P + "c"], 1.0)
                 elif kd == "U":
                     act(gv(0, 2 * w), lst(0, 2 * w), AF.Copy, 2 * w, rd, [G], r=GC)
-                    add("V", 50 + 0.83 * GC * w, rd, [G + "a"], lambda g, a=gv(2 * w, 3 * w), b=lst(2 * w, 3 * w): g.vector.tensor_copy(a, b))
-                    tt(pr(0, 2 * w), gv(0, 2 * w), gv(w, 3 * w), A.mult, 2 * w, [G, G + "a"], [P + "a"], TT)
-                    tt(pr(2 * w, 3 * w), gv(0, w), gv(2 * w, 3 * w), A.mult, w, [G, G + "a"], [P + "b"], TT)
+                    gcp(gv(2 * w, 3 * w), lst(2 * w, 3 * w), w, rd, [G + "a"])
+                    tt(pr(0, 2 * w), gv(0, 2 * w), gv(w, 3 * w), A.mult, 2 * w, [G, G + "a"], [P + "a"], 1.0)
+                    tt(pr(2 * w, 3 * w), gv(0, w), gv(2 * w, 3 * w), A.mult, w, [G, G + "a"], [P + "b"], 1.0)
                 else:
                     act(gv(0, 2 * w), lst(0, 2 * w), AF.Copy, 2 * w, rd, [G], r=GC)
-                    gtt(pr(0, w), lst(w, 2 * w), gv(0, w), A.mult, w, rd + [G], [P + "a"])
-                    gtt(pr(2 * w, 3 * w), lst(2 * w, 3 * w), gv(0, w), A.mult, w, rd + [G], [P + "c"])
-                    gtt(pr(w, 2 * w), lst(2 * w, 3 * w), gv(w, 2 * w), A.mult, w, rd + [G], [P + "b"])
-                if s == 0: mm(dlist, 1024, nrs + [F], [pmk])
-                if last and I == 3 * NC - 1 and kd in "WU":
-                    red(0, 2, [P + "a"], False); red(2, 3, [P + "b"], True)
-                else: red(0, 3, [P + "a", P + "b", P + "c"], last)
-                o += ns
+                    act(gv(2 * w, 3 * w), lst(2 * w, 3 * w), AF.Copy, w, rd, [G + "a"], r=GC)
+                    tt(pr(0, w), gv(0, w), gv(w, 2 * w), A.mult, w, [G], [P + "a"], 1.0)
+                    tt(pr(w, 2 * w), gv(w, 2 * w), gv(2 * w, 3 * w), A.mult, w, [G, G + "a"], [P + "b"], 1.0)
+                    tt(pr(2 * w, 3 * w), gv(0, w), gv(2 * w, 3 * w), A.mult, w, [G, G + "a"], [P + "c"], 1.0)
+                if s == max(0, nsb - 2): mm(dlist, 1024, nrs + [F], [pmk])
+                if last and kd in "WU": red(0, 2, [P + "a"], False); red(2, 3, [P + "b"], True)
+                elif last: red(0, 2, [P + "a", P + "b"], False); red(2, 3, [P + "c"], True)
+                else: red(0, 3, [P + "a", P + "b", P + "c"], False)
+            J = I
             if t < 2:
-                J = I
-                mm([(eb[:, ec + k:ec + n:16], T.ee[:, k, :], T.fi[:, I, 0, 0:H], True, True) for k in range(16)], 1024, ["ee", F], [ek])
-                act(T.ae[:, J, 0:n], eb[:, ec:ec + n], AF.Abs, n, [], [ek, "ae%d" % J])
-                nq = 14 if t == 0 else 8
+                mm([(T.pe[:, k:n:16], T.ee[:, k, :], fa, True, True) for k in range(16)], 1024, ["ee", F], ["pe"])
+                act(T.ae[:, J, 0:H, 0:16], T.pe[:, 0:n], AF.Abs, n, ["aez"], ["pe", "ae%d" % J])
+                nq = NQ[t]
                 if t == 0:
                     cand = T.cand1[:, c, :]
-                    act(cand, T.ww[:, :].indirect(T.o1[:, c, :]), AF.Copy, 448, ["ww1", "ww2", "ww3", "wwd", "wwz", "o1%d" % c], ["cand%d" % J], r=GC)
+                    act(cand, T.ww[:, :].indirect(T.o1[:, c, :]), AF.Copy, 416, ["wwc", "wwv", "wwz", "o1%d" % c], ["cand%d" % J], r=GC)
                 else:
                     cand = T.cand2[:, c, :]
-                    act(cand, T.si[:, c, :].indirect(T.o2[:, :]), AF.Copy, 256, ["si%d" % c, "sid%d" % c, "o2"], ["cand%d" % J], r=GC)
-            act(T.ab[:, I, :, 0:n], pm[:, 0:3, 0:n], AF.Abs, 3 * n, [], [pmk, "ab%d" % I], bias=-OFF)
-            ts(T.hd[:, I, 0:3, 0:n], T.ab[:, I, :, 0:n], 130.0, 16.0, A.is_le, A.mult, 3 * n, ["ab%d" % I], ["hd%d" % I], 0.5)
+                    act(cand, T.si[:, c, :].indirect(T.ol[:, 0:12]), AF.Copy, 192, ["si%d" % c, "ol"], ["cand%d" % J], r=GC)
+            ts(T.hd[:, I, 0:3, 0:n], pm[:, 0:3, 0:n], BIG, BIG, A.add, A.is_equal, 3 * n, [], [pmk, "hd%d" % I])
             if I < EVS:
                 mm([(T.pf1[:, 128:128 + n], T.eye[:, :], T.hd[:, I, e, 0:n], e == 0, e == 2) for e in range(3)], 3 * n, ["eye", "hd%d" % I], ["pf1"])
-                act(T.hd[:, I, 3, 0:n], T.pf1[:, 128:128 + n], AF.Relu, n, [], ["pf1", "ev%d" % I], bias=-8192.0, scale=256.0)
+                act(T.hd[:, I, 3, 0:n], T.pf1[:, 128:128 + n], AF.Relu, n, [], ["pf1", "ev%d" % I], bias=-8192.0, scale=4096.0)
             else:
-                tt(T.h2[:, I, 0:n], T.hd[:, I, 0, 0:n], T.hd[:, I, 1, 0:n], A.mult, n, ["hd%d" % I], ["h2%d" % I], TT)
-                tt(T.hd[:, I, 3, 0:n], T.h2[:, I, 0:n], T.hd[:, I, 2, 0:n], A.mult, n, ["hd%d" % I, "h2%d" % I], ["ev%d" % I], TT)
+                tt(T.h2[:, I, 0:n], T.hd[:, I, 0, 0:n], T.hd[:, I, 1, 0:n], A.mult, n, ["hd%d" % I], ["h2%d" % I], 1.0)
+                tt(T.hd[:, I, 3, 0:n], T.h2[:, I, 0:n], T.hd[:, I, 2, 0:n], A.mult, n, ["hd%d" % I, "h2%d" % I], ["ev%d" % I], 1.0)
             if t < 2:
-                mm([(kb[:, 32:36, :], T.eye[:, :], T.tie[:, :, :], True, False)] +
-                   [(kb[:, 32:36, 0:H], L(k), T.hd[:, I, :, k:n:16], False, k == 15) for k in range(16)], 1088,
-                   ["eye", "tie0", "tie1", "tie2", "zz", "hd%d" % I, "ev%d" % I], [kk])
+                mm([(T.pc[:, 32:36, :], T.eye[:, :], T.tie[:, :, :], True, False)] +
+                   [(T.pc[:, 32:36, 0:H], L(T.zz, k), T.hd[:, I, :, k:n:16], False, k == 15) for k in range(16)], 1088,
+                   ["eye", "tie0", "tie1", "tie2", "zz", "hd%d" % I, "ev%d" % I], ["pc"])
             mm([(T.pf1[:, 0:n], T.imt[:, :], T.hd[:, I, 3, 0:n], True, True)], n, ["imt", "ev%d" % I], ["pf1"])
-            act(T.ff[:, I, 0:n], T.pf1[:, 0:n], AF.Relu, n, [], ["pf1", "ff%d" % I])
+            act(T.ff[:, I, 0:n], T.pf1[:, 0:n], AF.Relu, n, [], ["pf1", "ff%d" % I], scale=1.0 if I < EVS else 4096.0)
             if t < 2:
-                if SCS: act(T.sc[:, J, :], kb[:, 32:36, :], AF.Identity, 32, [], [kk, "sc%d" % J])
-                else: cp(T.sc[:, J, :], kb[:, 32:36, :], 32, [], [kk, "sc%d" % J])
+                if SCS: act(T.sc[:, J, :], T.pc[:, 32:36, :], AF.Identity, 32, [], ["pc", "sc%d" % J])
+                else: cp(T.sc[:, J, :], T.pc[:, 32:36, :], 32, [], ["pc", "sc%d" % J])
                 tt(T.m1[:, J, :], T.sc[:, J, 0:16], T.sc[:, J, 16:32], A.max, 16, ["sc%d" % J], ["m1%d" % J])
                 tt(T.m2[:, J, :], T.m1[:, J, 0:8], T.m1[:, J, 8:16], A.max, 8, ["m1%d" % J], ["m2%d" % J])
-                gtt(T.mk[:, J, :], T.m2[:, J, :].indirect(T.orp[:, 44:46]), T.sc[:, J, :], A.is_equal, 32, ["m2%d" % J, "sc%d" % J, "orp"], ["mk%d" % J])
-                rep = T.orp[:, 0:28] if t == 0 else T.orp[:, 28:44]
-                gtt(T.msk[:, J, 0:32 * nq], T.mk[:, J, :].indirect(rep), cand, A.mult, 32 * nq, ["mk%d" % J, "cand%d" % J, "orp"], ["msk%d" % J])
-                mm([(T.ps[:, 0:nq, :], T.eye[:, :], T.msk[:, J, 8 * nq * q:8 * nq * (q + 1)], q == 0, q == 3) for q in range(4)],
-                   4 * max(64, 8 * nq), ["eye", "msk%d" % J], ["ps"])
-                convert(T.ps, 0, t + 1, c, T.uo[:, J], T.fo[:, J], ["uoz", "foz"], ["ps"], "uo%d" % J, "fo%d" % J)
-                N = I + NC; nsb = len(SB[t + 1][c])
-                def snd(g, J=J, N=N):
-                    d = [DstId(rid=rid, pnc=pid)]
-                    return g.remote_dma_fused([
-                        RemoteDMATransfer(dst_ids=d, dma_engine_mask=mask(eng[:4]), remote_sem=T.sem["r%d" % J], src=T.uo[:, J], dst=T.ui[:, N]),
-                        RemoteDMATransfer(dst_ids=d, dma_engine_mask=mask(eng[4:]), remote_sem=T.sem["r%d" % J], src=T.fo[:, J], dst=T.fi[:, N])],
-                        local_sem=T.sem.sent)
-                add("G", 300, ["uo%ds%d" % (J, s) for s in range(nsb)] + ["uo%dy" % J, "fo%d" % J],
-                    ["ui%ds%d" % (N, s) for s in range(nsb)] + ["ui%dy" % N, "fi%d" % N], snd, "r%d" % J)
-                if t == 0:
-                    act(T.so[:, c, :], T.ps[:, 0:13, :], AF.Identity, 104, [], ["ps", "so%d" % c])
-                    add("G", 300, ["so%d" % c], ["si%d" % c], lambda g, c=c: g.remote_dma(
-                        T.si[:, c, 0:104], T.so[:, c, :], T.sem["r%d" % (2 * NC + c)], T.sem.sent, pid, rid, mask(eng)), "r%d" % (2 * NC + c))
-                mm([(T.pl[:, 0:n], T.eye[:, :], T.c1[:, 0:n], True, False), (T.pl[:, 0:n], T.neye[:, :], T.ae[:, J, 0:n], False, False),
-                    (T.pl[:, 0:n], T.hblk[:, :], T.ff[:, I, 0:n], False, True)], 3 * n, ["eye", "neye", "hblk", "c1", "ae%d" % J, "ff%d" % I], ["pl"])
-                add("V", vns(n), ["rs", "foz"], ["pl", "ls%d" % J], lambda g, J=J, n=n: g.vector.tensor_tensor_scan(
-                    T.ls[:, J, 0:n], T.rs[:, 0:n], T.pl[:, 0:n], 0.0, A.mult, A.max))
-                tt(T.sf[:, J, 0:H], T.ls[:, J, 15:n:16], T.ps[:, 13 if t == 0 else 6, 0:H], A.max, H, ["ls%d" % J], ["ps", "sf%d" % J])
-                cp(T.su[:, J, 0:H], T.sf[:, J, 0:H], H, ["sf%d" % J], ["su%d" % J])
-                gtt(T.sv[:, J, 0:n], win.indirect(T.ui[:, I, y0 + 2 * H:y0 + 3 * H]), T.ff[:, I, 0:n], A.max, n, tks + [U + "y", "ff%d" % I], ["sv%d" % J])
-            Y = "yy%d" % (I % 2)
+                gtt(T.mk[:, J, :], T.m2[:, J, :].indirect(T.ol[:, 50:52]), T.sc[:, J, :], A.is_equal, 32, ["m2%d" % J, "sc%d" % J, "ol"], ["mk%d" % J])
+                rep = T.ol[:, 12:38] if t == 0 else T.ol[:, 38:50]
+                gtt(T.msk[:, J, 0:32 * nq], T.mk[:, J, :].indirect(rep), cand, A.mult, 32 * nq, ["mk%d" % J, "cand%d" % J, "ol"], ["msk%d" % J])
+                m = 8 * nq + 3 * H
+                mm([(T.ps[:, 0:m // 2, :], T.eye[:, :], T.k18[:, 0, 0:m], True, False)], m, ["eye", "k18"], ["ps"])
+                mm([(T.ps[:, 4 * nq + x:4 * nq + 3 * nsb:3, :], T.eye[:, :], T.msk[:, J, 8 * (nq * q + x):8 * (nq * q + x) + H], False, False)
+                    for q in range(4) for x in range(3)] +
+                   [(T.ps[:, 0:4 * nq, :], T.eye[:, :], T.msk[:, J, 8 * nq * q:8 * nq * (q + 1)], False, q == 3) for q in range(4)],
+                   768 + 4 * max(64, 8 * nq), ["eye", "msk%d" % J], ["ps"])
+                cp(T.uo[:, J, 0:m], T.ps[:, 0:m // 2, :], m, [], ["ps", "uo%d" % J])
+                add("G", 300, ["uo%d" % J], ["ui%d" % J], lambda g, J=J, m=m: g.remote_dma(
+                    T.ui[:, J, 0:m], T.uo[:, J, 0:m], T.sem["r%d" % J], T.sem.sent, pid, rid, mask), "r%d" % J)
+                mm([(T.pl[:, 0:18 * H], T.eye[:, :], T.c1[:, 0:H, :], True, False), (T.pl[:, 0:18 * H], T.neye[:, :], T.ae[:, J, 0:H, :], False, False),
+                    (T.pl[:, 16:18 * H:18], T.eye[:, :], fa, False, False)], 36 * H + 64, ["eye", "neye", "c1", F, "ae%d" % J], ["pl"])
+                mm([(T.pl[:, 18 * h:18 * h + 16], T.hblk[:, :], T.ff[:, I, 16 * h:16 * h + 16], False, False) for h in range(H)] +
+                   [(T.pl[:, 17:18 * H:18], T.neye[:, :], T.mk[:, J, 24:24 + H], False, True)], 64 * H + 64,
+                   ["neye", "hblk", "ff%d" % I, "mk%d" % J], ["pl"])
+                add("V", vns(18 * H), ["rs"], ["pl", "ls%d" % J], lambda g, J=J, H=H: g.vector.tensor_tensor_scan(
+                    T.ls[:, J, 0:18 * H], T.rs[:, 0:18 * H], T.pl[:, 0:18 * H], 0.0, A.mult, A.max))
+                cp(T.su[:, J, 0:H], T.ls[:, J, 17:18 * H:18], H, ["ls%d" % J], ["su%d" % J])
+                gtt(T.sv[:, J, 0:n], win.indirect(ua), T.ff[:, I, 0:n], A.max, n, tks + [UA, "ff%d" % I], ["sv%d" % J])
+                gcp(tsb[:, 0:1936].indirect(T.su[:, J, 0:H]), T.sv[:, J, 0:n], n, ["su%d" % J, "sv%d" % J], tks, SC)
+            Y = "yy%d" % I
             for m in range(3):
-                x = (m + 2) % 3
-                gtt(T.yy[:, I % 2, m, 0:n], win.indirect(T.ui[:, I, y0 + x * H:y0 + (x + 1) * H]), T.ff[:, I, 0:n], A.min, n,
-                    tks + [U + "y", "ff%d" % I], [Y + str(m)])
-            if t < 2:
-                add("V", 50 + 0.83 * SC * n, ["su%d" % J, "sv%d" % J], tks, lambda g, J=J, n=n, H=H, tsb=tsb: g.vector.tensor_copy(
-                    tsb[:, 0:1936].indirect(T.su[:, J, 0:H]), T.sv[:, J, 0:n]))
+                tt(T.yy[:, I, m, 0:n], T.nf[:, I, 0:nsb, (m + 2) % 3, :], T.ff[:, I, 0:n], A.mult, n, ["nf%d" % I, "ff%d" % I], [Y + str(m)], 1.0)
             ml = []
             for h in range(H):
-                ml.append((T.po[0:24, :, h], T.of[:, :], T.ff[:, I, 16 * h:16 * h + 16], True, False))
+                for x in range(2): ml.append((T.po[0:24, :, h], T.of[:, x, :], T.ff[:, I, 16 * h:16 * h + 16], x == 0, False))
                 for m in range(3):
-                    ml.append((T.po[0:24, :, h], T.zo[:, 2 - m:26 - m], T.yy[:, I % 2, m, 16 * h:16 * h + 16], False, m == 2))
-            mm(ml, H * 24 * 13, ["of", "zo", "ff%d" % I, Y + "0", Y + "1", Y + "2"], ["po"])
-            act(T.yb[0:24, t, :, H0[c]:H0[c] + H], T.po[0:24, :, 0:H], AF.Identity, n, [], ["po", "yb%d" % I], bias=-1.0)
+                    ml.append((T.po[0:24, :, h], T.zo[:, 2 - m:26 - m], T.yy[:, I, m, 16 * h:16 * h + 16], False, m == 2))
+            mm(ml, H * 24 * 5, ["of0", "of1", "zo", "ff%d" % I, Y + "0", Y + "1", Y + "2"], ["po"])
+            act(T.yb[0:24, t, :, h0:h0 + H], T.po[0:24, :, 0:H], AF.Identity, n, [], ["po", "yb%d" % I], bias=-1.0)
         dma(T.yn[:, 768 * t:768 * (t + 1)], T.yb[0:24, t], 24 * 1024, ["yb%d" % (t * NC + c) for c in range(NC)], ["yn%d" % t])
     return ops
 
 
-def plan(ops, alt=(), dma0=2000.0, tries=TRIES):
+def plan(ops, alt=(), dma0=1500.0, tries=TRIES):
     lw, lr = {}, {}
     for i, o in enumerate(ops):
         d = set()

@@ -1,19 +1,26 @@
 import numpy as np
-from concourse.bass import DstId, RemoteDMATransfer
 from concourse.mybir import AluOpType as A, ActivationFunctionType as AF
 
-SPLIT = ["UWWW WWWW", "WWWW WWWW", "WWWW WWWW"]
+SPLIT = ["UWWW WWWW", "XWWW XWWW", "XWWW WWWN"]
 FINE = 1
-EVS = 5
-SCS = 0
-FIGS = [(1.56, 3.8, 0.42, 120.0, 2200.0), (1.1, 2.0, 0.42, 100.0, 1800.0), (2.0, 5.5, 0.42, 100.0, 2200.0), (1.56, 3.8, 0.55, 200.0, 4000.0)]
-TRIES = 600
-SB = [r.split() for r in SPLIT]
+EVV = (5,)
+FFV = ()
+NM1 = 1
+ENDS = (0, 1, 2, 3, 5)
+PACK = any(k in "".join(SPLIT) for k in "FGA")
+K = 4096.0
+FIGS = [(1.56, 3.8, 0.42, 70.0, 1600.0), (1.1, 2.0, 0.42, 60.0, 1500.0), (2.0, 5.5, 0.42, 60.0, 1500.0), (1.3, 3.8, 0.45, 120.0, 2600.0)]
+RATE = 500.0
+TRIES = 100
+MOVES = 100000
+SB = [[c.replace("|", "") for c in r.split()] for r in SPLIT]
+CUT = [[[len(x) for x in c.split("|")] for c in r.split()] for r in SPLIT]
 NC = len(SB[0])
 HS = [2 * len(c) for c in SB[0]]
 H0 = [sum(HS[:c]) for c in range(NC)]
 DUM = 1808
-OFF = 1800.0
+WIN = 3856
+OFF = 1828.0
 BIG = 12582912.0
 CW = 251.0 / 65536
 
@@ -28,50 +35,55 @@ def _cand1():
     out = []
     for o, a, b, c in [(0, 4, 2, 3), (0, 1, 4, 3), (0, 1, 2, 4), (1, 2, 3, 4)]:
         out += [_col(o, b), _col(o, c), _col(o, a), _val(b, c), _val(a, c), _val(a, b), _col(o, 5), _col(a, b), _col(a, c),
-                _col(a, 5), _val(a, 5), _val(b, 5), _val(c, 5)]
+                _col(a, 5), _val(a, 5), _val(b, 5), _val(c, 5), 27]
     return out
 
 
 CAND1 = _cand1()
 CAND2 = [0, 1, 6, 3, 12, 11, 6, 1, 2, 12, 4, 10, 0, 6, 2, 11, 10, 5, 8, 9, 7, 12, 11, 3]
-NQ = (13, 6)
+NQ = (14, 6)
+NR = (13, 6)
 
 SCRATCH = {
     "cv": ("sbuf", [128, 4112], "bfloat16"), "ob": ("sbuf", [128, 1536], "bfloat16"), "gp": ("sbuf", [128, 12, 256], "bfloat16"),
     "gp0": ("sbuf", [128, 16, 8, 3, 2], "bfloat16"), "pi": ("sbuf", [128, 8], "int32"), "pf": ("sbuf", [128, 8], "float32"),
     "ia": ("sbuf", [128, 144], "float32"), "ib": ("sbuf", [128, 128], "float32"), "ik": ("sbuf", [128, 8, 18], "float32"),
-    "ij": ("sbuf", [128, 128], "float32"), "ic": ("sbuf", [128, 8, 18], "float32"), "id3": ("sbuf", [128, 24], "float32"),
+    "ic": ("sbuf", [128, 8, 18], "float32"), "id3": ("sbuf", [128, 24], "float32"),
     "tm": ("sbuf", [128, 8, 18], "float32"), "one": ("sbuf", [128, 128], "float32"), "cb0": ("sbuf", [128, 8, 3, 2], "float32"),
-    "blk": ("sbuf", [128, 128], "bfloat16"), "hblk": ("sbuf", [128, 128], "bfloat16"), "eye": ("sbuf", [128, 128], "bfloat16"),
-    "neye": ("sbuf", [128, 128], "bfloat16"), "ceye": ("sbuf", [128, 128], "bfloat16"), "imt": ("sbuf", [128, 128], "bfloat16"),
+    "blk": ("sbuf", [128, 128], "bfloat16"), "nblk": ("sbuf", [128, 128], "bfloat16"), "eye": ("sbuf", [128, 128], "bfloat16"),
+    "neye": ("sbuf", [128, 128], "bfloat16"), "imt": ("sbuf", [128, 128], "bfloat16"),
     "t2": ("sbuf", [128, 128], "bfloat16"), "zz": ("sbuf", [128, 144], "bfloat16"), "zc": ("sbuf", [128, 144], "bfloat16"),
     "zs": ("sbuf", [128, 144], "bfloat16"), "zo": ("sbuf", [128, 32], "bfloat16"), "of": ("sbuf", [128, 2, 24], "bfloat16"),
     "sk": ("sbuf", [128, 16], "float32"), "nr": ("sbuf", [128, 16, 128], "bfloat16"), "ee": ("sbuf", [128, 16, 128], "bfloat16"),
     "c1": ("sbuf", [128, 8, 18], "float16"), "rs": ("sbuf", [128, 144], "float32"), "tie": ("sbuf", [128, 4, 8], "bfloat16"),
-    "k18": ("sbuf", [128, 3, 128], "bfloat16"), "cb": ("sbuf", [128, 15, 16], "float32"), "gs": ("sbuf", [128, 240], "float32"),
-    "ww": ("sbuf", [128, 448], "float32"), "tab": ("sbuf", [128, 160], "float32"), "tb2": ("sbuf", [128, 80], "float32"),
-    "tb3": ("sbuf", [128, 80], "float32"), "o1": ("sbuf", [128, NC, 26], "uint16"), "ol": ("sbuf", [128, 52], "uint16"),
+    "cb": ("sbuf", [128, 15, 16], "float32"), "wt": ("sbuf", [128, 32], "float32"),
+    "ww": ("sbuf", [128, 432], "float32"), "wi": ("sbuf", [128, 464], "float32"), "tab": ("sbuf", [128, 124], "float32"), "tb2": ("sbuf", [128, 40], "float32"),
+    "tb3": ("sbuf", [128, 40], "float32"), "o1": ("sbuf", [128, NC, 28], "uint16"), "ol": ("sbuf", [128, 56], "uint16"),
     "ui0": ("sbuf", [128, 48], "uint16"), "ua0": ("sbuf", [128, 16], "uint16"), "fi0": ("sbuf", [128, 4, 16], "float16"),
-    "cand1": ("sbuf", [128, NC, 416], "float32"), "cand2": ("sbuf", [128, NC, 192], "float32"),
-    "msk": ("sbuf", [128, 2 * NC, 416], "float16"), "sc": ("sbuf", [128, 2 * NC, 32], "float32"),
+    "cand1": ("sbuf", [128, NC, 448], "float32"), "cand2": ("sbuf", [128, NC, 192], "float32"),
+    "msk": ("sbuf", [128, 2 * NC, 448], "float16"), "sc": ("sbuf", [128, 2 * NC, 32], "float32"),
     "m1": ("sbuf", [128, 2 * NC, 16], "float32"), "m2": ("sbuf", [128, 2 * NC, 8], "float32"), "mk": ("sbuf", [128, 2 * NC, 32], "bfloat16"),
-    "uo": ("sbuf", [128, 2 * NC, 128], "uint16"), "ui": ("sbuf", [128, 2 * NC, 128], "uint16"),
+    "mi": ("sbuf", [128, 2 * NC, 32], "bfloat16"), "ui": ("sbuf", [128, 2 * NC, 48], "uint16"), "so": ("sbuf", [128, NC, 104], "float32"),
     "fi": ("sbuf", [128, 2 * NC, 4, 8], "float16"), "si": ("sbuf", [128, NC, 104], "float32"),
     "nm": ("sbuf", [128, 3 * NC, 384], "uint16"), "nf": ("sbuf", [128, 3 * NC, 4, 3, 32], "float16"),
     "hd": ("sbuf", [128, 3 * NC, 4, 128], "bfloat16"), "h2": ("sbuf", [128, 3 * NC, 128], "bfloat16"),
     "ff": ("sbuf", [128, 3 * NC, 128], "bfloat16"), "ae": ("sbuf", [128, 2 * NC, 8, 18], "bfloat16"),
     "yy": ("sbuf", [128, 3 * NC, 3, 128], "float16"), "sv": ("sbuf", [128, 2 * NC, 128], "int32"), "ls": ("sbuf", [128, 2 * NC, 144], "float32"),
     "su": ("sbuf", [128, 2 * NC, 8], "uint16"), "yb": ("sbuf", [128, 3, 16, 16], "float32"),
+    "k18": ("sbuf", [128, 128], "float16"), "eyes": ("sbuf", [128, 6, 128], "bfloat16"), "zf": ("sbuf", [128, 144], "float32"),
+    "zer": ("sbuf", [128, 3, 128], "bfloat16"), "un": ("sbuf", [128, NC, 2, 128], "float16"), "ys": ("sbuf", [128, 512], "float32"),
     "pm0": ("psum", [128, 4, 128], "float32"), "pm1": ("psum", [128, 4, 128], "float32"), "pe": ("psum", [128, 512], "float32"),
-    "pf1": ("psum", [128, 512], "float32"), "pc": ("psum", [128, 64, 8], "float32"), "pl": ("psum", [128, 512], "float32"),
+    "pf1": ("psum", [128, 512], "float32"), "py0": ("psum", [128, 512], "float32"), "py1": ("psum", [128, 512], "float32"),
     "ps": ("psum", [128, 256, 2], "float32"), "po": ("psum", [128, 16, 32], "float32"),
 }
 for _c in range(NC):
-    SCRATCH["ts%d" % _c] = ("sbuf", [128, 1936], "int32")
+    SCRATCH["zq%d" % _c] = ("sbuf", [128, 256 * HS[_c]], "float32")
+    SCRATCH["pq%d" % _c] = ("sbuf", [128, 256 * HS[_c]], "bfloat16")
+    SCRATCH["ts%d" % _c] = ("sbuf", [128, WIN], "int32")
     for _t in range(2):
         SCRATCH["gv%d_%d" % (_t, _c)] = ("sbuf", [128, 768 * HS[_c]], "bfloat16")
         SCRATCH["pr%d_%d" % (_t, _c)] = ("sbuf", [128, 768 * HS[_c]], "bfloat16")
-SEMAPHORES = ["eV", "eS", "eP", "eG", "sent"] + ["d%d" % i for i in range(24)] + ["r%d" % i for i in range(2 * NC)]
+SEMAPHORES = ["eV", "eS", "eP", "eG", "sent"] + ["d%d" % i for i in range(24)] + ["rmi%d" % i for i in range(2 * NC)] + ["rsi%d" % i for i in range(NC)] + ["rwi"]
 
 
 BANKS = [k for k in SCRATCH if SCRATCH[k][0] == "psum"]
@@ -109,12 +121,14 @@ def build(T, nxt, topo, core, fig=FIGS[0]):
     def iota(out, pat, base, cm, n, wr, fl=True):
         if fl: add("G", 130 + 1.66 * n, [], wr, lambda g: g.iota(out, pat, base, cm, allow_small_or_imprecise_dtypes=True))
         else: add("G", 130 + 1.66 * n, [], wr, lambda g: g.iota(out, pat, base, cm))
+    def select(out, a, pat, op, fill, base, cm, n, rd, wr):
+        add("G", 170 + 1.66 * n, rd, wr, lambda g: g.affine_select(out, a, pat, op, fill, base, cm))
     def mm(lst, cyc, rd, wr):
         def fn(g):
             for m in lst: r = g.tensor.matmul(*m)
             return r
         add("P", 40 + PC * cyc + 8 * len(lst), rd, wr, fn)
-    def dma(out, in_, nbytes, rd, wr): add("Y", nbytes / 250.0, rd, wr, lambda g: g.sync.dma_start(out, in_), "dma")
+    def dma(out, in_, nbytes, rd, wr): add("Y", nbytes / RATE, rd, wr, lambda g: g.sync.dma_start(out, in_), "dma")
 
     dma(T.ob[:, 0:1024], T.obs[:, 0:1024], 128 * 2048, [], ["ob0"])
     part = [[2] * len(SB[0][c]) if c < FINE else [HS[c]] for c in range(NC)]
@@ -130,12 +144,11 @@ def build(T, nxt, topo, core, fig=FIGS[0]):
 
     iota(T.pi[:, 0:1], [[0, 1]], 0, 1, 1, ["pi0"], False)
     iota(T.ia[:, :], [[1, 144]], 0, 0, 144, ["ia"])
-    cp(T.pf[:, 0:1], T.pi[:, 0:1], 1, ["pi0"], ["pf0"])
     ts(T.pi[:, 4:5], T.pi[:, 0:1], 4, None, A.arith_shift_right, None, 1, ["pi0"], ["pi4"])
     ts(T.pf[:, 5:6], T.pi[:, 4:5], 16.0, 15.0, A.mult, A.add, 1, ["pi4"], ["pf5"])
     ts(T.zs[:, :], T.ia[:, :], T.pf[:, 5:6], 1.0 / 16, A.is_equal, A.mult, 144, ["ia", "pf5"], ["zs"])
-    ts(T.zz[:, :], T.zs[:, :], 16.0, None, A.mult, None, 144, ["zs"], ["zz"], 0.5)
-    ts(T.zc[:, :], T.zs[:, :], 16.0 * CW, None, A.mult, None, 144, ["zs"], ["zc"], 0.5)
+    act(T.zz[:, :], T.zs[:, :], AF.Identity, 144, ["zs"], ["zz"], scale=64.0)
+    act(T.zc[:, :], T.zs[:, :], AF.Identity, 144, ["zs"], ["zc"], scale=16.0 * CW)
     ts(T.pi[:, 1:2], T.pi[:, 0:1], 15, None, A.bitwise_and, None, 1, ["pi0"], ["pi1"])
     ts(T.pi[:, 2:3], T.pi[:, 0:1], 7, None, A.bitwise_and, None, 1, ["pi0"], ["pi2"])
     ts(T.pi[:, 3:4], T.pi[:, 0:1], 3, 1, A.arith_shift_right, A.bitwise_and, 1, ["pi0"], ["pi3"])
@@ -145,57 +158,59 @@ def build(T, nxt, topo, core, fig=FIGS[0]):
     for c in range(NC):
         iota(T.cb0[0:1, H0[c] // 2:(H0[c] + HS[c]) // 2], [[64 * 226, HS[c] // 2], [0, 3], [32 * 226, 2]], -15, 0, 3 * HS[c], ["cb0%d" % c])
     for c in range(NC):
-        iota(T.cb[:, :, H0[c]:H0[c] + HS[c]], [[0, 15], [-226, HS[c]]], int(BIG + OFF), 0, 15 * HS[c], ["cb%d" % c])
+        iota(T.cb[0:1, :, H0[c]:H0[c] + HS[c]], [[0, 15], [32 * 226, HS[c]]], -15 - 32 * int(OFF), 0, 15 * HS[c], ["cb%d" % c])
     cbs = ["cb%d" % c for c in range(NC)]
     iota(T.ib[:, :], [[1, 8], [0, 16]], 0, 0, 128, ["ib"])
-    iota(T.ij[:, :], [[0, 8], [1, 16]], 0, 0, 128, ["ij"])
-    iota(T.ik[:, :, :], [[0, 8], [1, 18]], 0, 0, 144, ["ik"])
-    iota(T.ic[:, :, :], [[16, 8], [0, 18]], DUM - 2048 + 30000, 0, 144, ["ic"])
     iota(T.id3[:, :], [[1, 8], [0, 3]], 0, 0, 24, ["id3"])
     ts(T.blk[:, :], T.ib[:, :], T.pf[:, 4:5], None, A.is_equal, None, 128, ["ib", "pf"], ["blk"])
-    ts(T.hblk[:, :], T.blk[:, :], 0.5, None, A.mult, None, 128, ["blk"], ["hblk"], 0.5)
-    ts(T.eye[:, :], T.ia[:, 0:128], T.pf[:, 0:1], None, A.is_equal, None, 128, ["ia", "pf0"], ["eye"])
-    ts(T.neye[:, :], T.eye[:, :], -1048576.0, None, A.mult, None, 128, ["eye"], ["neye"], 0.5)
-    ts(T.ceye[:, :], T.eye[:, :], -CW, None, A.mult, None, 128, ["eye"], ["ceye"], 0.5)
-    ts(T.t2[:, :], T.ij[:, :], T.pf[:, 1:2], -1.0, A.is_gt, A.mult, 128, ["ij", "pf"], ["t2"])
-    tt(T.t2[:, :], T.t2[:, :], T.blk[:, :], A.mult, 128, ["t2", "blk"], ["t2"], 1.0)
-    tt(T.imt[:, :], T.t2[:, :], T.eye[:, :], A.add, 128, ["t2", "eye"], ["imt"], 1.0)
+    select(T.eye[:, :], T.blk[:, :], [[-1, 128]], A.is_equal, 0.0, 0, 1, 128, ["blk"], ["eye"])
+    act(T.neye[:, :], T.eye[:, :], AF.Identity, 128, ["eye"], ["neye"], scale=-2097152.0)
+    act(T.nblk[:, :], T.blk[:, :], AF.Identity, 128, ["blk"], ["nblk"], scale=-1.0)
+    select(T.t2[:, :], T.nblk[:, :], [[1, 128]], A.is_gt, 0.0, 0, -1, 128, ["nblk"], ["t2"])
+    select(T.imt[:, :], T.t2[:, :], [[-1, 128]], A.not_equal, 1.0, 0, 1, 128, ["t2"], ["imt"])
     ts(T.zo[:, :], T.ia[:, 0:32], T.pf[:, 6:7], None, A.is_equal, None, 32, ["ia", "pf6"], ["zo"])
     ts(T.of[:, 0, :], T.id3[:, :], T.pf[:, 4:5], 0.5, A.is_equal, A.mult, 24, ["id3", "pf"], ["of0"])
-    ts(T.of[:, 1, :], T.id3[:, :], T.pf[:, 4:5], 1.0 / 4096, A.is_equal, A.mult, 24, ["id3", "pf"], ["of1"])
+    act(T.of[:, 1, :], T.of[:, 0, :], AF.Identity, 24, ["of0"], ["of1"], scale=1.0 / 2048)
+    iota(T.zer[:, :, :], [[0, 384]], 0, 0, 384, ["zer"])
+    if PACK:
+        for i, x in enumerate((K, -1.0, -1.0 / K, -CW, CW, CW * K)):
+            act(T.eyes[:, i, :], T.eye[:, :], AF.Identity, 128, ["eye"], ["eyes%d" % i], scale=x)
+        act(T.zf[:, :], T.zs[:, :], AF.Identity, 144, ["zs"], ["zf"], scale=16.0 / K)
+        ts(T.k18[:, :], T.ia[:, 0:128], 0.0, OFF, A.mult, A.add, 128, ["ia"], ["k18"])
     ts(T.sk[:, :], T.ia[:, 0:16], T.pf[:, 1:2], -CW, A.is_equal, A.mult, 16, ["ia", "pf"], ["sk"])
     for k in range(16):
         act(T.nr[:, k, :], T.blk[:, :], AF.Identity, 128, ["blk", "sk"], ["nr%d" % k], scale=T.sk[:, k:k + 1])
     nrs = ["nr%d" % k for k in range(16)]
-    add("G", 170 + 1.66 * 2048, nrs, ["ee"],
-        lambda g: g.affine_select(T.ee[:, :, :], T.nr[:, :, :], [[0, 16], [-1, 128]], A.not_equal, CW, 0, 1))
-    ts(T.tm[:, :, :], T.ik[:, :, :], T.pf[:, 1:2], None, A.is_lt, None, 144, ["ik", "pf"], ["tm"])
-    ts(T.ic[:, :, :], T.ic[:, :, :], T.pf[:, 1:2], None, A.add, None, 144, ["ic", "pf"], ["ic"])
-    tt(T.tm[:, :, :], T.tm[:, :, :], T.ic[:, :, :], A.mult, 144, ["tm", "ic"], ["tm"])
-    ts(T.c1[:, :, :], T.tm[:, :, :], -30000.0, None, A.add, None, 144, ["tm"], ["c1"])
-    ts(T.c1[:, :, 16], T.ik[:, :, 0], OFF, None, A.add, None, 8, ["ik", "c1"], ["c1"])
-    ts(T.c1[:, :, 17], T.ic[:, :, 0], 2048.0 - 30000.0, None, A.add, None, 8, ["ic", "c1"], ["c1"])
-    ts(T.rs[:, :], T.ik[:, :, :], 0.0, None, A.is_gt, None, 144, ["ik"], ["rs"])
-    ms(T.ae[:, :, :, 16:18], 0.0, 64, ["aez"])
-    ms(T.cv[:, 4096:4112], 0.0, 16, ["cvz"])
-    ms(T.k18[:, :, :], OFF, 384, ["k18"])
-    ms(T.tie[:, 0, :], 0.5, 8, ["tie0"]); ms(T.tie[:, 1, :], 0.25, 8, ["tie1"]); ms(T.tie[:, 2:4, :], 0.0, 16, ["tie2"])
-    ms(T.ww[:, 432:448], 0.0, 32, ["wwz"])
-    rows = [16 * x for x in CAND1] + [8 * x for x in CAND2] + [8 * (i // 13) for i in range(52)] + [8 * (i // 6) for i in range(24)] + [0] * 4
+    select(T.ee[:, :, :], T.nr[:, :, :], [[0, 16], [-1, 128]], A.not_equal, CW, 0, 1, 2048, nrs, ["ee"])
+    iota(T.ik[:, :, 0:16], [[0, 8], [1, 16]], 0, 0, 128, ["ik0"]); iota(T.ik[:, :, 16:18], [[0, 16]], -1, 0, 16, ["ik1"])
+    iota(T.ic[:, :, 0:16], [[2, 8], [0, 16]], DUM - 4096, 16, 128, ["ic0"]); iota(T.ic[:, :, 16], [[0, 8]], int(OFF), 0, 8, ["ic1"])
+    iota(T.ic[:, :, 17], [[2, 8]], DUM, 16, 8, ["ic2"])
+    ts(T.tm[:, :, :], T.ik[:, :, :], T.pf[:, 1:2], -30000.0, A.is_ge, A.mult, 144, ["ik0", "ik1", "pf"], ["tm"])
+    tt(T.c1[:, :, :], T.tm[:, :, :], T.ic[:, :, :], A.add, 144, ["tm", "ic0", "ic1", "ic2"], ["c1"])
+    iota(T.rs[:, :], [[0, 144]], 1, 0, 144, ["rs"]); iota(T.rs[:, 0:144:18], [[0, 8]], 0, 0, 8, ["rs"])
+    iota(T.ae[:, :, :, 16:18], [[0, 32 * NC]], 0, 0, 32 * NC, ["aez"])
+    iota(T.cv[:, 4096:4112], [[0, 16]], 0, 0, 16, ["cvz"])
+    iota(T.wi[:, 432:464], [[0, 32]], 0, 0, 32, ["wiz"])
+    iota(T.tie[:, 0:3, :], [[-1, 3], [0, 8]], 2, 0, 24, ["tie0"]); iota(T.tie[:, 3, :], [[0, 8]], 0, 0, 8, ["tie1"])
+    iota(T.wt[:, 0:24], [[0, 24]], 1, 0, 24, ["wt"]); iota(T.wt[:, 24:32], [[0, 8]], 64, 0, 8, ["wt"])
+    rows = [16 * x for x in CAND1] + [8 * x for x in CAND2]
     tabs = []
     for i, n, b, st in runs(rows[0::2] + [y - x for x, y in zip(rows[0::2], rows[1::2])]):
         tabs.append("tab%d" % i); iota(T.tab[:, i:i + n], [[st, n]], b, 0, n, [tabs[-1]])
-    ts(T.tb2[:, 0:78], T.tab[:, 78:156], T.pf[:, 3:4], T.pf[:, 2:3], A.mult, A.add, 78, tabs + ["pf"], ["tb2"])
-    tt(T.tb3[:, 0:78], T.tb2[:, 0:78], T.tab[:, 0:78], A.add, 78, tabs + ["tb2"], ["tb3"])
+    iota(T.tab[:, 80:108], [[8, 4], [0, 7]], 0, 0, 28, ["tr1"]); iota(T.tab[:, 108:120], [[8, 4], [0, 3]], 0, 0, 12, ["tr2"])
+    iota(T.tab[:, 120:124], [[0, 4]], 0, 0, 4, ["tr3"])
+    ts(T.tb2[:, :], T.tab[:, 40:80], T.pf[:, 3:4], T.pf[:, 2:3], A.mult, A.add, 40, tabs + ["pf"], ["tb2"])
+    tt(T.tb3[:, :], T.tb2[:, :], T.tab[:, 0:40], A.add, 40, tabs + ["tb2"], ["tb3"])
     for c in range(NC):
-        ts(T.o1[:, c, :], T.tb3[:, 0:26], float(H0[c]), None, A.add, None, 26, ["tb3"], ["o1%d" % c])
-    cp(T.ol[:, :], T.tb3[:, 26:78], 52, ["tb3"], ["ol"])
+        ts(T.o1[:, c, :], T.tb3[:, 0:28], float(H0[c]), None, A.add, None, 28, ["tb3"], ["o1%d" % c])
+    cp(T.ol[:, 0:12], T.tb3[:, 28:40], 12, ["tb3"], ["o2"])
+    ts(T.ol[:, 12:56], T.tab[:, 80:124], T.pf[:, 2:3], None, A.add, None, 44, ["tr1", "tr2", "tr3", "pf"], ["ol"])
 
     def star(j, n=1): return T.ob[:, 256 * j:256 * (j + n)]
     for w in range(3):
         tt(T.gp0[:, :, :, w, :], star(0), star(PAIRS[12 + w][1]), A.mult, 256, ["ob0"], ["gq%d" % w], 1.0)
     for i in range(3):
-        tt(T.gp[:, i, :], star(PAIRS[i][0]), star(PAIRS[i][1]), A.mult, 256, ["ob0"], ["gp%d" % i], 1.0)
+        tt(T.gp[:, i, :], star(PAIRS[i][0]), star(PAIRS[i][1]), A.mult, 256, ["ob0", "c1", "of0", "zo"], ["gp%d" % i], 1.0)
     for i in (3, 5, 7, 9):
         tt(T.gp[:, i:i + 2, :], star(PAIRS[i][0], 2), star(4, 2), A.mult, 512, ["ob0", "ob1"], ["gp%d" % i], 1.0)
     tt(T.gp[:, 11, :], star(0), star(5), A.mult, 256, ["ob0", "ob1"], ["gp11"], 1.0)
@@ -204,31 +219,52 @@ def build(T, nxt, topo, core, fig=FIGS[0]):
     mm([(T.pf1[:, 0:48], T.one[0:1, :], T.cb0[0:1], True, False)], 256, ["one"] + ["cb0%d" % c for c in range(NC)], ["pf1"])
     mm([(T.pf1[:, 0:48], L(T.zs, k), T.gp0[:, k], False, k == 15) for k in range(16)], 1024, gq, ["pf1"])
     ts(T.ui0[:, :], T.pf1[:, 0:48], BIG, BIG, A.add, A.subtract, 48, [], ["pf1", "uz"])
-    mm([(T.pe[:, 192 + 16 * w:208 + 16 * w], L(T.zs, k), T.gp0[:, k, :, w, :], k == 0, k == 15) for w in range(3) for k in range(16)], 3072, gq, ["pe"])
-    mm([(T.pe[:, 0:192], L(T.zs, k), T.gp[:, :, 16 * k:16 * k + 16], k == 0, k == 15) for k in range(16)], 3072,
-       ["zs"] + ["gp%d" % i for i in (0, 1, 2, 3, 5, 7, 9, 11)], ["pe"])
+    gps = ["zs"] + ["gp%d" % i for i in (0, 1, 2, 3, 5, 7, 9, 11)]
+    mm([(T.py0[:, 0:240], T.one[0:1, :], T.cb[0:1], True, False)], 960, ["one"] + cbs, ["py0"])
+    mm([(T.py0[:, 192 + 16 * w:208 + 16 * w], L(T.zs, k), T.gp0[:, k, :, w, :], False, False) for w in range(3) for k in range(16)], 3072, gq, ["py0"])
+    mm([(T.pe[:, 0:192], L(T.zs, k), T.gp[:, :, 16 * k:16 * k + 16], k == 0, k == 15) for k in range(16)], 3072, gps, ["pe"])
+    mm([(T.py0[:, 0:192], L(T.zs, k), T.gp[:, :, 16 * k:16 * k + 16], False, k == 15) for k in range(16)], 3072, gps, ["py0"])
     act(T.ww[:, 240:432], T.pe[:, 0:192], AF.Identity, 192, [], ["pe", "wwv"], bias=-OFF, scale=16.0)
-    ts(T.gs[:, :], T.pe[:, 0:240], -15.0 / 32, BIG, A.add, A.add, 240, [], ["pe", "gs"])
-    tt(T.ww[:, 0:240], T.gs[:, :], T.cb[:, :, :], A.subtract, 240, ["gs"] + cbs, ["wwc"])
+    ts(T.ww[:, 0:240], T.py0[:, 0:240], BIG, BIG, A.add, A.subtract, 240, [], ["py0", "wwc"])
     cp(T.fi0[:, :, :], T.ww[:, 224:288], 64, ["wwc", "wwv"], ["fz"])
     ts(T.ua0[:, :], T.ww[:, 224:240], OFF, None, A.add, None, 16, ["wwc"], ["ua0"])
 
     rid, pid, _ = topo.addr(nxt)
     mask = sum(1 << e for e in topo.engines(core, nxt)[:8])
+    def send(dst, src, rd, tok):
+        add("G", 300, rd, [tok], lambda g: g.remote_dma(dst, src, T.sem["r" + tok], T.sem.sent, pid, rid, mask), "r" + tok)
+    send(T.wi[:, 0:432], T.ww[:, :], ["wwc", "wwv"], "wi")
+    Q = 0
+    ny = [0]
+    pc, pck, pl, plk = (T.ps[:, 128:144, :], "ps", T.pe[:, 256:512], "pe") if PACK else (T.py0[:, 0:32], "py0", T.py1, "py1")
 
     for t in range(3):
+        ybs = []
         for c in range(NC):
-            I = t * NC + c; H = HS[c]; n = 16 * H; tsb = T["ts%d" % c]; nsb = H // 2; h0 = H0[c]
+            I = J = t * NC + c; H = HS[c]; n = 16 * H; tsb = T["ts%d" % c]; nsb = H // 2; h0 = H0[c]
             tks = ["ts%d_%d" % (c, s) for s in range(len(part[c]))]; fine = t == 0 and len(tks) > 1
-            pm = T["pm%d" % (I % 2)]; pmk = "pm%d" % (I % 2)
             if t == 0:
                 U, UA, F = "uz", "ua0", "fz"
                 ul, u0, ua, fa, fd = T.ui0, 3 * h0, T.ua0[:, h0:h0 + H], T.fi0[:, 0, h0:h0 + H], T.fi0[:, 1:4, h0:h0 + H]
             else:
-                M = I - NC; U = UA = "ui%d" % M; F = "fi%d" % M
-                ul, u0, ua, fa, fd = T.ui[:, M], 8 * NQ[t - 1], T.ui[:, M, 16:16 + H], T.fi[:, M, 0, 0:H], T.fi[:, M, 1:4, 0:H]
-                ts(T.fi[:, M], T.ui[:, M, 16:48], -OFF, None, A.add, None, 32, [U], [F])
-                if t == 1: ts(T.si[:, c, :], T.ui[:, M, 0:104], -OFF, None, A.add, None, 104, [U], ["si%d" % c])
+                M = I - NC; U = UA = "ui%d" % M; F = "fi%d" % M; nq, nr = NQ[t - 1], NR[t - 1]
+                ul, u0, ua, fa, fd = T.ui[:, M], 0, T.ui[:, M, 40:40 + H], T.fi[:, M, 0, 0:H], T.fi[:, M, 1:4, 0:H]
+                if t == 1:
+                    cand, rep = T.cand1[:, c, :], T.ol[:, 12:40]
+                    act(cand, T.wi[:, :].indirect(T.o1[:, c, :]), AF.Copy, 448, ["wi", "wiz", "o1%d" % c], ["cand%d" % M], r=GC)
+                else:
+                    cand, rep = T.cand2[:, c, :], T.ol[:, 40:52]
+                    act(cand, T.si[:, c, :].indirect(T.ol[:, 0:12]), AF.Copy, 192, ["si%d" % c, "o2"], ["cand%d" % M], r=GC)
+                gtt(T.msk[:, M, 0:32 * nq], T.mi[:, M, :].indirect(rep), cand, A.mult, 32 * nq, ["mi%d" % M, "cand%d" % M, "ol"], ["msk%d" % M])
+                mm([(T.ps[:, x:3 * nsb:3, :], T.eye[:, :], T.msk[:, M, 8 * (nq * q + x):8 * (nq * q + x) + H], q + x == 0, False)
+                    for q in range(4) for x in range(3)] +
+                   [(T.ps[:, 12:12 + 4 * nr, :], T.eye[:, :], T.msk[:, M, 8 * nq * q:8 * (nq * q + nr)], False, q == 3) for q in range(4)],
+                   768 + 4 * max(64, 8 * nr), ["eye", "msk%d" % M], ["ps"])
+                ts(T.ui[:, M, :], T.ps[:, 0:24, :], OFF, None, A.add, None, 48, [], ["ps", U])
+                cp(T.fi[:, M], T.ps[:, 20:36, :], 32, [], ["ps", F])
+                if t == 1:
+                    act(T.so[:, c, :], T.ps[:, 12:64, :], AF.Identity, 104, [], ["ps", "so%d" % c])
+                    send(T.si[:, c, :], T.so[:, c, :], ["so%d" % c], "si%d" % c)
             win = tsb[:, 0:226 * H]
             if fine:
                 for s in range(nsb):
@@ -236,114 +272,147 @@ def build(T, nxt, topo, core, fig=FIGS[0]):
                         [U] + tks[:s + 1], ["nm%d_%d" % (I, s)])
                 nms = ["nm%d_%d" % (I, s) for s in range(nsb)]
             else:
-                gcp(T.nm[:, I, 0:3 * n], win.indirect(ul[:, u0:u0 + 3 * H]), 3 * n, [U] + tks, ["nm%d" % I]); nms = ["nm%d" % I]
+                a = 6 * NM1
+                if a: gcp(T.nm[:, I, 0:16 * a], win.indirect(ul[:, u0:u0 + a]), 16 * a, [U] + tks, ["nm%d_0" % I])
+                gcp(T.nm[:, I, 16 * a:3 * n], win.indirect(ul[:, u0 + a:u0 + 3 * H]), 3 * n - 16 * a, [U] + tks, ["nm%d" % I])
+                nms = ["nm%d_0" % I if s < NM1 else "nm%d" % I for s in range(nsb)]
             ts(T.nf[:, I, 0:nsb], T.nm[:, I, 0:3 * n], -2048.0, 1.0 / 4096, A.add, A.mult, 3 * n, nms, ["nf%d" % I], 0.5)
-            mm([(pm[:, 0:3, 0:n], T.ceye[:, :], T.k18[:, :, 0:n], True, False)], 3 * n, ["ceye", "k18"], [pmk])
-            dlist = [(pm[:, 0:3, k:n:16], T.nr[:, k, :], fd, False, False) for k in range(16)]
             cw = T.cv[:, 0:4097]; w = 512
             gvb = T["gv%d_%d" % (t % 2, c)]; prb = T["pr%d_%d" % (t % 2, c)]
             old = ["mm%d" % c] if t == 2 else []; lt = ["mm%d" % c] if t == 0 else []
-            for s, kd in enumerate(SB[t][c]):
-                e0 = 3 * w * s
-                def gv(a, b): return gvb[:, e0 + a:e0 + b]
-                def pr(a, b): return prb[:, e0 + a:e0 + b]
-                G = "gv%d_%d" % (I, s); P = "pr%d_%d" % (I, s)
-                def lst(a, b): return cw.indirect(T.nm[:, I, 96 * s + a // 16:96 * s + b // 16])
-                rd = [nms[s] if fine else nms[0], "cv", "cvz"] + old
-                last = s == nsb - 1
-                def red(a, b, toks, fin):
-                    mm([(pm[:, a:b, 32 * s:32 * s + 32], L(T.zc, p), prb[:, e0 + a * w + p:e0 + b * w:16], False, fin and p == 15) for p in range(16)],
-                       16 * max(64, (b - a) * 32), ["zc"] + toks, [pmk] + (lt if fin else []))
-                if kd == "W":
-                    act(gv(0, 3 * w), lst(0, 3 * w), AF.Copy, 3 * w, rd, [G], r=GC)
-                    tt(pr(0, 2 * w), gv(0, 2 * w), gv(w, 3 * w), A.mult, 2 * w, [G], [P + "a"], 1.0)
-                    tt(pr(2 * w, 3 * w), gv(0, w), gv(2 * w, 3 * w), A.mult, w, [G], [P + "b"], 1.0)
-                elif kd == "X":
-                    act(gv(0, 2 * w), lst(0, 2 * w), AF.Copy, 2 * w, rd, [G], r=GC)
-                    tt(pr(0, w), gv(0, w), gv(w, 2 * w), A.mult, w, [G], [P + "a"], 1.0)
-                    gtt(pr(w, 2 * w), lst(2 * w, 3 * w), gv(w, 2 * w), A.mult, w, rd + [G], [P + "b"])
-                    gtt(pr(2 * w, 3 * w), lst(2 * w, 3 * w), gv(0, w), A.mult, w, rd + [G], [P + "c"])
-                elif kd == "U":
-                    act(gv(0, 2 * w), lst(0, 2 * w), AF.Copy, 2 * w, rd, [G], r=GC)
-                    gcp(gv(2 * w, 3 * w), lst(2 * w, 3 * w), w, rd, [G + "a"])
-                    tt(pr(0, 2 * w), gv(0, 2 * w), gv(w, 3 * w), A.mult, 2 * w, [G, G + "a"], [P + "a"], 1.0)
-                    tt(pr(2 * w, 3 * w), gv(0, w), gv(2 * w, 3 * w), A.mult, w, [G, G + "a"], [P + "b"], 1.0)
+            s0 = 0
+            for npart in CUT[t][c]:
+                s1 = s0 + npart; x0, x1 = 32 * s0, 32 * s1; nx = x1 - x0
+                pm = T["pm%d" % (Q % 2)]; pmk = "pm%d" % (Q % 2)
+                pack = SB[t][c][s0] in "FGA"
+                ds = s0 if I else s1 - 2
+                if I == 0: mm([(pm[:, 0:3, :], T.eye[:, :], T.zer[:, :, :], True, False)], 384, ["eye", "zer"], [pmk])
+                dlist = [(pm[:, 0:3, x0 + k:x1:16], T.nr[:, k, :], fd[:, :, 2 * s0:2 * s1], I > 0 and k == 0, False) for k in range(16)]
+                if pack:
+                    dlist += [(pm[:, r, x0:x1], T.eyes[:, e, :], T.k18[:, 0:nx], False, False) for r, e in ((3, 1), (3, 2), (2, 3))]
+                for s in range(s0, s1):
+                    kd = SB[t][c][s]; e0 = 3 * w * s
+                    def gv(a, b): return gvb[:, e0 + a:e0 + b]
+                    def pr(a, b): return prb[:, e0 + a:e0 + b]
+                    G = "gv%d_%d" % (I, s); P = "pr%d_%d" % (I, s)
+                    def lst(a, b): return cw.indirect(T.nm[:, I, 96 * s + a // 16:96 * s + b // 16])
+                    rd = [nms[s], "cv", "cvz"] + old
+                    last = s == s1 - 1
+                    def red(a, b, toks, fin):
+                        mm([(pm[:, a:b, 32 * s:32 * s + 32], L(T.zc, p), prb[:, e0 + a * w + p:e0 + b * w:16],
+                             False, fin and p == 15) for p in range(16)],
+                           16 * max(64, (b - a) * 32), ["zc"] + toks, [pmk] + (lt if fin else []))
+                    if pack:
+                        zq, pq = T["zq%d" % c], T["pq%d" % c]; Z, P = "zq%d_%d" % (c, s), "pq%d_%d" % (c, s)
+                        if kd == "A":
+                            act(gv(0, w), lst(0, w), AF.Copy, w, rd, [G], r=GC, scale=K)
+                            act(gv(w, 2 * w), gv(0, w), AF.Copy, w, [G], [G + "b"], scale=1.0 / K)
+                            gtt(T.ys[:, :], lst(2 * w, 3 * w), gv(0, w), A.add, w, rd + [G], ["ys"])
+                            gtt(zq[:, w * s:w * s + w], lst(w, 2 * w), T.ys[:, :], A.mult, w, rd + ["ys"], [Z])
+                            gtt(pq[:, w * s:w * s + w], lst(2 * w, 3 * w), gv(w, 2 * w), A.mult, w, rd + [G + "b"], [P])
+                        else:
+                            gs = [G]
+                            if kd == "F": act(gv(0, 3 * w), lst(0, 3 * w), AF.Copy, 3 * w, rd, [G], r=GC)
+                            else:
+                                act(gv(0, 2 * w), lst(0, 2 * w), AF.Copy, 2 * w, rd, [G], r=GC)
+                                gcp(gv(2 * w, 3 * w), lst(2 * w, 3 * w), w, rd, [G + "a"]); gs = [G, G + "a"]
+                            pyk = "py%d" % (ny[0] % 2); py = T[pyk]; ny[0] += 1
+                            mm([(py[:, :], T.eyes[:, 0, :], gv(0, w), True, False), (py[:, :], T.eye[:, :], gv(2 * w, 3 * w), False, True)], 2 * w,
+                               gs + ["eye", "eyes0"], [pyk])
+                            tt(zq[:, w * s:w * s + w], py[:, :], gv(w, 2 * w), A.mult, w, gs, [pyk, Z], 1.0)
+                            tt(pq[:, w * s:w * s + w], gv(0, w), gv(2 * w, 3 * w), A.mult, w, gs, [P], 1.0)
+                        if s == ds: mm(dlist, 1024 + 3 * nx, nrs + [F, "k18", "eyes1", "eyes2", "eyes3"], [pmk])
+                        if s % 2:
+                            for x in range(4):
+                                mm([(pm[:, 3, 32 * s - 32:32 * s + 32], L(T.zf, p), zq[:, w * (s - 1) + p:w * (s + 1):16], False, False) for p in range(4 * x, 4 * x + 4)],
+                                   1024, ["zf", Z, "zq%d_%d" % (c, s - 1)], [pmk])
+                            mm([(pm[:, 2, 32 * s - 32:32 * s + 32], L(T.zc, p), pq[:, w * (s - 1) + p:w * (s + 1):16], False, False) for p in range(16)],
+                               1024, ["zc", P, "pq%d_%d" % (c, s - 1)], [pmk])
+                        if last:
+                            ts(T.un[:, c, 0, x0:x1], pm[:, 3, x0:x1], BIG, BIG, A.add, A.subtract, nx, [], [pmk, "un0%d" % c])
+                            tt(T.un[:, c, 1, x0:x1], pm[:, 3, x0:x1], T.un[:, c, 0, x0:x1], A.subtract, nx, ["un0%d" % c], [pmk, "un1%d" % c], 1.0)
+                            mm([(pm[:, e, x0:x1], T.eyes[:, 4 + e, :], T.un[:, c, e, x0:x1], False, e == 1) for e in range(2)], 2 * nx,
+                               ["eyes4", "eyes5", "un0%d" % c, "un1%d" % c], [pmk] + lt)
+                        continue
+                    if kd == "W":
+                        act(gv(0, 3 * w), lst(0, 3 * w), AF.Copy, 3 * w, rd, [G], r=GC)
+                        tt(pr(0, 2 * w), gv(0, 2 * w), gv(w, 3 * w), A.mult, 2 * w, [G], [P + "a"], 1.0)
+                        tt(pr(2 * w, 3 * w), gv(0, w), gv(2 * w, 3 * w), A.mult, w, [G], [P + "b"], 1.0)
+                    elif kd == "X":
+                        act(gv(0, 2 * w), lst(0, 2 * w), AF.Copy, 2 * w, rd, [G], r=GC)
+                        tt(pr(0, w), gv(0, w), gv(w, 2 * w), A.mult, w, [G], [P + "a"], 1.0)
+                        gtt(pr(w, 2 * w), lst(2 * w, 3 * w), gv(w, 2 * w), A.mult, w, rd + [G], [P + "b"])
+                        gtt(pr(2 * w, 3 * w), lst(2 * w, 3 * w), gv(0, w), A.mult, w, rd + [G], [P + "c"])
+                    elif kd == "U":
+                        act(gv(0, 2 * w), lst(0, 2 * w), AF.Copy, 2 * w, rd, [G], r=GC)
+                        gcp(gv(2 * w, 3 * w), lst(2 * w, 3 * w), w, rd, [G + "a"])
+                        tt(pr(0, 2 * w), gv(0, 2 * w), gv(w, 3 * w), A.mult, 2 * w, [G, G + "a"], [P + "a"], 1.0)
+                        tt(pr(2 * w, 3 * w), gv(0, w), gv(2 * w, 3 * w), A.mult, w, [G, G + "a"], [P + "b"], 1.0)
+                    else:
+                        act(gv(0, 2 * w), lst(0, 2 * w), AF.Copy, 2 * w, rd, [G], r=GC)
+                        act(gv(2 * w, 3 * w), lst(2 * w, 3 * w), AF.Copy, w, rd, [G + "a"], r=GC)
+                        tt(pr(0, w), gv(0, w), gv(w, 2 * w), A.mult, w, [G], [P + "a"], 1.0)
+                        tt(pr(w, 2 * w), gv(w, 2 * w), gv(2 * w, 3 * w), A.mult, w, [G, G + "a"], [P + "b"], 1.0)
+                        tt(pr(2 * w, 3 * w), gv(0, w), gv(2 * w, 3 * w), A.mult, w, [G, G + "a"], [P + "c"], 1.0)
+                    if s == ds: mm(dlist, 1024, nrs + [F], [pmk])
+                    end = last and Q in ENDS
+                    if end and kd in "WU": red(0, 2, [P + "a"], False); red(2, 3, [P + "b"], True)
+                    elif end: red(0, 2, [P + "a", P + "b"], False); red(2, 3, [P + "c"], True)
+                    else: red(0, 3, [P + "a", P + "b", P + "c"], last)
+                if t < 2:
+                    if t == 1 or c == 0:
+                        na, fb = (256, T.fi0[:, 0, :]) if t == 0 else (n, fa)
+                        mm([(T.pe[:, k:na:16], T.ee[:, k, :], fb, True, True) for k in range(16)], 1024, ["ee", F], ["pe"])
+                    xa = 16 * h0 if t == 0 else 0
+                    act(T.ae[:, J, 0:H, 0:16], T.pe[:, xa:xa + n], AF.Abs, n, ["aez"], ["pe", "ae%d" % J])
+                HD, EV, FF = "hd%d" % Q, "ev%d" % Q, "ff%d" % Q
+                ts(T.hd[:, I, 0:3, x0:x1], pm[:, 0:3, x0:x1], BIG, BIG + (0.0 if pack else 7.0), A.add, A.is_equal, 3 * nx, [], [pmk, HD])
+                if Q not in EVV:
+                    mm([(T.pf1[:, 128:128 + nx], T.eye[:, :], T.hd[:, I, e, x0:x1], e == 0, e == 2) for e in range(3)], 3 * max(64, nx), ["eye", HD], ["pf1"])
+                    act(T.hd[:, I, 3, x0:x1], T.pf1[:, 128:128 + nx], AF.Relu, nx, [], ["pf1", EV], bias=-2.0)
                 else:
-                    act(gv(0, 2 * w), lst(0, 2 * w), AF.Copy, 2 * w, rd, [G], r=GC)
-                    act(gv(2 * w, 3 * w), lst(2 * w, 3 * w), AF.Copy, w, rd, [G + "a"], r=GC)
-                    tt(pr(0, w), gv(0, w), gv(w, 2 * w), A.mult, w, [G], [P + "a"], 1.0)
-                    tt(pr(w, 2 * w), gv(w, 2 * w), gv(2 * w, 3 * w), A.mult, w, [G, G + "a"], [P + "b"], 1.0)
-                    tt(pr(2 * w, 3 * w), gv(0, w), gv(2 * w, 3 * w), A.mult, w, [G, G + "a"], [P + "c"], 1.0)
-                if s == max(0, nsb - 2): mm(dlist, 1024, nrs + [F], [pmk])
-                if last and kd in "WU": red(0, 2, [P + "a"], False); red(2, 3, [P + "b"], True)
-                elif last: red(0, 2, [P + "a", P + "b"], False); red(2, 3, [P + "c"], True)
-                else: red(0, 3, [P + "a", P + "b", P + "c"], False)
-            J = I
-            if t < 2:
-                mm([(T.pe[:, k:n:16], T.ee[:, k, :], fa, True, True) for k in range(16)], 1024, ["ee", F], ["pe"])
-                act(T.ae[:, J, 0:H, 0:16], T.pe[:, 0:n], AF.Abs, n, ["aez"], ["pe", "ae%d" % J])
-                nq = NQ[t]
-                if t == 0:
-                    cand = T.cand1[:, c, :]
-                    act(cand, T.ww[:, :].indirect(T.o1[:, c, :]), AF.Copy, 416, ["wwc", "wwv", "wwz", "o1%d" % c], ["cand%d" % J], r=GC)
-                else:
-                    cand = T.cand2[:, c, :]
-                    act(cand, T.si[:, c, :].indirect(T.ol[:, 0:12]), AF.Copy, 192, ["si%d" % c, "ol"], ["cand%d" % J], r=GC)
-            ts(T.hd[:, I, 0:3, 0:n], pm[:, 0:3, 0:n], BIG, BIG, A.add, A.is_equal, 3 * n, [], [pmk, "hd%d" % I])
-            if I < EVS:
-                mm([(T.pf1[:, 128:128 + n], T.eye[:, :], T.hd[:, I, e, 0:n], e == 0, e == 2) for e in range(3)], 3 * n, ["eye", "hd%d" % I], ["pf1"])
-                act(T.hd[:, I, 3, 0:n], T.pf1[:, 128:128 + n], AF.Relu, n, [], ["pf1", "ev%d" % I], bias=-8192.0, scale=4096.0)
-            else:
-                tt(T.h2[:, I, 0:n], T.hd[:, I, 0, 0:n], T.hd[:, I, 1, 0:n], A.mult, n, ["hd%d" % I], ["h2%d" % I], 1.0)
-                tt(T.hd[:, I, 3, 0:n], T.h2[:, I, 0:n], T.hd[:, I, 2, 0:n], A.mult, n, ["hd%d" % I, "h2%d" % I], ["ev%d" % I], 1.0)
-            if t < 2:
-                mm([(T.pc[:, 32:36, :], T.eye[:, :], T.tie[:, :, :], True, False)] +
-                   [(T.pc[:, 32:36, 0:H], L(T.zz, k), T.hd[:, I, :, k:n:16], False, k == 15) for k in range(16)], 1088,
-                   ["eye", "tie0", "tie1", "tie2", "zz", "hd%d" % I, "ev%d" % I], ["pc"])
-            mm([(T.pf1[:, 0:n], T.imt[:, :], T.hd[:, I, 3, 0:n], True, True)], n, ["imt", "ev%d" % I], ["pf1"])
-            act(T.ff[:, I, 0:n], T.pf1[:, 0:n], AF.Relu, n, [], ["pf1", "ff%d" % I], scale=1.0 if I < EVS else 4096.0)
-            if t < 2:
-                if SCS: act(T.sc[:, J, :], T.pc[:, 32:36, :], AF.Identity, 32, [], ["pc", "sc%d" % J])
-                else: cp(T.sc[:, J, :], T.pc[:, 32:36, :], 32, [], ["pc", "sc%d" % J])
-                tt(T.m1[:, J, :], T.sc[:, J, 0:16], T.sc[:, J, 16:32], A.max, 16, ["sc%d" % J], ["m1%d" % J])
-                tt(T.m2[:, J, :], T.m1[:, J, 0:8], T.m1[:, J, 8:16], A.max, 8, ["m1%d" % J], ["m2%d" % J])
-                gtt(T.mk[:, J, :], T.m2[:, J, :].indirect(T.ol[:, 50:52]), T.sc[:, J, :], A.is_equal, 32, ["m2%d" % J, "sc%d" % J, "ol"], ["mk%d" % J])
-                rep = T.ol[:, 12:38] if t == 0 else T.ol[:, 38:50]
-                gtt(T.msk[:, J, 0:32 * nq], T.mk[:, J, :].indirect(rep), cand, A.mult, 32 * nq, ["mk%d" % J, "cand%d" % J, "ol"], ["msk%d" % J])
-                m = 8 * nq + 3 * H
-                mm([(T.ps[:, 0:m // 2, :], T.eye[:, :], T.k18[:, 0, 0:m], True, False)], m, ["eye", "k18"], ["ps"])
-                mm([(T.ps[:, 4 * nq + x:4 * nq + 3 * nsb:3, :], T.eye[:, :], T.msk[:, J, 8 * (nq * q + x):8 * (nq * q + x) + H], False, False)
-                    for q in range(4) for x in range(3)] +
-                   [(T.ps[:, 0:4 * nq, :], T.eye[:, :], T.msk[:, J, 8 * nq * q:8 * nq * (q + 1)], False, q == 3) for q in range(4)],
-                   768 + 4 * max(64, 8 * nq), ["eye", "msk%d" % J], ["ps"])
-                cp(T.uo[:, J, 0:m], T.ps[:, 0:m // 2, :], m, [], ["ps", "uo%d" % J])
-                add("G", 300, ["uo%d" % J], ["ui%d" % J], lambda g, J=J, m=m: g.remote_dma(
-                    T.ui[:, J, 0:m], T.uo[:, J, 0:m], T.sem["r%d" % J], T.sem.sent, pid, rid, mask), "r%d" % J)
-                mm([(T.pl[:, 0:18 * H], T.eye[:, :], T.c1[:, 0:H, :], True, False), (T.pl[:, 0:18 * H], T.neye[:, :], T.ae[:, J, 0:H, :], False, False),
-                    (T.pl[:, 16:18 * H:18], T.eye[:, :], fa, False, False)], 36 * H + 64, ["eye", "neye", "c1", F, "ae%d" % J], ["pl"])
-                mm([(T.pl[:, 18 * h:18 * h + 16], T.hblk[:, :], T.ff[:, I, 16 * h:16 * h + 16], False, False) for h in range(H)] +
-                   [(T.pl[:, 17:18 * H:18], T.neye[:, :], T.mk[:, J, 24:24 + H], False, True)], 64 * H + 64,
-                   ["neye", "hblk", "ff%d" % I, "mk%d" % J], ["pl"])
-                add("V", vns(18 * H), ["rs"], ["pl", "ls%d" % J], lambda g, J=J, H=H: g.vector.tensor_tensor_scan(
-                    T.ls[:, J, 0:18 * H], T.rs[:, 0:18 * H], T.pl[:, 0:18 * H], 0.0, A.mult, A.max))
-                cp(T.su[:, J, 0:H], T.ls[:, J, 17:18 * H:18], H, ["ls%d" % J], ["su%d" % J])
-                gtt(T.sv[:, J, 0:n], win.indirect(ua), T.ff[:, I, 0:n], A.max, n, tks + [UA, "ff%d" % I], ["sv%d" % J])
-                gcp(tsb[:, 0:1936].indirect(T.su[:, J, 0:H]), T.sv[:, J, 0:n], n, ["su%d" % J, "sv%d" % J], tks, SC)
-            Y = "yy%d" % I
-            for m in range(3):
-                tt(T.yy[:, I, m, 0:n], T.nf[:, I, 0:nsb, (m + 2) % 3, :], T.ff[:, I, 0:n], A.mult, n, ["nf%d" % I, "ff%d" % I], [Y + str(m)], 1.0)
-            ml = []
-            for h in range(H):
-                for x in range(2): ml.append((T.po[0:24, :, h], T.of[:, x, :], T.ff[:, I, 16 * h:16 * h + 16], x == 0, False))
+                    tt(T.h2[:, I, x0:x1], T.hd[:, I, 0, x0:x1], T.hd[:, I, 1, x0:x1], A.mult, nx, [HD], ["h2%d" % Q], 1.0)
+                    tt(T.hd[:, I, 3, x0:x1], T.h2[:, I, x0:x1], T.hd[:, I, 2, x0:x1], A.mult, nx, [HD, "h2%d" % Q], [EV], 1.0)
+                if t < 2:
+                    mm([(pc, T.eye[:, :], T.tie[:, :, :], True, False)] +
+                       [(pc, L(T.zz, k), T.hd[:, I, :, k:n:16], False, k == 15) for k in range(16)], 1088,
+                       ["eye", "tie0", "tie1", "zz", HD, EV], [pck])
+                    tt(T.sc[:, J, :], pc, T.wt[:, :], A.mult, 32, ["wt"], [pck, "sc%d" % J], 1.0)
+                mm([(T.pf1[:, 0:nx], T.imt[:, :], T.hd[:, I, 3, x0:x1], True, True)], max(64, nx), ["imt", EV], ["pf1"])
+                ff = T.ff[:, I, x0:x1]
+                if Q in FFV: ts(ff, T.pf1[:, 0:nx], 0.0, K, A.max, A.mult, nx, [], ["pf1", FF])
+                else: act(ff, T.pf1[:, 0:nx], AF.Relu, nx, [], ["pf1", FF], scale=K)
+                if t < 2:
+                    tt(T.m1[:, J, :], T.sc[:, J, 0:16], T.sc[:, J, 16:32], A.max, 16, ["sc%d" % J], ["m1%d" % J])
+                    tt(T.m2[:, J, :], T.m1[:, J, 0:8], T.m1[:, J, 8:16], A.max, 8, ["m1%d" % J], ["m2%d" % J])
+                    gtt(T.mk[:, J, :], T.m2[:, J, :].indirect(T.ol[:, 52:54]), T.sc[:, J, :], A.is_equal, 32, ["m2%d" % J, "sc%d" % J, "ol"], ["mk%d" % J])
+                    send(T.mi[:, J, :], T.mk[:, J, :], ["mk%d" % J], "mi%d" % J)
+                    mm([(pl[:, 0:18 * H], T.eye[:, :], T.c1[:, 0:H, :], True, False), (pl[:, 0:18 * H], T.neye[:, :], T.ae[:, J, 0:H, :], False, False),
+                        (pl[:, 16:18 * H:18], T.eye[:, :], fa, False, False)], 36 * H + 64, ["eye", "neye", "c1", F, "ae%d" % J], [plk])
+                    mm([(pl[:, 18 * h:18 * h + 16], T.blk[:, :], T.ff[:, I, 16 * h:16 * h + 16], False, False) for h in range(H)] +
+                       [(pl[:, 17:18 * H:18], T.neye[:, :], T.mk[:, J, 24:24 + H], False, True)], 64 * H + 64,
+                       ["neye", "blk", FF, "mk%d" % J], [plk])
+                    add("V", vns(18 * H), ["rs"], [plk, "ls%d" % J], lambda g, J=J, H=H: g.vector.tensor_tensor_scan(
+                        T.ls[:, J, 0:18 * H], T.rs[:, 0:18 * H], pl[:, 0:18 * H], 0.0, A.mult, A.max))
+                    cp(T.su[:, J, 0:H], T.ls[:, J, 17:18 * H:18], H, ["ls%d" % J], ["su%d" % J])
+                    gtt(T.sv[:, J, 0:n], win.indirect(ua), ff, A.max, n, tks + [UA, FF], ["sv%d" % J])
+                    gcp(tsb[:, :].indirect(T.su[:, J, 0:H]), T.sv[:, J, 0:n], n, ["su%d" % J, "sv%d" % J], tks, SC)
+                Y = "yy%d" % Q
                 for m in range(3):
-                    ml.append((T.po[0:24, :, h], T.zo[:, 2 - m:26 - m], T.yy[:, I, m, 16 * h:16 * h + 16], False, m == 2))
-            mm(ml, H * 24 * 5, ["of0", "of1", "zo", "ff%d" % I, Y + "0", Y + "1", Y + "2"], ["po"])
-            act(T.yb[0:24, t, :, h0:h0 + H], T.po[0:24, :, 0:H], AF.Identity, n, [], ["po", "yb%d" % I], bias=-1.0)
-        dma(T.yn[:, 768 * t:768 * (t + 1)], T.yb[0:24, t], 24 * 1024, ["yb%d" % (t * NC + c) for c in range(NC)], ["yn%d" % t])
+                    tt(T.yy[:, I, m, x0:x1], T.nf[:, I, s0:s1, (m + 2) % 3, :], ff, A.mult, nx, ["nf%d" % I, FF], [Y + str(m)], 1.0)
+                ml = []
+                for h in range(2 * s0, 2 * s1):
+                    for x in range(2): ml.append((T.po[0:24, :, h], T.of[:, x, :], T.ff[:, I, 16 * h:16 * h + 16], x == 0, False))
+                    for m in range(3):
+                        ml.append((T.po[0:24, :, h], T.zo[:, 2 - m:26 - m], T.yy[:, I, m, 16 * h:16 * h + 16], False, m == 2))
+                mm(ml, npart * 240, ["of0", "of1", "zo", FF, Y + "0", Y + "1", Y + "2"], ["po"])
+                act(T.yb[0:24, t, :, h0 + 2 * s0:h0 + 2 * s1], T.po[0:24, :, 2 * s0:2 * s1], AF.Identity, nx, [], ["po", "yb%d" % Q], bias=-1.0)
+                ybs.append("yb%d" % Q); Q += 1; s0 = s1
+        dma(T.yn[:, 768 * t:768 * (t + 1)], T.yb[0:24, t], 24 * 1024, ybs, ["yn%d" % t])
     return ops
 
 
-def plan(ops, alt=(), dma0=1500.0, tries=TRIES):
+def plan(ops, alt=(), dma0=1500.0, tries=TRIES, moves=MOVES):
     lw, lr = {}, {}
     for i, o in enumerate(ops):
         d = set()
@@ -361,7 +430,8 @@ def plan(ops, alt=(), dma0=1500.0, tries=TRIES):
     if tries < 0: return None
     hop, wire = FIGS[0][3:]
     n = len(ops); en = [o["e"] for o in ops]; ns = [o["ns"] for o in ops]
-    lat = [dma0 if o["kind"] == "dma" else wire if o["kind"] else 0.0 for o in ops]
+    def lats(w): return [dma0 if o["kind"] == "dma" else w + 4000.0 * (o["kind"] == "rwi") if o["kind"] else 0.0 for o in ops]
+    lat = lats(wire)
     pre = [[(j, lat[j] + (0.0 if en[j] == "P" == en[i] else hop)) for j in ops[i]["dep"]] for i in range(n)]
     ys = [i for i in range(n) if en[i] == "Y"]
     for a, b in zip(ys, ys[1:]): pre[b].append((a, 0.0))
@@ -409,8 +479,9 @@ def plan(ops, alt=(), dma0=1500.0, tries=TRIES):
 
     others = []
     for ns2, h2, w2 in alt:
-        lat2 = [dma0 if o["kind"] == "dma" else w2 if o["kind"] else 0.0 for o in ops]
+        lat2 = lats(w2)
         others.append((ns2, [[(j, lat2[j] + (0.0 if en[j] == "P" == en[i] else h2)) for j in ops[i]["dep"]] for i in range(n)], lat2))
+        for a, b in zip(ys, ys[1:]): others[-1][1][b].append((a, 0.0))
     rnd = np.random.RandomState(1)
     best, (end, each) = both(list(range(n)))
     now, cur = best, end
@@ -420,9 +491,51 @@ def plan(ops, alt=(), dma0=1500.0, tries=TRIES):
         t, e2 = both(topo_sort([cur[i] - ns[i] + (jit[i] if a <= cur[i] <= b else 0.0) for i in range(n)]))
         if t <= now + 400.0 * (1.0 - it / tries) * rnd.uniform(): now, cur = t, e2[0]
         if t <= best: best, (end, each) = t, e2
-    order = {e: sorted((i for i in range(n) if en[i] == e), key=lambda i: end[i]) for e in "VSPGY"}
-    for i in range(n): ops[i]["t0"] = end[i] - ns[i]
-    return order, each
+    figs = [(ns, pre, lat)] + others
+    qn = ["VSPGY".index(e) for e in en]
+    def run(seq, f):
+        ns2, pre2, lat2 = figs[f]; free = [0.0] * 5; who = [-1] * 5; e2 = [0.0] * n; by = [-1] * n
+        for i in seq:
+            q = qn[i]; t = free[q]; b = who[q]
+            for j, l in pre2[i]:
+                if e2[j] + l > t: t = e2[j] + l; b = j
+            e2[i] = free[q] = t + ns2[i]; who[q] = i; by[i] = b
+        last = max(ys, key=lambda i: e2[i])
+        return e2[last] + lat2[last], e2, by, last
+    seq = sorted(range(n), key=lambda i: end[i] - ns[i] * 0.999)
+    res = [run(seq, f) for f in range(len(figs))]; base = [r[0] for r in res]
+    def score(rs): return sum(r[0] / b for r, b in zip(rs, base))
+    now = best = score(res); keep = seq, res
+    deps = [set(j for j, l in pre[i]) for i in range(n)]
+    for it in range(moves):
+        r = res[rnd.randint(len(figs))]; path = []; i = r[3]
+        while i >= 0:
+            j = r[2][i]
+            if j >= 0 and j not in deps[i] and qn[i] != 4: path.append((j, i))
+            i = j
+        if not path: break
+        j, i = path[rnd.randint(len(path))]
+        a, b = seq.index(j), seq.index(i)
+        if rnd.randint(2):
+            a = max(0, a - (rnd.randint(12) if rnd.randint(2) else 0)); need = {i}; mv = []
+            for x in reversed(seq[a:b + 1]):
+                if x in need: mv.append(x); need |= deps[x]
+            if j in mv: continue
+            s2 = seq[:a] + mv[::-1] + [x for x in seq[a:b + 1] if x not in need] + seq[b + 1:]
+        else:
+            b = min(n - 1, b + (rnd.randint(12) if rnd.randint(2) else 0)); mv = {j}
+            for x in seq[a + 1:b + 1]:
+                if deps[x] & mv: mv.add(x)
+            if i in mv: continue
+            s2 = seq[:a] + [x for x in seq[a:b + 1] if x not in mv] + [x for x in seq[a:b + 1] if x in mv] + seq[b + 1:]
+        r2 = [run(s2, f) for f in range(len(figs))]; t = score(r2)
+        if t <= now + 0.004 * (1.0 - it / moves) * rnd.uniform():
+            now, seq, res = t, s2, r2
+            if t < best: best, keep = t, (s2, r2)
+    seq, res = keep
+    order = {e: [i for i in seq if en[i] == e] for e in "VSPGY"}
+    for i in range(n): ops[i]["t0"] = res[0][1][i] - ns[i]
+    return order, [r[0] for r in res]
 
 
 ORDER = {}

@@ -1,18 +1,23 @@
 import numpy as np
 from concourse.mybir import AluOpType as A, ActivationFunctionType as AF
 
-SPLIT = ["UWWW WWWW", "XWWW XWWW", "XWWW WWWN"]
+SPLIT = ["UWWW WUWW", "UWWW UWWW", "UWUW UWW|N"]
 FINE = 1
-EVV = (5,)
+EVV = (5, 6)
 FFV = ()
 NM1 = 1
-ENDS = (0, 1, 2, 3, 5)
-PACK = any(k in "".join(SPLIT) for k in "FGA")
-K = 4096.0
+ENDS = (0, 1, 2, 3, 6)
 FIGS = [(1.56, 3.8, 0.42, 70.0, 1600.0), (1.1, 2.0, 0.42, 60.0, 1500.0), (2.0, 5.5, 0.42, 60.0, 1500.0), (1.3, 3.8, 0.45, 120.0, 2600.0)]
 RATE = 500.0
-TRIES = 100
-MOVES = 100000
+MMO = 8.0
+VF = 30.0
+FIS = 0
+TWO = ()
+FAR = 3000.0
+YS = ()
+HEAT = 0.012
+TRIES = 60
+MOVES = 90000
 SB = [[c.replace("|", "") for c in r.split()] for r in SPLIT]
 CUT = [[[len(x) for x in c.split("|")] for c in r.split()] for r in SPLIT]
 NC = len(SB[0])
@@ -32,35 +37,35 @@ def _val(x, y): return 15 + _col(x, y)
 
 
 def _cand1():
-    out = []
+    cols, rest = [], []
     for o, a, b, c in [(0, 4, 2, 3), (0, 1, 4, 3), (0, 1, 2, 4), (1, 2, 3, 4)]:
-        out += [_col(o, b), _col(o, c), _col(o, a), _val(b, c), _val(a, c), _val(a, b), _col(o, 5), _col(a, b), _col(a, c),
-                _col(a, 5), _val(a, 5), _val(b, 5), _val(c, 5), 27]
-    return out
+        cols += [_col(o, b), _col(o, c), _col(o, a)]
+        rest += [_val(b, c), _val(a, c), _val(a, b), _col(o, 5), _col(a, b), _col(a, c), _col(a, 5), _val(a, 5), _val(b, 5), _val(c, 5)]
+    return cols + rest
 
 
 CAND1 = _cand1()
-CAND2 = [0, 1, 6, 3, 12, 11, 6, 1, 2, 12, 4, 10, 0, 6, 2, 11, 10, 5, 8, 9, 7, 12, 11, 3]
-NQ = (14, 6)
-NR = (13, 6)
+CAND2 = [0, 1, 6, 6, 1, 2, 0, 6, 2, 8, 9, 7] + [3, 12, 11, 12, 4, 10, 11, 10, 5, 12, 11, 3]
+NQ = (10, 3)
 
 SCRATCH = {
     "cv": ("sbuf", [128, 4112], "bfloat16"), "ob": ("sbuf", [128, 1536], "bfloat16"), "gp": ("sbuf", [128, 12, 256], "bfloat16"),
     "gp0": ("sbuf", [128, 16, 8, 3, 2], "bfloat16"), "pi": ("sbuf", [128, 8], "int32"), "pf": ("sbuf", [128, 8], "float32"),
     "ia": ("sbuf", [128, 144], "float32"), "ib": ("sbuf", [128, 128], "float32"), "ik": ("sbuf", [128, 8, 18], "float32"),
     "ic": ("sbuf", [128, 8, 18], "float32"), "id3": ("sbuf", [128, 24], "float32"),
-    "tm": ("sbuf", [128, 8, 18], "float32"), "one": ("sbuf", [128, 128], "float32"), "cb0": ("sbuf", [128, 8, 3, 2], "float32"),
+    "one": ("sbuf", [128, 128], "float32"), "cb0": ("sbuf", [128, 8, 3, 2], "float32"),
     "blk": ("sbuf", [128, 128], "bfloat16"), "nblk": ("sbuf", [128, 128], "bfloat16"), "eye": ("sbuf", [128, 128], "bfloat16"),
     "neye": ("sbuf", [128, 128], "bfloat16"), "imt": ("sbuf", [128, 128], "bfloat16"),
     "t2": ("sbuf", [128, 128], "bfloat16"), "zz": ("sbuf", [128, 144], "bfloat16"), "zc": ("sbuf", [128, 144], "bfloat16"),
-    "zs": ("sbuf", [128, 144], "bfloat16"), "zo": ("sbuf", [128, 32], "bfloat16"), "of": ("sbuf", [128, 2, 24], "bfloat16"),
+    "zs": ("sbuf", [128, 144], "bfloat16"), "zo": ("sbuf", [128, 32], "bfloat16"), "zp": ("sbuf", [128, 32], "float32"),
+    "of": ("sbuf", [128, 2, 24], "bfloat16"), "yz": ("sbuf", [128, 3, 128], "float32"), "icf": ("sbuf", [128, 8, 18], "float16"),
     "sk": ("sbuf", [128, 16], "float32"), "nr": ("sbuf", [128, 16, 128], "bfloat16"), "ee": ("sbuf", [128, 16, 128], "bfloat16"),
     "c1": ("sbuf", [128, 8, 18], "float16"), "rs": ("sbuf", [128, 144], "float32"), "tie": ("sbuf", [128, 4, 8], "bfloat16"),
     "cb": ("sbuf", [128, 15, 16], "float32"), "wt": ("sbuf", [128, 32], "float32"),
-    "ww": ("sbuf", [128, 432], "float32"), "wi": ("sbuf", [128, 464], "float32"), "tab": ("sbuf", [128, 124], "float32"), "tb2": ("sbuf", [128, 40], "float32"),
-    "tb3": ("sbuf", [128, 40], "float32"), "o1": ("sbuf", [128, NC, 28], "uint16"), "ol": ("sbuf", [128, 56], "uint16"),
+    "ww": ("sbuf", [128, 432], "float32"), "wi": ("sbuf", [128, 464], "float32"), "tab": ("sbuf", [128, 46], "float32"), "tb2": ("sbuf", [128, 46], "int32"),
+    "tb3": ("sbuf", [128, 46], "int32"), "ol": ("sbuf", [128, 46], "uint16"),
     "ui0": ("sbuf", [128, 48], "uint16"), "ua0": ("sbuf", [128, 16], "uint16"), "fi0": ("sbuf", [128, 4, 16], "float16"),
-    "cand1": ("sbuf", [128, NC, 448], "float32"), "cand2": ("sbuf", [128, NC, 192], "float32"),
+    "cand1": ("sbuf", [128, NC, 416], "float32"), "cand2": ("sbuf", [128, NC, 192], "float32"),
     "msk": ("sbuf", [128, 2 * NC, 448], "float16"), "sc": ("sbuf", [128, 2 * NC, 32], "float32"),
     "m1": ("sbuf", [128, 2 * NC, 16], "float32"), "m2": ("sbuf", [128, 2 * NC, 8], "float32"), "mk": ("sbuf", [128, 2 * NC, 32], "bfloat16"),
     "mi": ("sbuf", [128, 2 * NC, 32], "bfloat16"), "ui": ("sbuf", [128, 2 * NC, 48], "uint16"), "so": ("sbuf", [128, NC, 104], "float32"),
@@ -70,15 +75,12 @@ SCRATCH = {
     "ff": ("sbuf", [128, 3 * NC, 128], "bfloat16"), "ae": ("sbuf", [128, 2 * NC, 8, 18], "bfloat16"),
     "yy": ("sbuf", [128, 3 * NC, 3, 128], "float16"), "sv": ("sbuf", [128, 2 * NC, 128], "int32"), "ls": ("sbuf", [128, 2 * NC, 144], "float32"),
     "su": ("sbuf", [128, 2 * NC, 8], "uint16"), "yb": ("sbuf", [128, 3, 16, 16], "float32"),
-    "k18": ("sbuf", [128, 128], "float16"), "eyes": ("sbuf", [128, 6, 128], "bfloat16"), "zf": ("sbuf", [128, 144], "float32"),
-    "zer": ("sbuf", [128, 3, 128], "bfloat16"), "un": ("sbuf", [128, NC, 2, 128], "float16"), "ys": ("sbuf", [128, 512], "float32"),
+    "zer": ("sbuf", [128, 3, 128], "bfloat16"),
     "pm0": ("psum", [128, 4, 128], "float32"), "pm1": ("psum", [128, 4, 128], "float32"), "pe": ("psum", [128, 512], "float32"),
-    "pf1": ("psum", [128, 512], "float32"), "py0": ("psum", [128, 512], "float32"), "py1": ("psum", [128, 512], "float32"),
+    "pf1": ("psum", [128, 512], "float32"), "py0": ("psum", [128, 4, 16, 8], "float32"), "py1": ("psum", [128, 512], "float32"),
     "ps": ("psum", [128, 256, 2], "float32"), "po": ("psum", [128, 16, 32], "float32"),
 }
 for _c in range(NC):
-    SCRATCH["zq%d" % _c] = ("sbuf", [128, 256 * HS[_c]], "float32")
-    SCRATCH["pq%d" % _c] = ("sbuf", [128, 256 * HS[_c]], "bfloat16")
     SCRATCH["ts%d" % _c] = ("sbuf", [128, WIN], "int32")
     for _t in range(2):
         SCRATCH["gv%d_%d" % (_t, _c)] = ("sbuf", [128, 768 * HS[_c]], "bfloat16")
@@ -107,7 +109,7 @@ def build(T, nxt, topo, core, fig=FIGS[0]):
     GC, SC, PC = fig[:3]
 
     def add(e, ns, rd, wr, fn, kind=None): ops.append(dict(e=e, ns=ns, rd=rd, wr=wr, fn=fn, kind=kind))
-    def vns(n, r=1.0): return 30 + 0.83 * max(64, n * r)
+    def vns(n, r=1.0): return VF + 0.83 * max(64, n * r)
     def ts(out, in0, s1, s2, op0, op1, n, rd, wr, r=1.0):
         if op1 is None: add("V", vns(n, r), rd, wr, lambda g: g.vector.tensor_scalar(out, in0, s1, None, op0))
         else: add("V", vns(n, r), rd, wr, lambda g: g.vector.tensor_scalar(out, in0, s1, s2, op0, op1))
@@ -127,8 +129,9 @@ def build(T, nxt, topo, core, fig=FIGS[0]):
         def fn(g):
             for m in lst: r = g.tensor.matmul(*m)
             return r
-        add("P", 40 + PC * cyc + 8 * len(lst), rd, wr, fn)
-    def dma(out, in_, nbytes, rd, wr): add("Y", nbytes / RATE, rd, wr, lambda g: g.sync.dma_start(out, in_), "dma")
+        add("P", 40 + PC * cyc + MMO * len(lst), rd, wr, fn)
+    def dma(out, in_, nbytes, rd, wr):
+        add("Y", nbytes / RATE, rd, wr, lambda g: g.sync.dma_start(out, in_), "dma"); ops[-1]["io"] = (out, in_)
 
     dma(T.ob[:, 0:1024], T.obs[:, 0:1024], 128 * 2048, [], ["ob0"])
     part = [[2] * len(SB[0][c]) if c < FINE else [HS[c]] for c in range(NC)]
@@ -161,56 +164,48 @@ def build(T, nxt, topo, core, fig=FIGS[0]):
         iota(T.cb[0:1, :, H0[c]:H0[c] + HS[c]], [[0, 15], [32 * 226, HS[c]]], -15 - 32 * int(OFF), 0, 15 * HS[c], ["cb%d" % c])
     cbs = ["cb%d" % c for c in range(NC)]
     iota(T.ib[:, :], [[1, 8], [0, 16]], 0, 0, 128, ["ib"])
-    iota(T.id3[:, :], [[1, 8], [0, 3]], 0, 0, 24, ["id3"])
     ts(T.blk[:, :], T.ib[:, :], T.pf[:, 4:5], None, A.is_equal, None, 128, ["ib", "pf"], ["blk"])
     select(T.eye[:, :], T.blk[:, :], [[-1, 128]], A.is_equal, 0.0, 0, 1, 128, ["blk"], ["eye"])
     act(T.neye[:, :], T.eye[:, :], AF.Identity, 128, ["eye"], ["neye"], scale=-2097152.0)
-    act(T.nblk[:, :], T.blk[:, :], AF.Identity, 128, ["blk"], ["nblk"], scale=-1.0)
+    act(T.nblk[:, :], T.blk[:, :], AF.Identity, 128, ["blk"], ["nblk"], scale=-8192.0)
     select(T.t2[:, :], T.nblk[:, :], [[1, 128]], A.is_gt, 0.0, 0, -1, 128, ["nblk"], ["t2"])
-    select(T.imt[:, :], T.t2[:, :], [[-1, 128]], A.not_equal, 1.0, 0, 1, 128, ["t2"], ["imt"])
+    select(T.imt[:, :], T.t2[:, :], [[-1, 128]], A.not_equal, 8192.0, 0, 1, 128, ["t2"], ["imt"])
     ts(T.zo[:, :], T.ia[:, 0:32], T.pf[:, 6:7], None, A.is_equal, None, 32, ["ia", "pf6"], ["zo"])
-    ts(T.of[:, 0, :], T.id3[:, :], T.pf[:, 4:5], 0.5, A.is_equal, A.mult, 24, ["id3", "pf"], ["of0"])
-    act(T.of[:, 1, :], T.of[:, 0, :], AF.Identity, 24, ["of0"], ["of1"], scale=1.0 / 2048)
-    iota(T.zer[:, :, :], [[0, 384]], 0, 0, 384, ["zer"])
-    if PACK:
-        for i, x in enumerate((K, -1.0, -1.0 / K, -CW, CW, CW * K)):
-            act(T.eyes[:, i, :], T.eye[:, :], AF.Identity, 128, ["eye"], ["eyes%d" % i], scale=x)
-        act(T.zf[:, :], T.zs[:, :], AF.Identity, 144, ["zs"], ["zf"], scale=16.0 / K)
-        ts(T.k18[:, :], T.ia[:, 0:128], 0.0, OFF, A.mult, A.add, 128, ["ia"], ["k18"])
+    ms(T.zer[:, :, :], 0.0, 384, ["zer"])
+    if YS: act(T.zp[:, :], T.zo[:, :], AF.Identity, 32, ["zo"], ["zp"])
+    iota(T.id3[:, :], [[1, 8], [0, 3]], 0, 0, 24, ["id3"])
+    ts(T.of[:, 0], T.id3[:, :], T.pf[:, 4:5], 0.5, A.is_equal, A.mult, 24, ["id3", "pf"], ["of0"])
+    act(T.of[:, 1], T.of[:, 0], AF.Identity, 24, ["of0"], ["of1"], scale=1.0 / 2048)
     ts(T.sk[:, :], T.ia[:, 0:16], T.pf[:, 1:2], -CW, A.is_equal, A.mult, 16, ["ia", "pf"], ["sk"])
     for k in range(16):
         act(T.nr[:, k, :], T.blk[:, :], AF.Identity, 128, ["blk", "sk"], ["nr%d" % k], scale=T.sk[:, k:k + 1])
     nrs = ["nr%d" % k for k in range(16)]
-    select(T.ee[:, :, :], T.nr[:, :, :], [[0, 16], [-1, 128]], A.not_equal, CW, 0, 1, 2048, nrs, ["ee"])
+    ees = ["ee"]
+    select(T.ee[:, :, :], T.nr[:, :, :], [[0, 16], [-1, 128]], A.not_equal, CW, 0, 1, 2048, nrs, ees)
     iota(T.ik[:, :, 0:16], [[0, 8], [1, 16]], 0, 0, 128, ["ik0"]); iota(T.ik[:, :, 16:18], [[0, 16]], -1, 0, 16, ["ik1"])
     iota(T.ic[:, :, 0:16], [[2, 8], [0, 16]], DUM - 4096, 16, 128, ["ic0"]); iota(T.ic[:, :, 16], [[0, 8]], int(OFF), 0, 8, ["ic1"])
     iota(T.ic[:, :, 17], [[2, 8]], DUM, 16, 8, ["ic2"])
-    ts(T.tm[:, :, :], T.ik[:, :, :], T.pf[:, 1:2], -30000.0, A.is_ge, A.mult, 144, ["ik0", "ik1", "pf"], ["tm"])
-    tt(T.c1[:, :, :], T.tm[:, :, :], T.ic[:, :, :], A.add, 144, ["tm", "ic0", "ic1", "ic2"], ["c1"])
-    iota(T.rs[:, :], [[0, 144]], 1, 0, 144, ["rs"]); iota(T.rs[:, 0:144:18], [[0, 8]], 0, 0, 8, ["rs"])
-    iota(T.ae[:, :, :, 16:18], [[0, 32 * NC]], 0, 0, 32 * NC, ["aez"])
+    ts(T.c1[:, :, :], T.ik[:, :, :], T.pf[:, 1:2], -30000.0, A.is_ge, A.mult, 144, ["ik0", "ik1", "pf"], ["tm"])
+    act(T.icf[:, :, :], T.ic[:, :, :], AF.Identity, 144, ["ic0", "ic1", "ic2"], ["c1"])
+    ms(T.rs[:, :], 1.0, 144, ["rs"]); ms(T.rs[:, 0:144:18], 0.0, 8, ["rs"])
+    ms(T.ae[:, :, :, 16:18], 0.0, 32 * NC, ["aez"])
     iota(T.cv[:, 4096:4112], [[0, 16]], 0, 0, 16, ["cvz"])
-    iota(T.wi[:, 432:464], [[0, 32]], 0, 0, 32, ["wiz"])
     iota(T.tie[:, 0:3, :], [[-1, 3], [0, 8]], 2, 0, 24, ["tie0"]); iota(T.tie[:, 3, :], [[0, 8]], 0, 0, 8, ["tie1"])
-    iota(T.wt[:, 0:24], [[0, 24]], 1, 0, 24, ["wt"]); iota(T.wt[:, 24:32], [[0, 8]], 64, 0, 8, ["wt"])
-    rows = [16 * x for x in CAND1] + [8 * x for x in CAND2]
+    iota(T.wt[:, 0:16], [[0, 16]], 1, 0, 16, ["wu"]); iota(T.wt[:, 16:32], [[63, 2], [0, 8]], 1, 0, 16, ["wt"])
+    rows = [16 * x for x in CAND1] + [8 * x for x in CAND2] + [0] * 4 + [8 * (i // 3) for i in range(12)]
     tabs = []
-    for i, n, b, st in runs(rows[0::2] + [y - x for x, y in zip(rows[0::2], rows[1::2])]):
+    for i, n, b, st in runs([x // 8 + 8 * y for x, y in zip(rows[0::2], rows[1::2])]):
         tabs.append("tab%d" % i); iota(T.tab[:, i:i + n], [[st, n]], b, 0, n, [tabs[-1]])
-    iota(T.tab[:, 80:108], [[8, 4], [0, 7]], 0, 0, 28, ["tr1"]); iota(T.tab[:, 108:120], [[8, 4], [0, 3]], 0, 0, 12, ["tr2"])
-    iota(T.tab[:, 120:124], [[0, 4]], 0, 0, 4, ["tr3"])
-    ts(T.tb2[:, :], T.tab[:, 40:80], T.pf[:, 3:4], T.pf[:, 2:3], A.mult, A.add, 40, tabs + ["pf"], ["tb2"])
-    tt(T.tb3[:, :], T.tb2[:, :], T.tab[:, 0:40], A.add, 40, tabs + ["tb2"], ["tb3"])
-    for c in range(NC):
-        ts(T.o1[:, c, :], T.tb3[:, 0:28], float(H0[c]), None, A.add, None, 28, ["tb3"], ["o1%d" % c])
-    cp(T.ol[:, 0:12], T.tb3[:, 28:40], 12, ["tb3"], ["o2"])
-    ts(T.ol[:, 12:56], T.tab[:, 80:124], T.pf[:, 2:3], None, A.add, None, 44, ["tr1", "tr2", "tr3", "pf"], ["ol"])
+    ts(T.pf[:, 7:8], T.pf[:, 3:4], -63.0 / 64, 1.0, A.mult, A.add, 1, ["pf"], ["pf7"])
+    ts(T.tb2[:, :], T.tab[:, :], T.pf[:, 7:8], -63.0 / 128, A.mult, A.add, 46, tabs + ["pf7"], ["tb2"])
+    ts(T.tb3[:, :], T.tb2[:, :], 63, None, A.bitwise_and, None, 46, ["tb2"], ["tb3"])
+    ts(T.ol[:, :], T.tb3[:, :], 8.0, T.pf[:, 2:3], A.mult, A.add, 46, ["tb3", "pf"], ["ol"])
 
     def star(j, n=1): return T.ob[:, 256 * j:256 * (j + n)]
     for w in range(3):
         tt(T.gp0[:, :, :, w, :], star(0), star(PAIRS[12 + w][1]), A.mult, 256, ["ob0"], ["gq%d" % w], 1.0)
     for i in range(3):
-        tt(T.gp[:, i, :], star(PAIRS[i][0]), star(PAIRS[i][1]), A.mult, 256, ["ob0", "c1", "of0", "zo"], ["gp%d" % i], 1.0)
+        tt(T.gp[:, i, :], star(PAIRS[i][0]), star(PAIRS[i][1]), A.mult, 256, ["ob0", "tm", "zo", "of0", "zer", "pf7", "rs", "aez"], ["gp%d" % i], 1.0)
     for i in (3, 5, 7, 9):
         tt(T.gp[:, i:i + 2, :], star(PAIRS[i][0], 2), star(4, 2), A.mult, 512, ["ob0", "ob1"], ["gp%d" % i], 1.0)
     tt(T.gp[:, 11, :], star(0), star(5), A.mult, 256, ["ob0", "ob1"], ["gp11"], 1.0)
@@ -220,23 +215,22 @@ def build(T, nxt, topo, core, fig=FIGS[0]):
     mm([(T.pf1[:, 0:48], L(T.zs, k), T.gp0[:, k], False, k == 15) for k in range(16)], 1024, gq, ["pf1"])
     ts(T.ui0[:, :], T.pf1[:, 0:48], BIG, BIG, A.add, A.subtract, 48, [], ["pf1", "uz"])
     gps = ["zs"] + ["gp%d" % i for i in (0, 1, 2, 3, 5, 7, 9, 11)]
-    mm([(T.py0[:, 0:240], T.one[0:1, :], T.cb[0:1], True, False)], 960, ["one"] + cbs, ["py0"])
-    mm([(T.py0[:, 192 + 16 * w:208 + 16 * w], L(T.zs, k), T.gp0[:, k, :, w, :], False, False) for w in range(3) for k in range(16)], 3072, gq, ["py0"])
+    mm([(T.py1[:, 0:240], T.one[0:1, :], T.cb[0:1], True, False)], 960, ["one"] + cbs, ["py1"])
+    mm([(T.py1[:, 192 + 16 * w:208 + 16 * w], L(T.zs, k), T.gp0[:, k, :, w, :], False, False) for w in range(3) for k in range(16)], 3072, gq, ["py1"])
     mm([(T.pe[:, 0:192], L(T.zs, k), T.gp[:, :, 16 * k:16 * k + 16], k == 0, k == 15) for k in range(16)], 3072, gps, ["pe"])
-    mm([(T.py0[:, 0:192], L(T.zs, k), T.gp[:, :, 16 * k:16 * k + 16], False, k == 15) for k in range(16)], 3072, gps, ["py0"])
+    mm([(T.py1[:, 0:192], L(T.zs, k), T.gp[:, :, 16 * k:16 * k + 16], False, k == 15) for k in range(16)], 3072, gps, ["py1"])
     act(T.ww[:, 240:432], T.pe[:, 0:192], AF.Identity, 192, [], ["pe", "wwv"], bias=-OFF, scale=16.0)
-    ts(T.ww[:, 0:240], T.py0[:, 0:240], BIG, BIG, A.add, A.subtract, 240, [], ["py0", "wwc"])
+    ts(T.ww[:, 0:240], T.py1[:, 0:240], BIG, BIG, A.add, A.subtract, 240, [], ["py1", "wwc"])
     cp(T.fi0[:, :, :], T.ww[:, 224:288], 64, ["wwc", "wwv"], ["fz"])
     ts(T.ua0[:, :], T.ww[:, 224:240], OFF, None, A.add, None, 16, ["wwc"], ["ua0"])
 
     rid, pid, _ = topo.addr(nxt)
     mask = sum(1 << e for e in topo.engines(core, nxt)[:8])
     def send(dst, src, rd, tok):
-        add("G", 300, rd, [tok], lambda g: g.remote_dma(dst, src, T.sem["r" + tok], T.sem.sent, pid, rid, mask), "r" + tok)
-    send(T.wi[:, 0:432], T.ww[:, :], ["wwc", "wwv"], "wi")
+        add("G", 2500 if tok == "wi" else 400, rd, [tok], lambda g: g.remote_dma(dst, src, T.sem["r" + tok], T.sem.sent, pid, rid, mask), "r" + tok)
+    send(T.wi[:, 0:432], T.ww[:, :], ["wwc", "wwv", "imt", "wt", "wu", "tie0", "tie1", "ic0", "ic1", "ic2"] + ees + tabs, "wi")
     Q = 0
-    ny = [0]
-    pc, pck, pl, plk = (T.ps[:, 128:144, :], "ps", T.pe[:, 256:512], "pe") if PACK else (T.py0[:, 0:32], "py0", T.py1, "py1")
+    pc, pck, pl, plk = T.pf1[:, 256:288], "pf1", T.py1, "py1"
 
     for t in range(3):
         ybs = []
@@ -247,21 +241,26 @@ def build(T, nxt, topo, core, fig=FIGS[0]):
                 U, UA, F = "uz", "ua0", "fz"
                 ul, u0, ua, fa, fd = T.ui0, 3 * h0, T.ua0[:, h0:h0 + H], T.fi0[:, 0, h0:h0 + H], T.fi0[:, 1:4, h0:h0 + H]
             else:
-                M = I - NC; U = UA = "ui%d" % M; F = "fi%d" % M; nq, nr = NQ[t - 1], NR[t - 1]
+                M = I - NC; U = UA = "ui%d" % M; F = "fi%d" % M; nq = NQ[t - 1]
                 ul, u0, ua, fa, fd = T.ui[:, M], 0, T.ui[:, M, 40:40 + H], T.fi[:, M, 0, 0:H], T.fi[:, M, 1:4, 0:H]
                 if t == 1:
-                    cand, rep = T.cand1[:, c, :], T.ol[:, 12:40]
-                    act(cand, T.wi[:, :].indirect(T.o1[:, c, :]), AF.Copy, 448, ["wi", "wiz", "o1%d" % c], ["cand%d" % M], r=GC)
+                    cand = T.cand1[:, c, :]
+                    act(cand, T.wi[:, h0:432].indirect(T.ol[:, 0:26]), AF.Copy, 416, ["wi", "ol"], ["cand%d" % M], r=GC)
                 else:
-                    cand, rep = T.cand2[:, c, :], T.ol[:, 40:52]
-                    act(cand, T.si[:, c, :].indirect(T.ol[:, 0:12]), AF.Copy, 192, ["si%d" % c, "o2"], ["cand%d" % M], r=GC)
-                gtt(T.msk[:, M, 0:32 * nq], T.mi[:, M, :].indirect(rep), cand, A.mult, 32 * nq, ["mi%d" % M, "cand%d" % M, "ol"], ["msk%d" % M])
-                mm([(T.ps[:, x:3 * nsb:3, :], T.eye[:, :], T.msk[:, M, 8 * (nq * q + x):8 * (nq * q + x) + H], q + x == 0, False)
+                    cand = T.cand2[:, c, :]
+                    act(cand, T.si[:, c, :].indirect(T.ol[:, 26:38]), AF.Copy, 192, ["si%d" % c, "ol"], ["cand%d" % M], r=GC)
+                gtt(T.msk[:, M, 0:96], T.mi[:, M, :].indirect(T.ol[:, 40:46]), cand[:, 0:96], A.mult, 96, ["mi%d" % M, "cand%d" % M, "ol"], ["msk%d" % M])
+                mm([(T.py0[:, :, x, :], T.eye[:, :], T.mi[:, M, :], True, True) for x in range(nq)], 64 * nq, ["eye", "mi%d" % M], ["py0"])
+                tt(T.msk[:, M, 96:96 + 32 * nq], T.py0[:, :, 0:nq, :], cand[:, 96:96 + 32 * nq], A.mult, 32 * nq, ["cand%d" % M], ["py0", "msl%d" % M], 1.0)
+                mm([(T.ps[:, x:3 * nsb:3, :], T.eye[:, :], T.msk[:, M, 24 * q + 8 * x:24 * q + 8 * x + H], q + x == 0, False)
                     for q in range(4) for x in range(3)] +
-                   [(T.ps[:, 12:12 + 4 * nr, :], T.eye[:, :], T.msk[:, M, 8 * nq * q:8 * (nq * q + nr)], False, q == 3) for q in range(4)],
-                   768 + 4 * max(64, 8 * nr), ["eye", "msk%d" % M], ["ps"])
+                   [(T.ps[:, 12:24, :], T.eye[:, :], T.msk[:, M, 24 * q:24 * q + 24], False, q == 3) for q in range(4)],
+                   1024, ["eye", "msk%d" % M], ["ps"])
                 ts(T.ui[:, M, :], T.ps[:, 0:24, :], OFF, None, A.add, None, 48, [], ["ps", U])
-                cp(T.fi[:, M], T.ps[:, 20:36, :], 32, [], ["ps", F])
+                mm([(T.ps[:, 24:24 + 4 * nq, :], T.eye[:, :], T.msk[:, M, 96 + 8 * nq * q:96 + 8 * nq * (q + 1)], q == 0, q == 3) for q in range(4)],
+                   4 * max(64, 8 * nq), ["eye", "msl%d" % M], ["ps"])
+                if FIS: act(T.fi[:, M], T.ps[:, 20:36, :], AF.Identity, 32, [], ["ps", F])
+                else: cp(T.fi[:, M], T.ps[:, 20:36, :], 32, [], ["ps", F])
                 if t == 1:
                     act(T.so[:, c, :], T.ps[:, 12:64, :], AF.Identity, 104, [], ["ps", "so%d" % c])
                     send(T.si[:, c, :], T.so[:, c, :], ["so%d" % c], "si%d" % c)
@@ -276,7 +275,7 @@ def build(T, nxt, topo, core, fig=FIGS[0]):
                 if a: gcp(T.nm[:, I, 0:16 * a], win.indirect(ul[:, u0:u0 + a]), 16 * a, [U] + tks, ["nm%d_0" % I])
                 gcp(T.nm[:, I, 16 * a:3 * n], win.indirect(ul[:, u0 + a:u0 + 3 * H]), 3 * n - 16 * a, [U] + tks, ["nm%d" % I])
                 nms = ["nm%d_0" % I if s < NM1 else "nm%d" % I for s in range(nsb)]
-            ts(T.nf[:, I, 0:nsb], T.nm[:, I, 0:3 * n], -2048.0, 1.0 / 4096, A.add, A.mult, 3 * n, nms, ["nf%d" % I], 0.5)
+            ts(T.nf[:, I, 0:nsb], T.nm[:, I, 0:3 * n], -2048.0, 1.0 if I in YS else 1.0 / 4096, A.add, A.mult, 3 * n, nms, ["nf%d" % I], 0.5)
             cw = T.cv[:, 0:4097]; w = 512
             gvb = T["gv%d_%d" % (t % 2, c)]; prb = T["pr%d_%d" % (t % 2, c)]
             old = ["mm%d" % c] if t == 2 else []; lt = ["mm%d" % c] if t == 0 else []
@@ -284,56 +283,21 @@ def build(T, nxt, topo, core, fig=FIGS[0]):
             for npart in CUT[t][c]:
                 s1 = s0 + npart; x0, x1 = 32 * s0, 32 * s1; nx = x1 - x0
                 pm = T["pm%d" % (Q % 2)]; pmk = "pm%d" % (Q % 2)
-                pack = SB[t][c][s0] in "FGA"
-                ds = s0 if I else s1 - 2
-                if I == 0: mm([(pm[:, 0:3, :], T.eye[:, :], T.zer[:, :, :], True, False)], 384, ["eye", "zer"], [pmk])
-                dlist = [(pm[:, 0:3, x0 + k:x1:16], T.nr[:, k, :], fd[:, :, 2 * s0:2 * s1], I > 0 and k == 0, False) for k in range(16)]
-                if pack:
-                    dlist += [(pm[:, r, x0:x1], T.eyes[:, e, :], T.k18[:, 0:nx], False, False) for r, e in ((3, 1), (3, 2), (2, 3))]
+                ds = max(s0, s1 - 2)
+                mm([(pm[:, 0:3, x0:x1], T.eye[:, :], T.zer[:, :, 0:nx], True, False)], 3 * nx, ["eye", "zer"], [pmk])
+                dlist = [(pm[:, 0:3, x0 + k:x1:16], T.nr[:, k, :], fd[:, :, 2 * s0:2 * s1], False, False) for k in range(16)]
                 for s in range(s0, s1):
                     kd = SB[t][c][s]; e0 = 3 * w * s
                     def gv(a, b): return gvb[:, e0 + a:e0 + b]
                     def pr(a, b): return prb[:, e0 + a:e0 + b]
                     G = "gv%d_%d" % (I, s); P = "pr%d_%d" % (I, s)
                     def lst(a, b): return cw.indirect(T.nm[:, I, 96 * s + a // 16:96 * s + b // 16])
-                    rd = [nms[s], "cv", "cvz"] + old
+                    rd = [nms[s], "cv", "cvz"] + old + (["wwv"] if (I, s) >= (0, 3) else [])
                     last = s == s1 - 1
                     def red(a, b, toks, fin):
                         mm([(pm[:, a:b, 32 * s:32 * s + 32], L(T.zc, p), prb[:, e0 + a * w + p:e0 + b * w:16],
                              False, fin and p == 15) for p in range(16)],
                            16 * max(64, (b - a) * 32), ["zc"] + toks, [pmk] + (lt if fin else []))
-                    if pack:
-                        zq, pq = T["zq%d" % c], T["pq%d" % c]; Z, P = "zq%d_%d" % (c, s), "pq%d_%d" % (c, s)
-                        if kd == "A":
-                            act(gv(0, w), lst(0, w), AF.Copy, w, rd, [G], r=GC, scale=K)
-                            act(gv(w, 2 * w), gv(0, w), AF.Copy, w, [G], [G + "b"], scale=1.0 / K)
-                            gtt(T.ys[:, :], lst(2 * w, 3 * w), gv(0, w), A.add, w, rd + [G], ["ys"])
-                            gtt(zq[:, w * s:w * s + w], lst(w, 2 * w), T.ys[:, :], A.mult, w, rd + ["ys"], [Z])
-                            gtt(pq[:, w * s:w * s + w], lst(2 * w, 3 * w), gv(w, 2 * w), A.mult, w, rd + [G + "b"], [P])
-                        else:
-                            gs = [G]
-                            if kd == "F": act(gv(0, 3 * w), lst(0, 3 * w), AF.Copy, 3 * w, rd, [G], r=GC)
-                            else:
-                                act(gv(0, 2 * w), lst(0, 2 * w), AF.Copy, 2 * w, rd, [G], r=GC)
-                                gcp(gv(2 * w, 3 * w), lst(2 * w, 3 * w), w, rd, [G + "a"]); gs = [G, G + "a"]
-                            pyk = "py%d" % (ny[0] % 2); py = T[pyk]; ny[0] += 1
-                            mm([(py[:, :], T.eyes[:, 0, :], gv(0, w), True, False), (py[:, :], T.eye[:, :], gv(2 * w, 3 * w), False, True)], 2 * w,
-                               gs + ["eye", "eyes0"], [pyk])
-                            tt(zq[:, w * s:w * s + w], py[:, :], gv(w, 2 * w), A.mult, w, gs, [pyk, Z], 1.0)
-                            tt(pq[:, w * s:w * s + w], gv(0, w), gv(2 * w, 3 * w), A.mult, w, gs, [P], 1.0)
-                        if s == ds: mm(dlist, 1024 + 3 * nx, nrs + [F, "k18", "eyes1", "eyes2", "eyes3"], [pmk])
-                        if s % 2:
-                            for x in range(4):
-                                mm([(pm[:, 3, 32 * s - 32:32 * s + 32], L(T.zf, p), zq[:, w * (s - 1) + p:w * (s + 1):16], False, False) for p in range(4 * x, 4 * x + 4)],
-                                   1024, ["zf", Z, "zq%d_%d" % (c, s - 1)], [pmk])
-                            mm([(pm[:, 2, 32 * s - 32:32 * s + 32], L(T.zc, p), pq[:, w * (s - 1) + p:w * (s + 1):16], False, False) for p in range(16)],
-                               1024, ["zc", P, "pq%d_%d" % (c, s - 1)], [pmk])
-                        if last:
-                            ts(T.un[:, c, 0, x0:x1], pm[:, 3, x0:x1], BIG, BIG, A.add, A.subtract, nx, [], [pmk, "un0%d" % c])
-                            tt(T.un[:, c, 1, x0:x1], pm[:, 3, x0:x1], T.un[:, c, 0, x0:x1], A.subtract, nx, ["un0%d" % c], [pmk, "un1%d" % c], 1.0)
-                            mm([(pm[:, e, x0:x1], T.eyes[:, 4 + e, :], T.un[:, c, e, x0:x1], False, e == 1) for e in range(2)], 2 * nx,
-                               ["eyes4", "eyes5", "un0%d" % c, "un1%d" % c], [pmk] + lt)
-                        continue
                     if kd == "W":
                         act(gv(0, 3 * w), lst(0, 3 * w), AF.Copy, 3 * w, rd, [G], r=GC)
                         tt(pr(0, 2 * w), gv(0, 2 * w), gv(w, 3 * w), A.mult, 2 * w, [G], [P + "a"], 1.0)
@@ -343,6 +307,12 @@ def build(T, nxt, topo, core, fig=FIGS[0]):
                         tt(pr(0, w), gv(0, w), gv(w, 2 * w), A.mult, w, [G], [P + "a"], 1.0)
                         gtt(pr(w, 2 * w), lst(2 * w, 3 * w), gv(w, 2 * w), A.mult, w, rd + [G], [P + "b"])
                         gtt(pr(2 * w, 3 * w), lst(2 * w, 3 * w), gv(0, w), A.mult, w, rd + [G], [P + "c"])
+                    elif kd == "Y":
+                        act(gv(0, w), lst(0, w), AF.Copy, w, rd, [G], r=GC)
+                        act(gv(w, 2 * w), lst(w, 2 * w), AF.Copy, w, rd, [G + "c"], r=GC)
+                        gtt(pr(2 * w, 3 * w), lst(2 * w, 3 * w), gv(0, w), A.mult, w, rd + [G], [P + "c"])
+                        tt(pr(0, w), gv(0, w), gv(w, 2 * w), A.mult, w, [G, G + "c"], [P + "a"], 1.0)
+                        gtt(pr(w, 2 * w), lst(2 * w, 3 * w), gv(w, 2 * w), A.mult, w, rd + [G + "c"], [P + "b"])
                     elif kd == "U":
                         act(gv(0, 2 * w), lst(0, 2 * w), AF.Copy, 2 * w, rd, [G], r=GC)
                         gcp(gv(2 * w, 3 * w), lst(2 * w, 3 * w), w, rd, [G + "a"])
@@ -362,11 +332,11 @@ def build(T, nxt, topo, core, fig=FIGS[0]):
                 if t < 2:
                     if t == 1 or c == 0:
                         na, fb = (256, T.fi0[:, 0, :]) if t == 0 else (n, fa)
-                        mm([(T.pe[:, k:na:16], T.ee[:, k, :], fb, True, True) for k in range(16)], 1024, ["ee", F], ["pe"])
-                    xa = 16 * h0 if t == 0 else 0
-                    act(T.ae[:, J, 0:H, 0:16], T.pe[:, xa:xa + n], AF.Abs, n, ["aez"], ["pe", "ae%d" % J])
+                        mm([(T.pe[:, k:na:16], T.ee[:, k, :], fb, True, True) for k in range(16)], 1024, ees + [F], ["pe"])
+                        if t: act(T.ae[:, J, 0:H, 0:16], T.pe[:, 0:n], AF.Abs, n, ["aez"], ["pe", "ae%d" % J])
+                        else: act(T.ae[:, 0:2, :, 0:16], T.pe[:, 0:256], AF.Abs, 256, ["aez"], ["pe", "ae0", "ae1"])
                 HD, EV, FF = "hd%d" % Q, "ev%d" % Q, "ff%d" % Q
-                ts(T.hd[:, I, 0:3, x0:x1], pm[:, 0:3, x0:x1], BIG, BIG + (0.0 if pack else 7.0), A.add, A.is_equal, 3 * nx, [], [pmk, HD])
+                ts(T.hd[:, I, 0:3, x0:x1], pm[:, 0:3, x0:x1], BIG, BIG + 7.0, A.add, A.is_equal, 3 * nx, [], [pmk, HD])
                 if Q not in EVV:
                     mm([(T.pf1[:, 128:128 + nx], T.eye[:, :], T.hd[:, I, e, x0:x1], e == 0, e == 2) for e in range(3)], 3 * max(64, nx), ["eye", HD], ["pf1"])
                     act(T.hd[:, I, 3, x0:x1], T.pf1[:, 128:128 + nx], AF.Relu, nx, [], ["pf1", EV], bias=-2.0)
@@ -377,18 +347,19 @@ def build(T, nxt, topo, core, fig=FIGS[0]):
                     mm([(pc, T.eye[:, :], T.tie[:, :, :], True, False)] +
                        [(pc, L(T.zz, k), T.hd[:, I, :, k:n:16], False, k == 15) for k in range(16)], 1088,
                        ["eye", "tie0", "tie1", "zz", HD, EV], [pck])
-                    tt(T.sc[:, J, :], pc, T.wt[:, :], A.mult, 32, ["wt"], [pck, "sc%d" % J], 1.0)
-                mm([(T.pf1[:, 0:nx], T.imt[:, :], T.hd[:, I, 3, x0:x1], True, True)], max(64, nx), ["imt", EV], ["pf1"])
-                ff = T.ff[:, I, x0:x1]
-                if Q in FFV: ts(ff, T.pf1[:, 0:nx], 0.0, K, A.max, A.mult, nx, [], ["pf1", FF])
-                else: act(ff, T.pf1[:, 0:nx], AF.Relu, nx, [], ["pf1", FF], scale=K)
+                    tt(T.sc[:, J, :], pc, T.wt[:, :], A.mult, 32, ["wt", "wu"], [pck, "sc%d" % J], 1.0)
+                if t < 2 or I not in YS:
+                    mm([(T.pf1[:, 0:nx], T.imt[:, :], T.hd[:, I, 3, x0:x1], True, True)], max(64, nx), ["imt", EV], ["pf1"])
+                    ff = T.ff[:, I, x0:x1]
+                    act(ff, T.pf1[:, 0:nx], AF.Relu, nx, [], ["pf1", FF], scale=0.5)
                 if t < 2:
                     tt(T.m1[:, J, :], T.sc[:, J, 0:16], T.sc[:, J, 16:32], A.max, 16, ["sc%d" % J], ["m1%d" % J])
                     tt(T.m2[:, J, :], T.m1[:, J, 0:8], T.m1[:, J, 8:16], A.max, 8, ["m1%d" % J], ["m2%d" % J])
-                    gtt(T.mk[:, J, :], T.m2[:, J, :].indirect(T.ol[:, 52:54]), T.sc[:, J, :], A.is_equal, 32, ["m2%d" % J, "sc%d" % J, "ol"], ["mk%d" % J])
+                    gtt(T.mk[:, J, :], T.m2[:, J, :].indirect(T.ol[:, 38:40]), T.sc[:, J, :], A.is_equal, 32, ["m2%d" % J, "sc%d" % J, "ol"], ["mk%d" % J])
                     send(T.mi[:, J, :], T.mk[:, J, :], ["mk%d" % J], "mi%d" % J)
                     mm([(pl[:, 0:18 * H], T.eye[:, :], T.c1[:, 0:H, :], True, False), (pl[:, 0:18 * H], T.neye[:, :], T.ae[:, J, 0:H, :], False, False),
-                        (pl[:, 16:18 * H:18], T.eye[:, :], fa, False, False)], 36 * H + 64, ["eye", "neye", "c1", F, "ae%d" % J], [plk])
+                        (pl[:, 0:18 * H], T.eye[:, :], T.icf[:, 0:H, :], False, False),
+                        (pl[:, 16:18 * H:18], T.eye[:, :], fa, False, False)], 54 * H + 64, ["eye", "neye", "c1", "tm", F, "ae%d" % J], [plk])
                     mm([(pl[:, 18 * h:18 * h + 16], T.blk[:, :], T.ff[:, I, 16 * h:16 * h + 16], False, False) for h in range(H)] +
                        [(pl[:, 17:18 * H:18], T.neye[:, :], T.mk[:, J, 24:24 + H], False, True)], 64 * H + 64,
                        ["neye", "blk", FF, "mk%d" % J], [plk])
@@ -398,14 +369,23 @@ def build(T, nxt, topo, core, fig=FIGS[0]):
                     gtt(T.sv[:, J, 0:n], win.indirect(ua), ff, A.max, n, tks + [UA, FF], ["sv%d" % J])
                     gcp(tsb[:, :].indirect(T.su[:, J, 0:H]), T.sv[:, J, 0:n], n, ["su%d" % J, "sv%d" % J], tks, SC)
                 Y = "yy%d" % Q
-                for m in range(3):
-                    tt(T.yy[:, I, m, x0:x1], T.nf[:, I, s0:s1, (m + 2) % 3, :], ff, A.mult, nx, ["nf%d" % I, FF], [Y + str(m)], 1.0)
-                ml = []
-                for h in range(2 * s0, 2 * s1):
-                    for x in range(2): ml.append((T.po[0:24, :, h], T.of[:, x, :], T.ff[:, I, 16 * h:16 * h + 16], x == 0, False))
+                if I in YS:
+                    px, pxk = (T.pe, "pe") if Q % 2 else (T.py1, "py1")
+                    mm([(px[:, m * nx:m * nx + nx], T.eye[:, :], T.nf[:, I, s0:s1, (m + 2) % 3, :], m == 0, False) for m in range(3)], 3 * max(64, nx),
+                       ["eye", "nf%d" % I], [pxk])
+                    mm([(px[:, m * nx:m * nx + nx], T.imt[:, :], T.hd[:, I, 3, x0:x1], False, m == 2) for m in range(3)], 3 * max(64, nx), ["imt", EV], [pxk])
+                    act(T.yz[:, :, x0:x1], px[:, 0:3 * nx], AF.Relu, 3 * nx, [], [pxk, Y], bias=-6143.0)
+                    mm([(T.po[0:24, :, h], T.zp[:, 2 - m:26 - m], T.yz[:, m, 16 * h:16 * h + 16], m == 0, m == 2)
+                        for h in range(2 * s0, 2 * s1) for m in range(3)], 576 * npart, ["zp", Y], ["po"])
+                else:
                     for m in range(3):
-                        ml.append((T.po[0:24, :, h], T.zo[:, 2 - m:26 - m], T.yy[:, I, m, 16 * h:16 * h + 16], False, m == 2))
-                mm(ml, npart * 240, ["of0", "of1", "zo", FF, Y + "0", Y + "1", Y + "2"], ["po"])
+                        tt(T.yy[:, I, m, x0:x1], T.nf[:, I, s0:s1, (m + 2) % 3, :], ff, A.mult, nx, ["nf%d" % I, FF], [Y + str(m)], 1.0)
+                    ml = []
+                    for h in range(2 * s0, 2 * s1):
+                        for x in range(2): ml.append((T.po[0:24, :, h], T.of[:, x], T.ff[:, I, 16 * h:16 * h + 16], x == 0, False))
+                        for m in range(3):
+                            ml.append((T.po[0:24, :, h], T.zo[:, 2 - m:26 - m], T.yy[:, I, m, 16 * h:16 * h + 16], False, m == 2))
+                    mm(ml, npart * 240, ["of0", "of1", "zo", FF, Y + "0", Y + "1", Y + "2"], ["po"])
                 act(T.yb[0:24, t, :, h0 + 2 * s0:h0 + 2 * s1], T.po[0:24, :, 2 * s0:2 * s1], AF.Identity, nx, [], ["po", "yb%d" % Q], bias=-1.0)
                 ybs.append("yb%d" % Q); Q += 1; s0 = s1
         dma(T.yn[:, 768 * t:768 * (t + 1)], T.yb[0:24, t], 24 * 1024, ybs, ["yn%d" % t])
@@ -430,7 +410,7 @@ def plan(ops, alt=(), dma0=1500.0, tries=TRIES, moves=MOVES):
     if tries < 0: return None
     hop, wire = FIGS[0][3:]
     n = len(ops); en = [o["e"] for o in ops]; ns = [o["ns"] for o in ops]
-    def lats(w): return [dma0 if o["kind"] == "dma" else w + 4000.0 * (o["kind"] == "rwi") if o["kind"] else 0.0 for o in ops]
+    def lats(w): return [dma0 if o["kind"] == "dma" else w + FAR * (o["kind"] == "rwi") + 1000.0 * (o["kind"][:3] == "rsi") if o["kind"] else 0.0 for o in ops]
     lat = lats(wire)
     pre = [[(j, lat[j] + (0.0 if en[j] == "P" == en[i] else hop)) for j in ops[i]["dep"]] for i in range(n)]
     ys = [i for i in range(n) if en[i] == "Y"]
@@ -493,15 +473,19 @@ def plan(ops, alt=(), dma0=1500.0, tries=TRIES, moves=MOVES):
         if t <= best: best, (end, each) = t, e2
     figs = [(ns, pre, lat)] + others
     qn = ["VSPGY".index(e) for e in en]
-    def run(seq, f):
-        ns2, pre2, lat2 = figs[f]; free = [0.0] * 5; who = [-1] * 5; e2 = [0.0] * n; by = [-1] * n
-        for i in seq:
+    def run(seq, f, a=0, old=None):
+        ns2, pre2, lat2 = figs[f]; who = [-1] * 5
+        e2, by = (list(old[1]), list(old[2])) if a else ([0.0] * n, [-1] * n)
+        for i in seq[:a]: who[qn[i]] = i
+        free = [e2[i] if i >= 0 else 0.0 for i in who]
+        for i in seq[a:]:
             q = qn[i]; t = free[q]; b = who[q]
             for j, l in pre2[i]:
                 if e2[j] + l > t: t = e2[j] + l; b = j
             e2[i] = free[q] = t + ns2[i]; who[q] = i; by[i] = b
         last = max(ys, key=lambda i: e2[i])
         return e2[last] + lat2[last], e2, by, last
+    if not tries: end = place(list(range(n)), pre, zero)
     seq = sorted(range(n), key=lambda i: end[i] - ns[i] * 0.999)
     res = [run(seq, f) for f in range(len(figs))]; base = [r[0] for r in res]
     def score(rs): return sum(r[0] / b for r, b in zip(rs, base))
@@ -528,8 +512,8 @@ def plan(ops, alt=(), dma0=1500.0, tries=TRIES, moves=MOVES):
                 if deps[x] & mv: mv.add(x)
             if i in mv: continue
             s2 = seq[:a] + [x for x in seq[a:b + 1] if x not in mv] + [x for x in seq[a:b + 1] if x in mv] + seq[b + 1:]
-        r2 = [run(s2, f) for f in range(len(figs))]; t = score(r2)
-        if t <= now + 0.004 * (1.0 - it / moves) * rnd.uniform():
+        r2 = [run(s2, f, a, res[f]) for f in range(len(figs))]; t = score(r2)
+        if t <= now - HEAT * (1.0 - it / moves) ** 2 * np.log(rnd.uniform(1e-9, 1.0)):
             now, seq, res = t, s2, r2
             if t < best: best, keep = t, (s2, r2)
     seq, res = keep
@@ -575,8 +559,11 @@ def rank_program(g, core, T, topo):
             if i in need: c += 1; cnt[i] = c
     q = {"V": g.vector, "S": g.scalar, "P": g.tensor, "G": g, "Y": g.sync}
     sent = 0
+    second = [i for i in order["Y"] if ops[i]["wr"][0] in TWO]
+    for i in second: g.scalar.dma_start(*ops[i]["io"]).then_inc(T.sem[ops[i]["sem"]], 16)
     for e in order:
         for i in order[e]:
+            if i in second: continue
             o = ops[i]
             for k, j in waits[i].items():
                 if ops[j]["kind"] == "dma": q[e].wait_ge(T.sem[k], 16)

import numpy as np
from concourse.mybir import AluOpType as A, ActivationFunctionType as AF

SPLIT = ["UWWW WUWW", "UWWW UWWW", "UWUW UWW|N"]
FINE = 1
EVV = (5, 6)
FFV = ()
NM1 = 1
ENDS = (0, 1, 2, 3, 6)
FIGS = [(1.56, 3.8, 0.42, 70.0, 1600.0), (1.1, 2.0, 0.42, 60.0, 1500.0), (2.0, 5.5, 0.42, 60.0, 1500.0), (1.3, 3.8, 0.45, 120.0, 2600.0)]
RATE = 500.0
MMO = 8.0
VF = 30.0
FIS = 0
TWO = ()
FAR = 3000.0
YS = ()
HEAT = 0.012
TRIES = 60
MOVES = 90000
SB = [[c.replace("|", "") for c in r.split()] for r in SPLIT]
CUT = [[[len(x) for x in c.split("|")] for c in r.split()] for r in SPLIT]
NC = len(SB[0])
HS = [2 * len(c) for c in SB[0]]
H0 = [sum(HS[:c]) for c in range(NC)]
DUM = 1808
WIN = 3856
OFF = 1828.0
BIG = 12582912.0
CW = 251.0 / 65536

PAIRS = [(2, 3), (1, 3), (1, 2), (0, 4), (1, 5), (1, 4), (2, 5), (2, 4), (3, 5), (3, 4), (4, 5), (0, 5), (0, 2), (0, 3), (0, 1)]


def _col(x, y): return PAIRS.index((min(x, y), max(x, y)))
def _val(x, y): return 15 + _col(x, y)


def _cand1():
    cols, rest = [], []
    for o, a, b, c in [(0, 4, 2, 3), (0, 1, 4, 3), (0, 1, 2, 4), (1, 2, 3, 4)]:
        cols += [_col(o, b), _col(o, c), _col(o, a)]
        rest += [_val(b, c), _val(a, c), _val(a, b), _col(o, 5), _col(a, b), _col(a, c), _col(a, 5), _val(a, 5), _val(b, 5), _val(c, 5)]
    return cols + rest


CAND1 = _cand1()
CAND2 = [0, 1, 6, 6, 1, 2, 0, 6, 2, 8, 9, 7] + [3, 12, 11, 12, 4, 10, 11, 10, 5, 12, 11, 3]
NQ = (10, 3)

SCRATCH = {
    "cv": ("sbuf", [128, 4112], "bfloat16"), "ob": ("sbuf", [128, 1536], "bfloat16"), "gp": ("sbuf", [128, 12, 256], "bfloat16"),
    "gp0": ("sbuf", [128, 16, 8, 3, 2], "bfloat16"), "pi": ("sbuf", [128, 8], "int32"), "pf": ("sbuf", [128, 8], "float32"),
    "ia": ("sbuf", [128, 144], "float32"), "ib": ("sbuf", [128, 128], "float32"), "ik": ("sbuf", [128, 8, 18], "float32"),
    "ic": ("sbuf", [128, 8, 18], "float32"), "id3": ("sbuf", [128, 24], "float32"),
    "one": ("sbuf", [128, 128], "float32"), "cb0": ("sbuf", [128, 8, 3, 2], "float32"),
    "blk": ("sbuf", [128, 128], "bfloat16"), "nblk": ("sbuf", [128, 128], "bfloat16"), "eye": ("sbuf", [128, 128], "bfloat16"),
    "neye": ("sbuf", [128, 128], "bfloat16"), "imt": ("sbuf", [128, 128], "bfloat16"),
    "t2": ("sbuf", [128, 128], "bfloat16"), "zz": ("sbuf", [128, 144], "bfloat16"), "zc": ("sbuf", [128, 144], "bfloat16"),
    "zs": ("sbuf", [128, 144], "bfloat16"), "zo": ("sbuf", [128, 32], "bfloat16"), "zp": ("sbuf", [128, 32], "float32"),
    "of": ("sbuf", [128, 2, 24], "bfloat16"), "yz": ("sbuf", [128, 3, 128], "float32"), "icf": ("sbuf", [128, 8, 18], "float16"),
    "sk": ("sbuf", [128, 16], "float32"), "nr": ("sbuf", [128, 16, 128], "bfloat16"), "ee": ("sbuf", [128, 16, 128], "bfloat16"),
    "c1": ("sbuf", [128, 8, 18], "float16"), "rs": ("sbuf", [128, 144], "float32"), "tie": ("sbuf", [128, 4, 8], "bfloat16"),
    "cb": ("sbuf", [128, 15, 16], "float32"), "wt": ("sbuf", [128, 32], "float32"),
    "ww": ("sbuf", [128, 432], "float32"), "wi": ("sbuf", [128, 464], "float32"), "tab": ("sbuf", [128, 46], "float32"), "tb2": ("sbuf", [128, 46], "int32"),
    "tb3": ("sbuf", [128, 46], "int32"), "ol": ("sbuf", [128, 46], "uint16"),
    "ui0": ("sbuf", [128, 48], "uint16"), "ua0": ("sbuf", [128, 16], "uint16"), "fi0": ("sbuf", [128, 4, 16], "float16"),
    "cand1": ("sbuf", [128, NC, 416], "float32"), "cand2": ("sbuf", [128, NC, 192], "float32"),
    "msk": ("sbuf", [128, 2 * NC, 448], "float16"), "sc": ("sbuf", [128, 2 * NC, 32], "float32"),
    "m1": ("sbuf", [128, 2 * NC, 16], "float32"), "m2": ("sbuf", [128, 2 * NC, 8], "float32"), "mk": ("sbuf", [128, 2 * NC, 32], "bfloat16"),
    "mi": ("sbuf", [128, 2 * NC, 32], "bfloat16"), "ui": ("sbuf", [128, 2 * NC, 48], "uint16"), "so": ("sbuf", [128, NC, 104], "float32"),
    "fi": ("sbuf", [128, 2 * NC, 4, 8], "float16"), "si": ("sbuf", [128, NC, 104], "float32"),
    "nm": ("sbuf", [128, 3 * NC, 384], "uint16"), "nf": ("sbuf", [128, 3 * NC, 4, 3, 32], "float16"),
    "hd": ("sbuf", [128, 3 * NC, 4, 128], "bfloat16"), "h2": ("sbuf", [128, 3 * NC, 128], "bfloat16"),
    "ff": ("sbuf", [128, 3 * NC, 128], "bfloat16"), "ae": ("sbuf", [128, 2 * NC, 8, 18], "bfloat16"),
    "yy": ("sbuf", [128, 3 * NC, 3, 128], "float16"), "sv": ("sbuf", [128, 2 * NC, 128], "int32"), "ls": ("sbuf", [128, 2 * NC, 144], "float32"),
    "su": ("sbuf", [128, 2 * NC, 8], "uint16"), "yb": ("sbuf", [128, 3, 16, 16], "float32"),
    "zer": ("sbuf", [128, 3, 128], "bfloat16"),
    "pm0": ("psum", [128, 4, 128], "float32"), "pm1": ("psum", [128, 4, 128], "float32"), "pe": ("psum", [128, 512], "float32"),
    "pf1": ("psum", [128, 512], "float32"), "py0": ("psum", [128, 4, 16, 8], "float32"), "py1": ("psum", [128, 512], "float32"),
    "ps": ("psum", [128, 256, 2], "float32"), "po": ("psum", [128, 16, 32], "float32"),
}
for _c in range(NC):
    SCRATCH["ts%d" % _c] = ("sbuf", [128, WIN], "int32")
    for _t in range(2):
        SCRATCH["gv%d_%d" % (_t, _c)] = ("sbuf", [128, 768 * HS[_c]], "bfloat16")
        SCRATCH["pr%d_%d" % (_t, _c)] = ("sbuf", [128, 768 * HS[_c]], "bfloat16")
SEMAPHORES = ["eV", "eS", "eP", "eG", "sent"] + ["d%d" % i for i in range(24)] + ["rmi%d" % i for i in range(2 * NC)] + ["rsi%d" % i for i in range(NC)] + ["rwi"]


BANKS = [k for k in SCRATCH if SCRATCH[k][0] == "psum"]


def runs(vals):
    out, i = [], 0
    while i < len(vals):
        j = i + 1
        if j < len(vals):
            st = vals[j] - vals[i]
            while j + 1 < len(vals) and vals[j + 1] - vals[j] == st: j += 1
            out.append((i, j - i + 1, vals[i], st)); i = j + 1
        else:
            out.append((i, 1, vals[i], 0)); i = j
    return out


def build(T, nxt, topo, core, fig=FIGS[0]):
    ops = []
    GC, SC, PC = fig[:3]

    def add(e, ns, rd, wr, fn, kind=None): ops.append(dict(e=e, ns=ns, rd=rd, wr=wr, fn=fn, kind=kind))
    def vns(n, r=1.0): return VF + 0.83 * max(64, n * r)
    def ts(out, in0, s1, s2, op0, op1, n, rd, wr, r=1.0):
        if op1 is None: add("V", vns(n, r), rd, wr, lambda g: g.vector.tensor_scalar(out, in0, s1, None, op0))
        else: add("V", vns(n, r), rd, wr, lambda g: g.vector.tensor_scalar(out, in0, s1, s2, op0, op1))
    def tt(out, a, b, op, n, rd, wr, r=2.0): add("V", vns(n, r), rd, wr, lambda g: g.vector.tensor_tensor(out, a, b, op))
    def cp(out, a, n, rd, wr, r=1.0): add("V", vns(n, r), rd, wr, lambda g: g.vector.tensor_copy(out, a))
    def ms(ap, v, n, wr): add("V", vns(n, 0.5), [], wr, lambda g: g.vector.memset(ap, v))
    def gtt(out, a, b, op, n, rd, wr): add("V", 50 + 0.83 * GC * n, rd, wr, lambda g: g.vector.tensor_tensor(out, a, b, op))
    def gcp(out, a, n, rd, wr, r=GC): add("V", 50 + 0.83 * r * n, rd, wr, lambda g: g.vector.tensor_copy(out, a))
    def act(out, a, f, n, rd, wr, bias=0.0, scale=1.0, r=1.0):
        add("S", 50 + 0.83 * max(64, n * r), rd, wr, lambda g: g.scalar.activation(out, a, f, bias=bias, scale=scale))
    def iota(out, pat, base, cm, n, wr, fl=True):
        if fl: add("G", 130 + 1.66 * n, [], wr, lambda g: g.iota(out, pat, base, cm, allow_small_or_imprecise_dtypes=True))
        else: add("G", 130 + 1.66 * n, [], wr, lambda g: g.iota(out, pat, base, cm))
    def select(out, a, pat, op, fill, base, cm, n, rd, wr):
        add("G", 170 + 1.66 * n, rd, wr, lambda g: g.affine_select(out, a, pat, op, fill, base, cm))
    def mm(lst, cyc, rd, wr):
        def fn(g):
            for m in lst: r = g.tensor.matmul(*m)
            return r
        add("P", 40 + PC * cyc + MMO * len(lst), rd, wr, fn)
    def dma(out, in_, nbytes, rd, wr):
        add("Y", nbytes / RATE, rd, wr, lambda g: g.sync.dma_start(out, in_), "dma"); ops[-1]["io"] = (out, in_)

    dma(T.ob[:, 0:1024], T.obs[:, 0:1024], 128 * 2048, [], ["ob0"])
    part = [[2] * len(SB[0][c]) if c < FINE else [HS[c]] for c in range(NC)]
    def table(c, s):
        a = sum(part[c][:s]); b = a + part[c][s]
        dma(T["ts%d" % c][:, 226 * a:226 * b], T.tsee[:, 226 * (H0[c] + a):226 * (H0[c] + b)], 128 * 904 * (b - a), [], ["ts%d_%d" % (c, s)])
    table(0, 0)
    dma(T.ob[:, 1024:1536], T.obs[:, 1024:1536], 128 * 1024, [], ["ob1"])
    dma(T.cv[:, 0:4096], T.cvec[:, :], 128 * 8192, [], ["cv"])
    for c in range(NC):
        for s in range(len(part[c])):
            if c or s: table(c, s)

    iota(T.pi[:, 0:1], [[0, 1]], 0, 1, 1, ["pi0"], False)
    iota(T.ia[:, :], [[1, 144]], 0, 0, 144, ["ia"])
    ts(T.pi[:, 4:5], T.pi[:, 0:1], 4, None, A.arith_shift_right, None, 1, ["pi0"], ["pi4"])
    ts(T.pf[:, 5:6], T.pi[:, 4:5], 16.0, 15.0, A.mult, A.add, 1, ["pi4"], ["pf5"])
    ts(T.zs[:, :], T.ia[:, :], T.pf[:, 5:6], 1.0 / 16, A.is_equal, A.mult, 144, ["ia", "pf5"], ["zs"])
    act(T.zz[:, :], T.zs[:, :], AF.Identity, 144, ["zs"], ["zz"], scale=64.0)
    act(T.zc[:, :], T.zs[:, :], AF.Identity, 144, ["zs"], ["zc"], scale=16.0 * CW)
    ts(T.pi[:, 1:2], T.pi[:, 0:1], 15, None, A.bitwise_and, None, 1, ["pi0"], ["pi1"])
    ts(T.pi[:, 2:3], T.pi[:, 0:1], 7, None, A.bitwise_and, None, 1, ["pi0"], ["pi2"])
    ts(T.pi[:, 3:4], T.pi[:, 0:1], 3, 1, A.arith_shift_right, A.bitwise_and, 1, ["pi0"], ["pi3"])
    cp(T.pf[:, 1:5], T.pi[:, 1:5], 4, ["pi1", "pi2", "pi3", "pi4"], ["pf"])
    ts(T.pf[:, 6:7], T.pi[:, 4:5], 3.0, 2.0, A.mult, A.add, 1, ["pi4"], ["pf6"])
    ms(T.one[0:1, :], 1.0 / 32, 128, ["one"])
    for c in range(NC):
        iota(T.cb0[0:1, H0[c] // 2:(H0[c] + HS[c]) // 2], [[64 * 226, HS[c] // 2], [0, 3], [32 * 226, 2]], -15, 0, 3 * HS[c], ["cb0%d" % c])
    for c in range(NC):
        iota(T.cb[0:1, :, H0[c]:H0[c] + HS[c]], [[0, 15], [32 * 226, HS[c]]], -15 - 32 * int(OFF), 0, 15 * HS[c], ["cb%d" % c])
    cbs = ["cb%d" % c for c in range(NC)]
    iota(T.ib[:, :], [[1, 8], [0, 16]], 0, 0, 128, ["ib"])
    ts(T.blk[:, :], T.ib[:, :], T.pf[:, 4:5], None, A.is_equal, None, 128, ["ib", "pf"], ["blk"])
    select(T.eye[:, :], T.blk[:, :], [[-1, 128]], A.is_equal, 0.0, 0, 1, 128, ["blk"], ["eye"])
    act(T.neye[:, :], T.eye[:, :], AF.Identity, 128, ["eye"], ["neye"], scale=-2097152.0)
    act(T.nblk[:, :], T.blk[:, :], AF.Identity, 128, ["blk"], ["nblk"], scale=-8192.0)
    select(T.t2[:, :], T.nblk[:, :], [[1, 128]], A.is_gt, 0.0, 0, -1, 128, ["nblk"], ["t2"])
    select(T.imt[:, :], T.t2[:, :], [[-1, 128]], A.not_equal, 8192.0, 0, 1, 128, ["t2"], ["imt"])
    ts(T.zo[:, :], T.ia[:, 0:32], T.pf[:, 6:7], None, A.is_equal, None, 32, ["ia", "pf6"], ["zo"])
    ms(T.zer[:, :, :], 0.0, 384, ["zer"])
    if YS: act(T.zp[:, :], T.zo[:, :], AF.Identity, 32, ["zo"], ["zp"])
    iota(T.id3[:, :], [[1, 8], [0, 3]], 0, 0, 24, ["id3"])
    ts(T.of[:, 0], T.id3[:, :], T.pf[:, 4:5], 0.5, A.is_equal, A.mult, 24, ["id3", "pf"], ["of0"])
    act(T.of[:, 1], T.of[:, 0], AF.Identity, 24, ["of0"], ["of1"], scale=1.0 / 2048)
    ts(T.sk[:, :], T.ia[:, 0:16], T.pf[:, 1:2], -CW, A.is_equal, A.mult, 16, ["ia", "pf"], ["sk"])
    for k in range(16):
        act(T.nr[:, k, :], T.blk[:, :], AF.Identity, 128, ["blk", "sk"], ["nr%d" % k], scale=T.sk[:, k:k + 1])
    nrs = ["nr%d" % k for k in range(16)]
    ees = ["ee"]
    select(T.ee[:, :, :], T.nr[:, :, :], [[0, 16], [-1, 128]], A.not_equal, CW, 0, 1, 2048, nrs, ees)
    iota(T.ik[:, :, 0:16], [[0, 8], [1, 16]], 0, 0, 128, ["ik0"]); iota(T.ik[:, :, 16:18], [[0, 16]], -1, 0, 16, ["ik1"])
    iota(T.ic[:, :, 0:16], [[2, 8], [0, 16]], DUM - 4096, 16, 128, ["ic0"]); iota(T.ic[:, :, 16], [[0, 8]], int(OFF), 0, 8, ["ic1"])
    iota(T.ic[:, :, 17], [[2, 8]], DUM, 16, 8, ["ic2"])
    ts(T.c1[:, :, :], T.ik[:, :, :], T.pf[:, 1:2], -30000.0, A.is_ge, A.mult, 144, ["ik0", "ik1", "pf"], ["tm"])
    act(T.icf[:, :, :], T.ic[:, :, :], AF.Identity, 144, ["ic0", "ic1", "ic2"], ["c1"])
    ms(T.rs[:, :], 1.0, 144, ["rs"]); ms(T.rs[:, 0:144:18], 0.0, 8, ["rs"])
    ms(T.ae[:, :, :, 16:18], 0.0, 32 * NC, ["aez"])
    iota(T.cv[:, 4096:4112], [[0, 16]], 0, 0, 16, ["cvz"])
    iota(T.tie[:, 0:3, :], [[-1, 3], [0, 8]], 2, 0, 24, ["tie0"]); iota(T.tie[:, 3, :], [[0, 8]], 0, 0, 8, ["tie1"])
    iota(T.wt[:, 0:16], [[0, 16]], 1, 0, 16, ["wu"]); iota(T.wt[:, 16:32], [[63, 2], [0, 8]], 1, 0, 16, ["wt"])
    rows = [16 * x for x in CAND1] + [8 * x for x in CAND2] + [0] * 4 + [8 * (i // 3) for i in range(12)]
    tabs = []
    for i, n, b, st in runs([x // 8 + 8 * y for x, y in zip(rows[0::2], rows[1::2])]):
        tabs.append("tab%d" % i); iota(T.tab[:, i:i + n], [[st, n]], b, 0, n, [tabs[-1]])
    ts(T.pf[:, 7:8], T.pf[:, 3:4], -63.0 / 64, 1.0, A.mult, A.add, 1, ["pf"], ["pf7"])
    ts(T.tb2[:, :], T.tab[:, :], T.pf[:, 7:8], -63.0 / 128, A.mult, A.add, 46, tabs + ["pf7"], ["tb2"])
    ts(T.tb3[:, :], T.tb2[:, :], 63, None, A.bitwise_and, None, 46, ["tb2"], ["tb3"])
    ts(T.ol[:, :], T.tb3[:, :], 8.0, T.pf[:, 2:3], A.mult, A.add, 46, ["tb3", "pf"], ["ol"])

    def star(j, n=1): return T.ob[:, 256 * j:256 * (j + n)]
    for w in range(3):
        tt(T.gp0[:, :, :, w, :], star(0), star(PAIRS[12 + w][1]), A.mult, 256, ["ob0"], ["gq%d" % w], 1.0)
    for i in range(3):
        tt(T.gp[:, i, :], star(PAIRS[i][0]), star(PAIRS[i][1]), A.mult, 256, ["ob0", "tm", "zo", "of0", "zer", "pf7", "rs", "aez"], ["gp%d" % i], 1.0)
    for i in (3, 5, 7, 9):
        tt(T.gp[:, i:i + 2, :], star(PAIRS[i][0], 2), star(4, 2), A.mult, 512, ["ob0", "ob1"], ["gp%d" % i], 1.0)
    tt(T.gp[:, 11, :], star(0), star(5), A.mult, 256, ["ob0", "ob1"], ["gp11"], 1.0)
    def L(z, k): return z[:, 15 - k:143 - k]
    gq = ["gq0", "gq1", "gq2", "zs"]
    mm([(T.pf1[:, 0:48], T.one[0:1, :], T.cb0[0:1], True, False)], 256, ["one"] + ["cb0%d" % c for c in range(NC)], ["pf1"])
    mm([(T.pf1[:, 0:48], L(T.zs, k), T.gp0[:, k], False, k == 15) for k in range(16)], 1024, gq, ["pf1"])
    ts(T.ui0[:, :], T.pf1[:, 0:48], BIG, BIG, A.add, A.subtract, 48, [], ["pf1", "uz"])
    gps = ["zs"] + ["gp%d" % i for i in (0, 1, 2, 3, 5, 7, 9, 11)]
    mm([(T.py1[:, 0:240], T.one[0:1, :], T.cb[0:1], True, False)], 960, ["one"] + cbs, ["py1"])
    mm([(T.py1[:, 192 + 16 * w:208 + 16 * w], L(T.zs, k), T.gp0[:, k, :, w, :], False, False) for w in range(3) for k in range(16)], 3072, gq, ["py1"])
    mm([(T.pe[:, 0:192], L(T.zs, k), T.gp[:, :, 16 * k:16 * k + 16], k == 0, k == 15) for k in range(16)], 3072, gps, ["pe"])
    mm([(T.py1[:, 0:192], L(T.zs, k), T.gp[:, :, 16 * k:16 * k + 16], False, k == 15) for k in range(16)], 3072, gps, ["py1"])
    act(T.ww[:, 240:432], T.pe[:, 0:192], AF.Identity, 192, [], ["pe", "wwv"], bias=-OFF, scale=16.0)
    ts(T.ww[:, 0:240], T.py1[:, 0:240], BIG, BIG, A.add, A.subtract, 240, [], ["py1", "wwc"])
    cp(T.fi0[:, :, :], T.ww[:, 224:288], 64, ["wwc", "wwv"], ["fz"])
    ts(T.ua0[:, :], T.ww[:, 224:240], OFF, None, A.add, None, 16, ["wwc"], ["ua0"])

    rid, pid, _ = topo.addr(nxt)
    mask = sum(1 << e for e in topo.engines(core, nxt)[:8])
    def send(dst, src, rd, tok):
        add("G", 2500 if tok == "wi" else 400, rd, [tok], lambda g: g.remote_dma(dst, src, T.sem["r" + tok], T.sem.sent, pid, rid, mask), "r" + tok)
    send(T.wi[:, 0:432], T.ww[:, :], ["wwc", "wwv", "imt", "wt", "wu", "tie0", "tie1", "ic0", "ic1", "ic2"] + ees + tabs, "wi")
    Q = 0
    pc, pck, pl, plk = T.pf1[:, 256:288], "pf1", T.py1, "py1"

    for t in range(3):
        ybs = []
        for c in range(NC):
            I = J = t * NC + c; H = HS[c]; n = 16 * H; tsb = T["ts%d" % c]; nsb = H // 2; h0 = H0[c]
            tks = ["ts%d_%d" % (c, s) for s in range(len(part[c]))]; fine = t == 0 and len(tks) > 1
            if t == 0:
                U, UA, F = "uz", "ua0", "fz"
                ul, u0, ua, fa, fd = T.ui0, 3 * h0, T.ua0[:, h0:h0 + H], T.fi0[:, 0, h0:h0 + H], T.fi0[:, 1:4, h0:h0 + H]
            else:
                M = I - NC; U = UA = "ui%d" % M; F = "fi%d" % M; nq = NQ[t - 1]
                ul, u0, ua, fa, fd = T.ui[:, M], 0, T.ui[:, M, 40:40 + H], T.fi[:, M, 0, 0:H], T.fi[:, M, 1:4, 0:H]
                if t == 1:
                    cand = T.cand1[:, c, :]
                    act(cand, T.wi[:, h0:432].indirect(T.ol[:, 0:26]), AF.Copy, 416, ["wi", "ol"], ["cand%d" % M], r=GC)
                else:
                    cand = T.cand2[:, c, :]
                    act(cand, T.si[:, c, :].indirect(T.ol[:, 26:38]), AF.Copy, 192, ["si%d" % c, "ol"], ["cand%d" % M], r=GC)
                gtt(T.msk[:, M, 0:96], T.mi[:, M, :].indirect(T.ol[:, 40:46]), cand[:, 0:96], A.mult, 96, ["mi%d" % M, "cand%d" % M, "ol"], ["msk%d" % M])
                mm([(T.py0[:, :, x, :], T.eye[:, :], T.mi[:, M, :], True, True) for x in range(nq)], 64 * nq, ["eye", "mi%d" % M], ["py0"])
                tt(T.msk[:, M, 96:96 + 32 * nq], T.py0[:, :, 0:nq, :], cand[:, 96:96 + 32 * nq], A.mult, 32 * nq, ["cand%d" % M], ["py0", "msl%d" % M], 1.0)
                mm([(T.ps[:, x:3 * nsb:3, :], T.eye[:, :], T.msk[:, M, 24 * q + 8 * x:24 * q + 8 * x + H], q + x == 0, False)
                    for q in range(4) for x in range(3)] +
                   [(T.ps[:, 12:24, :], T.eye[:, :], T.msk[:, M, 24 * q:24 * q + 24], False, q == 3) for q in range(4)],
                   1024, ["eye", "msk%d" % M], ["ps"])
                ts(T.ui[:, M, :], T.ps[:, 0:24, :], OFF, None, A.add, None, 48, [], ["ps", U])
                mm([(T.ps[:, 24:24 + 4 * nq, :], T.eye[:, :], T.msk[:, M, 96 + 8 * nq * q:96 + 8 * nq * (q + 1)], q == 0, q == 3) for q in range(4)],
                   4 * max(64, 8 * nq), ["eye", "msl%d" % M], ["ps"])
                if FIS: act(T.fi[:, M], T.ps[:, 20:36, :], AF.Identity, 32, [], ["ps", F])
                else: cp(T.fi[:, M], T.ps[:, 20:36, :], 32, [], ["ps", F])
                if t == 1:
                    act(T.so[:, c, :], T.ps[:, 12:64, :], AF.Identity, 104, [], ["ps", "so%d" % c])
                    send(T.si[:, c, :], T.so[:, c, :], ["so%d" % c], "si%d" % c)
            win = tsb[:, 0:226 * H]
            if fine:
                for s in range(nsb):
                    gcp(T.nm[:, I, 96 * s:96 * s + 96], tsb[:, 0:452 * (s + 1)].indirect(ul[:, u0 + 6 * s:u0 + 6 * s + 6]), 96,
                        [U] + tks[:s + 1], ["nm%d_%d" % (I, s)])
                nms = ["nm%d_%d" % (I, s) for s in range(nsb)]
            else:
                a = 6 * NM1
                if a: gcp(T.nm[:, I, 0:16 * a], win.indirect(ul[:, u0:u0 + a]), 16 * a, [U] + tks, ["nm%d_0" % I])
                gcp(T.nm[:, I, 16 * a:3 * n], win.indirect(ul[:, u0 + a:u0 + 3 * H]), 3 * n - 16 * a, [U] + tks, ["nm%d" % I])
                nms = ["nm%d_0" % I if s < NM1 else "nm%d" % I for s in range(nsb)]
            ts(T.nf[:, I, 0:nsb], T.nm[:, I, 0:3 * n], -2048.0, 1.0 if I in YS else 1.0 / 4096, A.add, A.mult, 3 * n, nms, ["nf%d" % I], 0.5)
            cw = T.cv[:, 0:4097]; w = 512
            gvb = T["gv%d_%d" % (t % 2, c)]; prb = T["pr%d_%d" % (t % 2, c)]
            old = ["mm%d" % c] if t == 2 else []; lt = ["mm%d" % c] if t == 0 else []
            s0 = 0
            for npart in CUT[t][c]:
                s1 = s0 + npart; x0, x1 = 32 * s0, 32 * s1; nx = x1 - x0
                pm = T["pm%d" % (Q % 2)]; pmk = "pm%d" % (Q % 2)
                ds = max(s0, s1 - 2)
                mm([(pm[:, 0:3, x0:x1], T.eye[:, :], T.zer[:, :, 0:nx], True, False)], 3 * nx, ["eye", "zer"], [pmk])
                dlist = [(pm[:, 0:3, x0 + k:x1:16], T.nr[:, k, :], fd[:, :, 2 * s0:2 * s1], False, False) for k in range(16)]
                for s in range(s0, s1):
                    kd = SB[t][c][s]; e0 = 3 * w * s
                    def gv(a, b): return gvb[:, e0 + a:e0 + b]
                    def pr(a, b): return prb[:, e0 + a:e0 + b]
                    G = "gv%d_%d" % (I, s); P = "pr%d_%d" % (I, s)
                    def lst(a, b): return cw.indirect(T.nm[:, I, 96 * s + a // 16:96 * s + b // 16])
                    rd = [nms[s], "cv", "cvz"] + old + (["wwv"] if (I, s) >= (0, 3) else [])
                    last = s == s1 - 1
                    def red(a, b, toks, fin):
                        mm([(pm[:, a:b, 32 * s:32 * s + 32], L(T.zc, p), prb[:, e0 + a * w + p:e0 + b * w:16],
                             False, fin and p == 15) for p in range(16)],
                           16 * max(64, (b - a) * 32), ["zc"] + toks, [pmk] + (lt if fin else []))
                    if kd == "W":
                        act(gv(0, 3 * w), lst(0, 3 * w), AF.Copy, 3 * w, rd, [G], r=GC)
                        tt(pr(0, 2 * w), gv(0, 2 * w), gv(w, 3 * w), A.mult, 2 * w, [G], [P + "a"], 1.0)
                        tt(pr(2 * w, 3 * w), gv(0, w), gv(2 * w, 3 * w), A.mult, w, [G], [P + "b"], 1.0)
                    elif kd == "X":
                        act(gv(0, 2 * w), lst(0, 2 * w), AF.Copy, 2 * w, rd, [G], r=GC)
                        tt(pr(0, w), gv(0, w), gv(w, 2 * w), A.mult, w, [G], [P + "a"], 1.0)
                        gtt(pr(w, 2 * w), lst(2 * w, 3 * w), gv(w, 2 * w), A.mult, w, rd + [G], [P + "b"])
                        gtt(pr(2 * w, 3 * w), lst(2 * w, 3 * w), gv(0, w), A.mult, w, rd + [G], [P + "c"])
                    elif kd == "Y":
                        act(gv(0, w), lst(0, w), AF.Copy, w, rd, [G], r=GC)
                        act(gv(w, 2 * w), lst(w, 2 * w), AF.Copy, w, rd, [G + "c"], r=GC)
                        gtt(pr(2 * w, 3 * w), lst(2 * w, 3 * w), gv(0, w), A.mult, w, rd + [G], [P + "c"])
                        tt(pr(0, w), gv(0, w), gv(w, 2 * w), A.mult, w, [G, G + "c"], [P + "a"], 1.0)
                        gtt(pr(w, 2 * w), lst(2 * w, 3 * w), gv(w, 2 * w), A.mult, w, rd + [G + "c"], [P + "b"])
                    elif kd == "U":
                        act(gv(0, 2 * w), lst(0, 2 * w), AF.Copy, 2 * w, rd, [G], r=GC)
                        gcp(gv(2 * w, 3 * w), lst(2 * w, 3 * w), w, rd, [G + "a"])
                        tt(pr(0, 2 * w), gv(0, 2 * w), gv(w, 3 * w), A.mult, 2 * w, [G, G + "a"], [P + "a"], 1.0)
                        tt(pr(2 * w, 3 * w), gv(0, w), gv(2 * w, 3 * w), A.mult, w, [G, G + "a"], [P + "b"], 1.0)
                    else:
                        act(gv(0, 2 * w), lst(0, 2 * w), AF.Copy, 2 * w, rd, [G], r=GC)
                        act(gv(2 * w, 3 * w), lst(2 * w, 3 * w), AF.Copy, w, rd, [G + "a"], r=GC)
                        tt(pr(0, w), gv(0, w), gv(w, 2 * w), A.mult, w, [G], [P + "a"], 1.0)
                        tt(pr(w, 2 * w), gv(w, 2 * w), gv(2 * w, 3 * w), A.mult, w, [G, G + "a"], [P + "b"], 1.0)
                        tt(pr(2 * w, 3 * w), gv(0, w), gv(2 * w, 3 * w), A.mult, w, [G, G + "a"], [P + "c"], 1.0)
                    if s == ds: mm(dlist, 1024, nrs + [F], [pmk])
                    end = last and Q in ENDS
                    if end and kd in "WU": red(0, 2, [P + "a"], False); red(2, 3, [P + "b"], True)
                    elif end: red(0, 2, [P + "a", P + "b"], False); red(2, 3, [P + "c"], True)
                    else: red(0, 3, [P + "a", P + "b", P + "c"], last)
                if t < 2:
                    if t == 1 or c == 0:
                        na, fb = (256, T.fi0[:, 0, :]) if t == 0 else (n, fa)
                        mm([(T.pe[:, k:na:16], T.ee[:, k, :], fb, True, True) for k in range(16)], 1024, ees + [F], ["pe"])
                        if t: act(T.ae[:, J, 0:H, 0:16], T.pe[:, 0:n], AF.Abs, n, ["aez"], ["pe", "ae%d" % J])
                        else: act(T.ae[:, 0:2, :, 0:16], T.pe[:, 0:256], AF.Abs, 256, ["aez"], ["pe", "ae0", "ae1"])
                HD, EV, FF = "hd%d" % Q, "ev%d" % Q, "ff%d" % Q
                ts(T.hd[:, I, 0:3, x0:x1], pm[:, 0:3, x0:x1], BIG, BIG + 7.0, A.add, A.is_equal, 3 * nx, [], [pmk, HD])
                if Q not in EVV:
                    mm([(T.pf1[:, 128:128 + nx], T.eye[:, :], T.hd[:, I, e, x0:x1], e == 0, e == 2) for e in range(3)], 3 * max(64, nx), ["eye", HD], ["pf1"])
                    act(T.hd[:, I, 3, x0:x1], T.pf1[:, 128:128 + nx], AF.Relu, nx, [], ["pf1", EV], bias=-2.0)
                else:
                    tt(T.h2[:, I, x0:x1], T.hd[:, I, 0, x0:x1], T.hd[:, I, 1, x0:x1], A.mult, nx, [HD], ["h2%d" % Q], 1.0)
                    tt(T.hd[:, I, 3, x0:x1], T.h2[:, I, x0:x1], T.hd[:, I, 2, x0:x1], A.mult, nx, [HD, "h2%d" % Q], [EV], 1.0)
                if t < 2:
                    mm([(pc, T.eye[:, :], T.tie[:, :, :], True, False)] +
                       [(pc, L(T.zz, k), T.hd[:, I, :, k:n:16], False, k == 15) for k in range(16)], 1088,
                       ["eye", "tie0", "tie1", "zz", HD, EV], [pck])
                    tt(T.sc[:, J, :], pc, T.wt[:, :], A.mult, 32, ["wt", "wu"], [pck, "sc%d" % J], 1.0)
                if t < 2 or I not in YS:
                    mm([(T.pf1[:, 0:nx], T.imt[:, :], T.hd[:, I, 3, x0:x1], True, True)], max(64, nx), ["imt", EV], ["pf1"])
                    ff = T.ff[:, I, x0:x1]
                    act(ff, T.pf1[:, 0:nx], AF.Relu, nx, [], ["pf1", FF], scale=0.5)
                if t < 2:
                    tt(T.m1[:, J, :], T.sc[:, J, 0:16], T.sc[:, J, 16:32], A.max, 16, ["sc%d" % J], ["m1%d" % J])
                    tt(T.m2[:, J, :], T.m1[:, J, 0:8], T.m1[:, J, 8:16], A.max, 8, ["m1%d" % J], ["m2%d" % J])
                    gtt(T.mk[:, J, :], T.m2[:, J, :].indirect(T.ol[:, 38:40]), T.sc[:, J, :], A.is_equal, 32, ["m2%d" % J, "sc%d" % J, "ol"], ["mk%d" % J])
                    send(T.mi[:, J, :], T.mk[:, J, :], ["mk%d" % J], "mi%d" % J)
                    mm([(pl[:, 0:18 * H], T.eye[:, :], T.c1[:, 0:H, :], True, False), (pl[:, 0:18 * H], T.neye[:, :], T.ae[:, J, 0:H, :], False, False),
                        (pl[:, 0:18 * H], T.eye[:, :], T.icf[:, 0:H, :], False, False),
                        (pl[:, 16:18 * H:18], T.eye[:, :], fa, False, False)], 54 * H + 64, ["eye", "neye", "c1", "tm", F, "ae%d" % J], [plk])
                    mm([(pl[:, 18 * h:18 * h + 16], T.blk[:, :], T.ff[:, I, 16 * h:16 * h + 16], False, False) for h in range(H)] +
                       [(pl[:, 17:18 * H:18], T.neye[:, :], T.mk[:, J, 24:24 + H], False, True)], 64 * H + 64,
                       ["neye", "blk", FF, "mk%d" % J], [plk])
                    add("V", vns(18 * H), ["rs"], [plk, "ls%d" % J], lambda g, J=J, H=H: g.vector.tensor_tensor_scan(
                        T.ls[:, J, 0:18 * H], T.rs[:, 0:18 * H], pl[:, 0:18 * H], 0.0, A.mult, A.max))
                    cp(T.su[:, J, 0:H], T.ls[:, J, 17:18 * H:18], H, ["ls%d" % J], ["su%d" % J])
                    gtt(T.sv[:, J, 0:n], win.indirect(ua), ff, A.max, n, tks + [UA, FF], ["sv%d" % J])
                    gcp(tsb[:, :].indirect(T.su[:, J, 0:H]), T.sv[:, J, 0:n], n, ["su%d" % J, "sv%d" % J], tks, SC)
                Y = "yy%d" % Q
                if I in YS:
                    px, pxk = (T.pe, "pe") if Q % 2 else (T.py1, "py1")
                    mm([(px[:, m * nx:m * nx + nx], T.eye[:, :], T.nf[:, I, s0:s1, (m + 2) % 3, :], m == 0, False) for m in range(3)], 3 * max(64, nx),
                       ["eye", "nf%d" % I], [pxk])
                    mm([(px[:, m * nx:m * nx + nx], T.imt[:, :], T.hd[:, I, 3, x0:x1], False, m == 2) for m in range(3)], 3 * max(64, nx), ["imt", EV], [pxk])
                    act(T.yz[:, :, x0:x1], px[:, 0:3 * nx], AF.Relu, 3 * nx, [], [pxk, Y], bias=-6143.0)
                    mm([(T.po[0:24, :, h], T.zp[:, 2 - m:26 - m], T.yz[:, m, 16 * h:16 * h + 16], m == 0, m == 2)
                        for h in range(2 * s0, 2 * s1) for m in range(3)], 576 * npart, ["zp", Y], ["po"])
                else:
                    for m in range(3):
                        tt(T.yy[:, I, m, x0:x1], T.nf[:, I, s0:s1, (m + 2) % 3, :], ff, A.mult, nx, ["nf%d" % I, FF], [Y + str(m)], 1.0)
                    ml = []
                    for h in range(2 * s0, 2 * s1):
                        for x in range(2): ml.append((T.po[0:24, :, h], T.of[:, x], T.ff[:, I, 16 * h:16 * h + 16], x == 0, False))
                        for m in range(3):
                            ml.append((T.po[0:24, :, h], T.zo[:, 2 - m:26 - m], T.yy[:, I, m, 16 * h:16 * h + 16], False, m == 2))
                    mm(ml, npart * 240, ["of0", "of1", "zo", FF, Y + "0", Y + "1", Y + "2"], ["po"])
                act(T.yb[0:24, t, :, h0 + 2 * s0:h0 + 2 * s1], T.po[0:24, :, 2 * s0:2 * s1], AF.Identity, nx, [], ["po", "yb%d" % Q], bias=-1.0)
                ybs.append("yb%d" % Q); Q += 1; s0 = s1
        dma(T.yn[:, 768 * t:768 * (t + 1)], T.yb[0:24, t], 24 * 1024, ybs, ["yn%d" % t])
    return ops


def plan(ops, alt=(), dma0=1500.0, tries=TRIES, moves=MOVES):
    lw, lr = {}, {}
    for i, o in enumerate(ops):
        d = set()
        if o["e"] != "P":
            for k in [k for k in o["wr"] if k in BANKS]:
                o["wr"].remove(k); o["rd"] = o["rd"] + [k]
        for k in o["rd"]:
            if k in BANKS and o["e"] != "P": d.update(j for j in lr.get(k, []) if ops[j]["e"] != o["e"])
        for k in o["rd"] + o["wr"]:
            if k in lw: d.add(lw[k])
        for k in o["wr"]: d.update(lr.get(k, []))
        d.discard(i); o["dep"] = sorted(d)
        for k in o["rd"]: lr.setdefault(k, []).append(i)
        for k in o["wr"]: lw[k] = i; lr[k] = []
    if tries < 0: return None
    hop, wire = FIGS[0][3:]
    n = len(ops); en = [o["e"] for o in ops]; ns = [o["ns"] for o in ops]
    def lats(w): return [dma0 if o["kind"] == "dma" else w + FAR * (o["kind"] == "rwi") + 1000.0 * (o["kind"][:3] == "rsi") if o["kind"] else 0.0 for o in ops]
    lat = lats(wire)
    pre = [[(j, lat[j] + (0.0 if en[j] == "P" == en[i] else hop)) for j in ops[i]["dep"]] for i in range(n)]
    ys = [i for i in range(n) if en[i] == "Y"]
    for a, b in zip(ys, ys[1:]): pre[b].append((a, 0.0))
    suc = [[] for _ in ops]
    for i in range(n):
        for j, l in pre[i]: suc[j].append((i, l))

    def place(seq, before, tail):
        end = [0.0] * n; busy = {e: [] for e in "VSPGY"}
        for i in seq:
            t = tail[i]
            for j, l in before[i]:
                if end[j] + l > t: t = end[j] + l
            b = busy[en[i]]; k = len(b); d = ns[i]
            while k > 0 and b[k - 1][1] > t: k -= 1
            while k < len(b) and b[k][0] < t + d:
                if b[k][1] > t: t = b[k][1]
                k += 1
            b.insert(k, (t, t + d)); end[i] = t + d
        return end

    def topo_sort(key):
        k2 = list(key)
        for i in range(n):
            for j, l in pre[i]:
                if k2[j] >= k2[i]: k2[i] = k2[j] + 1e-6
        return sorted(range(n), key=lambda i: (k2[i], i))

    zero = [0.0] * n
    def both(seq):
        end = place(seq, pre, zero)
        back = place(sorted(range(n), key=lambda i: (-end[i] - lat[i], -i)), suc, lat)
        end = place(sorted(range(n), key=lambda i: (-back[i], i)), pre, zero)
        ts = [max(end[i] + lat[i] for i in range(n))]
        seq = sorted(range(n), key=lambda i: end[i] - ns[i] * 0.999)
        for ns2, pre2, lat2 in others:
            free = {e: 0.0 for e in "VSPGY"}; e2 = [0.0] * n
            for i in seq:
                t = free[en[i]]
                for j, l in pre2[i]:
                    if e2[j] + l > t: t = e2[j] + l
                e2[i] = free[en[i]] = t + ns2[i]
            ts.append(max(e2[i] + lat2[i] for i in range(n)))
        return sum(ts) / len(ts), (end, ts)

    others = []
    for ns2, h2, w2 in alt:
        lat2 = lats(w2)
        others.append((ns2, [[(j, lat2[j] + (0.0 if en[j] == "P" == en[i] else h2)) for j in ops[i]["dep"]] for i in range(n)], lat2))
        for a, b in zip(ys, ys[1:]): others[-1][1][b].append((a, 0.0))
    rnd = np.random.RandomState(1)
    best, (end, each) = both(list(range(n)))
    now, cur = best, end
    for it in range(tries):
        jit = (rnd.uniform(0.0, 1.0, n) ** 3 * (300.0, 1000.0, 2500.0)[it % 3]).tolist()
        a = rnd.uniform(-5000.0, each[0]); b = a + rnd.uniform(3000.0, 15000.0)
        t, e2 = both(topo_sort([cur[i] - ns[i] + (jit[i] if a <= cur[i] <= b else 0.0) for i in range(n)]))
        if t <= now + 400.0 * (1.0 - it / tries) * rnd.uniform(): now, cur = t, e2[0]
        if t <= best: best, (end, each) = t, e2
    figs = [(ns, pre, lat)] + others
    qn = ["VSPGY".index(e) for e in en]
    def run(seq, f, a=0, old=None):
        ns2, pre2, lat2 = figs[f]; who = [-1] * 5
        e2, by = (list(old[1]), list(old[2])) if a else ([0.0] * n, [-1] * n)
        for i in seq[:a]: who[qn[i]] = i
        free = [e2[i] if i >= 0 else 0.0 for i in who]
        for i in seq[a:]:
            q = qn[i]; t = free[q]; b = who[q]
            for j, l in pre2[i]:
                if e2[j] + l > t: t = e2[j] + l; b = j
            e2[i] = free[q] = t + ns2[i]; who[q] = i; by[i] = b
        last = max(ys, key=lambda i: e2[i])
        return e2[last] + lat2[last], e2, by, last
    if not tries: end = place(list(range(n)), pre, zero)
    seq = sorted(range(n), key=lambda i: end[i] - ns[i] * 0.999)
    res = [run(seq, f) for f in range(len(figs))]; base = [r[0] for r in res]
    def score(rs): return sum(r[0] / b for r, b in zip(rs, base))
    now = best = score(res); keep = seq, res
    deps = [set(j for j, l in pre[i]) for i in range(n)]
    for it in range(moves):
        r = res[rnd.randint(len(figs))]; path = []; i = r[3]
        while i >= 0:
            j = r[2][i]
            if j >= 0 and j not in deps[i] and qn[i] != 4: path.append((j, i))
            i = j
        if not path: break
        j, i = path[rnd.randint(len(path))]
        a, b = seq.index(j), seq.index(i)
        if rnd.randint(2):
            a = max(0, a - (rnd.randint(12) if rnd.randint(2) else 0)); need = {i}; mv = []
            for x in reversed(seq[a:b + 1]):
                if x in need: mv.append(x); need |= deps[x]
            if j in mv: continue
            s2 = seq[:a] + mv[::-1] + [x for x in seq[a:b + 1] if x not in need] + seq[b + 1:]
        else:
            b = min(n - 1, b + (rnd.randint(12) if rnd.randint(2) else 0)); mv = {j}
            for x in seq[a + 1:b + 1]:
                if deps[x] & mv: mv.add(x)
            if i in mv: continue
            s2 = seq[:a] + [x for x in seq[a:b + 1] if x not in mv] + [x for x in seq[a:b + 1] if x in mv] + seq[b + 1:]
        r2 = [run(s2, f, a, res[f]) for f in range(len(figs))]; t = score(r2)
        if t <= now - HEAT * (1.0 - it / moves) ** 2 * np.log(rnd.uniform(1e-9, 1.0)):
            now, seq, res = t, s2, r2
            if t < best: best, keep = t, (s2, r2)
    seq, res = keep
    order = {e: [i for i in seq if en[i] == e] for e in "VSPGY"}
    for i in range(n): ops[i]["t0"] = res[0][1][i] - ns[i]
    return order, [r[0] for r in res]


ORDER = {}


def rank_program(g, core, T, topo):
    rank = T.rank_of(core)
    if rank is None:
        return
    nxt = T.cores[(rank + 1) % len(T.cores)]
    ops = build(T, nxt, topo, core)
    if not ORDER: ORDER.update(plan(ops, [([o["ns"] for o in build(T, nxt, topo, core, f)], f[3], f[4]) for f in FIGS[1:]])[0])
    else: plan(ops, tries=-1)
    order = ORDER
    pos = {i: k for e in order for k, i in enumerate(order[e])}
    nd = 0
    for i in order["Y"]: ops[i]["sem"] = "d%d" % nd; nd += 1
    need = set(); waits = {}
    for e in order:
        seen = {}
        for i in order[e]:
            w = {}
            for j in ops[i]["dep"]:
                o = ops[j]
                if o["kind"]:
                    key = o.get("sem", o["kind"])
                    if key not in seen: seen[key] = 1; w[key] = j
                elif not (o["e"] == "P" == e) and pos[j] > seen.get(o["e"], -1) and pos[j] > pos.get(w.get(o["e"]), -1):
                    w[o["e"]] = j
            for k, j in w.items():
                if not ops[j]["kind"]: seen[k] = pos[j]; need.add(j)
            waits[i] = w
    cnt = {}
    for e in order:
        c = 0
        for i in order[e]:
            if i in need: c += 1; cnt[i] = c
    q = {"V": g.vector, "S": g.scalar, "P": g.tensor, "G": g, "Y": g.sync}
    sent = 0
    second = [i for i in order["Y"] if ops[i]["wr"][0] in TWO]
    for i in second: g.scalar.dma_start(*ops[i]["io"]).then_inc(T.sem[ops[i]["sem"]], 16)
    for e in order:
        for i in order[e]:
            if i in second: continue
            o = ops[i]
            for k, j in waits[i].items():
                if ops[j]["kind"] == "dma": q[e].wait_ge(T.sem[k], 16)
                elif ops[j]["kind"]: q[e].wait_ge(T.sem[k], 8)
                else: q[e].wait_ge(T.sem["e" + k], cnt[j])
            r = o["fn"](g)
            if o["kind"] == "dma": r.then_inc(T.sem[o["sem"]], 16)
            elif o["kind"]: sent += 8
            elif i in need: r.then_inc(T.sem["e" + e], 1)
    g.wait_ge(T.sem.sent, sent)
    for i in order["Y"]:
        if ops[i]["wr"][0].startswith("yn"): g.sync.wait_ge(T.sem[ops[i]["sem"]], 16)
